import numpy as np
import ml_dtypes


def mxq(x, axis, fmt="e4m3"):
    dtype, down = {"e4m3": (ml_dtypes.float8_e4m3fn, 7), "e5m2": (ml_dtypes.float8_e5m2, 14)}[fmt]
    v = np.moveaxis(np.asarray(x, np.float32).astype(ml_dtypes.bfloat16).astype(np.float64), axis, -1)
    blocks = v.reshape(v.shape[:-1] + (-1, 32))
    amax = np.abs(blocks).max(-1, keepdims=True)
    byte = np.maximum(np.where(amax > 0, np.frexp(amax)[1] - 1 + 127, 0) - down, 1)
    scale = np.exp2(byte - 127.0)
    codes = (blocks / scale).astype(np.float32).astype(dtype).astype(np.float64)
    return np.moveaxis((codes * scale).reshape(v.shape), -1, axis)


WIDE = False


def mx_kscale(k):
    if not WIDE:
        return np.ones(k)
    levels = np.array([30, -30])
    if k % 512:
        return np.exp2(np.random.permutation(np.resize(levels, k // 32))).repeat(32)
    a = np.empty((k // 512, 16))
    for p in range(k // 512):
        a[p, :8] = np.random.permutation(np.resize(levels, 8))
        for g in range(8):
            far = levels[np.abs(levels - a[p, g]) >= 10]
            a[p, g + 8] = far[np.random.randint(len(far))]
    return np.exp2(a.ravel()).repeat(32)


def f64(x):
    return np.asarray(x).astype(np.float64)


E2M1 = np.array([0.0, 0.5, 1.0, 1.5, 2.0, 3.0, 4.0, 6.0, -0.0, -0.5, -1.0, -1.5, -2.0, -3.0, -4.0, -6.0])


def pack_weight(w, fmt):
    k, n = w.shape
    w = f64(np.asarray(w, np.float32).astype(ml_dtypes.bfloat16)).reshape(k // 32, 32, n)
    amax = np.abs(w).max(1)
    if fmt == "e4m3":
        byte = np.frexp(amax)[1] - 1 + 127 - 7
    else:
        mant, ex = np.frexp(amax / 6.0)
        byte = np.where(mant > 0.5, ex, ex - 1) + 127
    byte = np.clip(np.where(amax > 0, byte, 1), 1, 254)
    scaled = (w * np.exp2(127.0 - byte)[:, None, :]).reshape(k, n).astype(np.float32)
    by_word = np.ascontiguousarray(scaled.reshape(k // 512, 128, 4, n).transpose(0, 1, 3, 2))
    if fmt == "e4m3":
        words = by_word.astype(ml_dtypes.float8_e4m3fn).view(np.uint8)
    else:
        c = by_word.astype(ml_dtypes.float4_e2m1fn).view(np.uint8) & 0xF
        words = (c[..., 0::2] | (c[..., 1::2] << 4)).reshape(k // 512, 128, 2 * n)
    return np.ascontiguousarray(words), np.ascontiguousarray(byte.astype(np.uint8).reshape(k // 512, 16, n))


def unpack_weight(words, scales, fmt):
    g, _, n = scales.shape
    words = np.ascontiguousarray(words).reshape(g, 128, n, -1)
    if fmt == "e4m3":
        vals = words.view(ml_dtypes.float8_e4m3fn).astype(np.float64)
    else:
        nib = np.empty((g, 128, n, 4), np.uint8)
        nib[..., 0::2] = words & 0xF
        nib[..., 1::2] = words >> 4
        vals = E2M1[nib]
    vals = vals * np.repeat(np.exp2(scales.astype(np.float64) - 127.0), 8, axis=1)[..., None]
    return vals.transpose(0, 1, 3, 2).reshape(g * 512, n)


K, N, T = 512, 512, 1024


def setup_inputs():
    n = np.random.standard_normal
    s = mx_kscale(K)[:, None]
    m = np.exp(0.5 * n((1, T)))
    p_w8 = pack_weight(n((K, N)) / np.sqrt(K) / s, "e4m3")
    return {
        "g": (m * n((K, T)) * s).astype(np.float32),
        "w8_words": p_w8[0],
        "w8_scales": p_w8[1],
        "d": (0.5 + 0.3 * n((N, T))).astype(np.float32),
    }


def reference(g, w8_words, w8_scales, d):
    g_q_ = mxq(f64(g), 0, "e5m2")
    g_r_ = mxq(f64(g) - g_q_, 0, "e4m3")
    w8_ = unpack_weight(w8_words, w8_scales, "e4m3")
    dx = w8_.T @ g_q_ + w8_.T @ g_r_
    return dx * f64(d)

@@ -1,0 +1,215 @@
+from contextlib import ExitStack
+
+import concourse.mybir as mybir
+
+K, N, T = 512, 512, 1024
+FLOPS = 2 * 2 * K * N * T
+
+F32 = mybir.dt.float32
+BF16 = mybir.dt.bfloat16
+I32 = mybir.dt.int32
+U32 = mybir.dt.uint32
+U8 = mybir.dt.uint8
+E4M3 = mybir.dt.float8_e4m3fn_x4
+E5M2 = mybir.dt.float8_e5m2_x4
+ALU = mybir.AluOpType
+
+P = 128
+PACK = 4
+CHUNK = 256
+HALF = 512
+RUN = 4
+VECTOR_SHARE = 160
+WARMUP = 5
+
+
+def tile_mix_tierg_mul_kernel(tc, g, w8_words, w8_scales, d, out):
+    nc = tc.nc
+    n_chunks = T // CHUNK
+    n_tiles = N // P
+
+    with ExitStack() as ctx:
+        sb = ctx.enter_context(tc.tile_pool(name="sb", bufs=1))
+        psum = ctx.enter_context(tc.psum_pool(name="psum", bufs=1))
+        ctx.enter_context(tc.manual_schedule())
+
+        g_raw = [sb.tile([P, PACK, CHUNK], F32, name="g_raw%d" % c, align_bytes=64) for c in range(n_chunks)]
+        g_bf = [sb.tile([P, CHUNK, PACK], BF16, name="g_bf%d" % c, align_bytes=64) for c in range(n_chunks)]
+        r_rows = [sb.tile([P, PACK, CHUNK], BF16, name="r_rows%d" % c, align_bytes=64) for c in range(n_chunks)]
+        r_bf = [sb.tile([P, CHUNK, PACK], BF16, name="r_bf%d" % c, align_bytes=64) for c in range(n_chunks)]
+        q_codes = sb.tile([P, T], U32, name="q_codes", align_bytes=64)
+        q_scales = sb.tile([P, T], U8, name="q_scales", align_bytes=64)
+        r_codes = sb.tile([P, T], U32, name="r_codes", align_bytes=64)
+        r_scales = sb.tile([P, T], U8, name="r_scales", align_bytes=64)
+        w_codes = sb.tile([P, N], I32, name="w_codes", align_bytes=64)
+        w_scales = sb.tile([P, N], U8, name="w_scales", align_bytes=64)
+        d_sb = [sb.tile([P, n_tiles, HALF], F32, name="d_sb%d" % h, align_bytes=64) for h in range(2)]
+        ramp = sb.tile([P, K], BF16, name="ramp", align_bytes=64)
+        eye_bf = sb.tile([P, PACK * K], BF16, name="eye_bf", align_bytes=64)
+        eye_codes = sb.tile([P, K], U32, name="eye_codes", align_bytes=64)
+        eye_scales = sb.tile([P, K], U8, name="eye_scales", align_bytes=64)
+        warm_in = sb.tile([P, 8], F32, name="warm_in")
+        warm_out = sb.tile([P, 8], F32, name="warm_out")
+
+        def bank(b):
+            return psum.tile([P, HALF], F32, name="bank%d" % b, tag="bank%d" % b)
+
+        g_view = g.rearrange("(p j) t -> p j t", j=PACK)
+        for c in range(n_chunks):
+            nc.sync.dma_start(out=g_raw[c][:], in_=g_view[:, :, c * CHUNK : (c + 1) * CHUNK])
+        nc.gpsimd.iota(ramp[:], pattern=[[1, K]], base=0, channel_multiplier=-PACK, allow_small_or_imprecise_dtypes=True)
+        nc.vector.memset(warm_in[:], 0.0)
+        nc.scalar.copy(out=warm_out[:], in_=warm_in[:])
+        nc.vector.memset(w_scales[:].bitcast(I32), 0)
+        for q in range(4):
+            nc.sync.dma_start(
+                out=w_scales[32 * q : 32 * q + 4, :].bitcast(I32),
+                in_=w8_scales[0, 4 * q : 4 * q + 4, :].bitcast(I32),
+            )
+        nc.sync.dma_start(out=w_codes[:], in_=w8_words[0].rearrange("p n i -> p (n i)").bitcast(I32))
+        d_view = d.rearrange("(m p) t -> p m t", p=P)
+        for h in range(2):
+            nc.sync.dma_start(out=d_sb[h][:], in_=d_view[:, :, h * HALF : (h + 1) * HALF])
+
+        for j in range(PACK):
+            nc.vector.tensor_scalar(
+                out=eye_bf[:, j * K : (j + 1) * K], in0=ramp[:], scalar1=float(j), scalar2=None, op0=ALU.is_equal
+            )
+        for u in range(2):
+            nc.vector.quantize_mx(
+                out=eye_codes[:, u * 256 : (u + 1) * 256].bitcast(E4M3),
+                scales=eye_scales[:, u * 256 : (u + 1) * 256],
+                in_=eye_bf[:, u * 1024 : (u + 1) * 1024],
+            )
+        warm_bank = bank(7)
+        for i in range(WARMUP):
+            nc.tensor.matmul_mx(
+                out=warm_bank[:],
+                lhsT=eye_codes[:, 0:P].bitcast(E4M3),
+                lhsT_scale=eye_scales[:, 0:P],
+                rhs=eye_codes[:].bitcast(E4M3),
+                rhs_scale=eye_scales[:],
+                start=True,
+                stop=True,
+            )
+
+        def interleave(copy, dst, src, lo, hi):
+            copy(
+                out=dst[:, lo:hi, :].rearrange("p (c i) j -> p c j i", i=RUN),
+                in_=src[:, :, lo:hi].rearrange("p j (c i) -> p c j i", i=RUN),
+            )
+
+        def cast(c, share):
+            if share > 0:
+                interleave(nc.vector.tensor_copy, g_bf[c], g_raw[c], 0, share)
+            interleave(nc.scalar.copy, g_bf[c], g_raw[c], share, CHUNK)
+
+        def quantize(codes, scales, fmt, src, c):
+            cols = slice(c * CHUNK, (c + 1) * CHUNK)
+            nc.vector.quantize_mx(
+                out=codes[:, cols].bitcast(fmt), scales=scales[:, cols], in_=src[c][:].rearrange("p t j -> p (t j)")
+            )
+
+        def quant_q(c):
+            quantize(q_codes, q_scales, E5M2, g_bf, c)
+
+        def quant_r(c):
+            quantize(r_codes, r_scales, E4M3, r_bf, c)
+
+        def dequantize(h):
+            cols = slice(h * HALF, (h + 1) * HALF)
+            banks = []
+            for j in range(PACK):
+                values = bank(4 * h + j)
+                nc.tensor.matmul_mx(
+                    out=values[:],
+                    lhsT=eye_codes[:, j * P : (j + 1) * P].bitcast(E4M3),
+                    lhsT_scale=eye_scales[:, j * P : (j + 1) * P],
+                    rhs=q_codes[:, cols].bitcast(E5M2),
+                    rhs_scale=q_scales[:, cols],
+                    start=True,
+                    stop=True,
+                )
+                banks.append(values)
+            return banks
+
+        def subtract(c, banks):
+            lo = (c % 2) * CHUNK
+            for j in range(PACK):
+                nc.vector.tensor_tensor(
+                    out=r_rows[c][:, j, :], in0=g_raw[c][:, j, :], in1=banks[j][:, lo : lo + CHUNK], op=ALU.subtract
+                )
+
+        def regroup(c):
+            interleave(nc.scalar.copy, r_bf[c], r_rows[c], 0, CHUNK)
+
+        def first_tier(h):
+            cols = slice(h * HALF, (h + 1) * HALF)
+            banks = []
+            for m in range(n_tiles):
+                acc = bank(4 * h + m)
+                nc.tensor.matmul_mx(
+                    out=acc[:],
+                    lhsT=w_codes[:, m * P : (m + 1) * P].bitcast(E4M3),
+                    lhsT_scale=w_scales[:, m * P : (m + 1) * P],
+                    rhs=q_codes[:, cols].bitcast(E5M2),
+                    rhs_scale=q_scales[:, cols],
+                    start=True,
+                    stop=False,
+                )
+                banks.append(acc)
+            return banks
+
+        def second_tier(c, banks):
+            cols = slice(c * CHUNK, (c + 1) * CHUNK)
+            lo = (c % 2) * CHUNK
+            for m in range(n_tiles):
+                nc.tensor.matmul_mx(
+                    out=banks[m][:, lo : lo + CHUNK],
+                    lhsT=w_codes[:, m * P : (m + 1) * P].bitcast(E4M3),
+                    lhsT_scale=w_scales[:, m * P : (m + 1) * P],
+                    rhs=r_codes[:, cols].bitcast(E4M3),
+                    rhs_scale=r_scales[:, cols],
+                    start=False,
+                    stop=(c % 2 == 1),
+                )
+
+        def finish(h, m, banks):
+            result = sb.tile([P, HALF], F32, name="result%d_%d" % (h, m), align_bytes=64)
+            nc.vector.tensor_tensor(out=result[:], in0=d_sb[h][:, m, :], in1=banks[m][:], op=ALU.mult)
+            nc.sync.dma_start(out=out[m * P : (m + 1) * P, h * HALF : (h + 1) * HALF], in_=result[:])
+
+        cast(0, VECTOR_SHARE)
+        quant_q(0)
+        cast(1, VECTOR_SHARE)
+        quant_q(1)
+        values0 = dequantize(0)
+        cast(2, 0)
+        cast(3, 0)
+        subtract(0, values0)
+        quant_q(2)
+        regroup(0)
+        subtract(1, values0)
+        quant_q(3)
+        values1 = dequantize(1)
+        acc0 = first_tier(0)
+        regroup(1)
+        quant_r(0)
+        second_tier(0, acc0)
+        subtract(2, values1)
+        regroup(2)
+        quant_r(1)
+        second_tier(1, acc0)
+        subtract(3, values1)
+        regroup(3)
+        acc1 = first_tier(1)
+        quant_r(2)
+        second_tier(2, acc1)
+        finish(0, 0, acc0)
+        finish(0, 1, acc0)
+        quant_r(3)
+        second_tier(3, acc1)
+        finish(0, 2, acc0)
+        finish(0, 3, acc0)
+        for m in range(n_tiles):
+            finish(1, m, acc1)

@@ -20,7 +20,7 @@ CHUNK = 256
 HALF = 512
 RUN = 4
 VECTOR_SHARE = 160
-WARMUP = 5
+WARMUP = 7
 
 
 def tile_mix_tierg_mul_kernel(tc, g, w8_words, w8_scales, d, out):
@@ -37,8 +37,8 @@ def tile_mix_tierg_mul_kernel(tc, g, w8_words, w8_scales, d, out):
         g_bf = [sb.tile([P, CHUNK, PACK], BF16, name="g_bf%d" % c, align_bytes=64) for c in range(n_chunks)]
         r_rows = [sb.tile([P, PACK, CHUNK], BF16, name="r_rows%d" % c, align_bytes=64) for c in range(n_chunks)]
         r_bf = [sb.tile([P, CHUNK, PACK], BF16, name="r_bf%d" % c, align_bytes=64) for c in range(n_chunks)]
-        q_codes = sb.tile([P, T], U32, name="q_codes", align_bytes=64)
-        q_scales = sb.tile([P, T], U8, name="q_scales", align_bytes=64)
+        q_codes = sb.tile([P, CHUNK + T], U32, name="q_codes", align_bytes=64)
+        q_scales = sb.tile([P, CHUNK + T], U8, name="q_scales", align_bytes=64)
         r_codes = sb.tile([P, T], U32, name="r_codes", align_bytes=64)
         r_scales = sb.tile([P, T], U8, name="r_scales", align_bytes=64)
         w_codes = sb.tile([P, N], I32, name="w_codes", align_bytes=64)
@@ -61,6 +61,8 @@ def tile_mix_tierg_mul_kernel(tc, g, w8_words, w8_scales, d, out):
         nc.vector.memset(warm_in[:], 0.0)
         nc.scalar.copy(out=warm_out[:], in_=warm_in[:])
         nc.vector.memset(w_scales[:].bitcast(I32), 0)
+        nc.vector.memset(q_codes[:, 0:CHUNK], 0)
+        nc.vector.memset(q_scales[:, 0:CHUNK].bitcast(I32), 0)
         for q in range(4):
             nc.sync.dma_start(
                 out=w_scales[32 * q : 32 * q + 4, :].bitcast(I32),
@@ -71,24 +73,32 @@ def tile_mix_tierg_mul_kernel(tc, g, w8_words, w8_scales, d, out):
         for h in range(2):
             nc.sync.dma_start(out=d_sb[h][:], in_=d_view[:, :, h * HALF : (h + 1) * HALF])
 
-        for j in range(PACK):
+        def eye_rows(j):
             nc.vector.tensor_scalar(
                 out=eye_bf[:, j * K : (j + 1) * K], in0=ramp[:], scalar1=float(j), scalar2=None, op0=ALU.is_equal
             )
-        for u in range(2):
+
+        def eye_quantize(u):
             nc.vector.quantize_mx(
                 out=eye_codes[:, u * 256 : (u + 1) * 256].bitcast(E4M3),
                 scales=eye_scales[:, u * 256 : (u + 1) * 256],
                 in_=eye_bf[:, u * 1024 : (u + 1) * 1024],
             )
-        warm_bank = bank(7)
+
+        eye_rows(0)
+        eye_rows(1)
+        eye_rows(2)
+        eye_quantize(0)
+        eye_rows(3)
+        eye_quantize(1)
+        warm_bank = bank(0)
         for i in range(WARMUP):
             nc.tensor.matmul_mx(
-                out=warm_bank[:],
+                out=warm_bank[:, 0:256],
                 lhsT=eye_codes[:, 0:P].bitcast(E4M3),
                 lhsT_scale=eye_scales[:, 0:P],
-                rhs=eye_codes[:].bitcast(E4M3),
-                rhs_scale=eye_scales[:],
+                rhs=eye_codes[:, 0:256].bitcast(E4M3),
+                rhs_scale=eye_scales[:, 0:256],
                 start=True,
                 stop=True,
             )
@@ -99,28 +109,40 @@ def tile_mix_tierg_mul_kernel(tc, g, w8_words, w8_scales, d, out):
                 in_=src[:, :, lo:hi].rearrange("p j (c i) -> p c j i", i=RUN),
             )
 
-        def cast(c, share):
+        def interleave_pool(dst, src, lo, hi):
+            nc.gpsimd.tensor_scalar(
+                out=dst[:, lo:hi, :],
+                in0=src[:, :, lo:hi].rearrange("p j t -> p t j"),
+                scalar1=1.0,
+                scalar2=0.0,
+                op0=ALU.mult,
+                op1=ALU.add,
+            )
+
+        def cast(c, share, pool_share=0):
             if share > 0:
                 interleave(nc.vector.tensor_copy, g_bf[c], g_raw[c], 0, share)
-            interleave(nc.scalar.copy, g_bf[c], g_raw[c], share, CHUNK)
+            if pool_share > 0:
+                interleave_pool(g_bf[c], g_raw[c], 0, pool_share)
+            interleave(nc.scalar.copy, g_bf[c], g_raw[c], share + pool_share, CHUNK)
 
-        def quantize(codes, scales, fmt, src, c):
-            cols = slice(c * CHUNK, (c + 1) * CHUNK)
+        def quantize(codes, scales, fmt, src, c, first):
+            cols = slice(first + c * CHUNK, first + (c + 1) * CHUNK)
             nc.vector.quantize_mx(
                 out=codes[:, cols].bitcast(fmt), scales=scales[:, cols], in_=src[c][:].rearrange("p t j -> p (t j)")
             )
 
         def quant_q(c):
-            quantize(q_codes, q_scales, E5M2, g_bf, c)
+            quantize(q_codes, q_scales, E5M2, g_bf, c, CHUNK)
 
         def quant_r(c):
-            quantize(r_codes, r_scales, E4M3, r_bf, c)
+            quantize(r_codes, r_scales, E4M3, r_bf, c, 0)
 
-        def dequantize(h):
-            cols = slice(h * HALF, (h + 1) * HALF)
+        def dequantize(first, first_bank):
+            cols = slice(first, first + HALF)
             banks = []
             for j in range(PACK):
-                values = bank(4 * h + j)
+                values = bank(first_bank + j)
                 nc.tensor.matmul_mx(
                     out=values[:],
                     lhsT=eye_codes[:, j * P : (j + 1) * P].bitcast(E4M3),
@@ -133,21 +155,27 @@ def tile_mix_tierg_mul_kernel(tc, g, w8_words, w8_scales, d, out):
                 banks.append(values)
             return banks
 
-        def subtract(c, banks):
-            lo = (c % 2) * CHUNK
-            for j in range(PACK):
+        def subtract(c, banks, lo, rows=(0, 1, 2, 3)):
+            for j in rows:
                 nc.vector.tensor_tensor(
                     out=r_rows[c][:, j, :], in0=g_raw[c][:, j, :], in1=banks[j][:, lo : lo + CHUNK], op=ALU.subtract
                 )
 
-        def regroup(c):
-            interleave(nc.scalar.copy, r_bf[c], r_rows[c], 0, CHUNK)
+        def regroup(c, pool_share=0):
+            if pool_share > 0:
+                interleave_pool(r_bf[c], r_rows[c], 0, pool_share)
+            interleave(nc.scalar.copy, r_bf[c], r_rows[c], pool_share, CHUNK)
+
+        def regroup_pool(c):
+            nc.gpsimd.tensor_scalar(
+                out=r_bf[c][:], in0=r_rows[c][:].rearrange("p j t -> p t j"), scalar1=1.0, scalar2=0.0, op0=ALU.mult, op1=ALU.add
+            )
 
         def first_tier(h):
-            cols = slice(h * HALF, (h + 1) * HALF)
+            cols = slice(CHUNK + h * HALF, CHUNK + (h + 1) * HALF)
             banks = []
             for m in range(n_tiles):
-                acc = bank(4 * h + m)
+                acc = bank(4 * (1 - h) + m)
                 nc.tensor.matmul_mx(
                     out=acc[:],
                     lhsT=w_codes[:, m * P : (m + 1) * P].bitcast(E4M3),
@@ -174,42 +202,54 @@ def tile_mix_tierg_mul_kernel(tc, g, w8_words, w8_scales, d, out):
                     stop=(c % 2 == 1),
                 )
 
-        def finish(h, m, banks):
+        def finish(h, m, banks, lo=0, hi=HALF):
+            result = sb.tile([P, hi - lo], F32, name="result%d_%d_%d" % (h, m, lo), align_bytes=64)
+            nc.vector.tensor_tensor(out=result[:], in0=d_sb[h][:, m, lo:hi], in1=banks[m][:, lo:hi], op=ALU.mult)
+            nc.sync.dma_start(out=out[m * P : (m + 1) * P, h * HALF + lo : h * HALF + hi], in_=result[:])
+
+        def finish_pool(h, m, banks):
+            sums = sb.tile([P, HALF], F32, name="sums%d_%d" % (h, m), align_bytes=64)
+            nc.scalar.copy(out=sums[:], in_=banks[m][:])
             result = sb.tile([P, HALF], F32, name="result%d_%d" % (h, m), align_bytes=64)
-            nc.vector.tensor_tensor(out=result[:], in0=d_sb[h][:, m, :], in1=banks[m][:], op=ALU.mult)
+            nc.gpsimd.tensor_tensor(out=result[:], in0=sums[:], in1=d_sb[h][:, m, :], op=ALU.mult)
             nc.sync.dma_start(out=out[m * P : (m + 1) * P, h * HALF : (h + 1) * HALF], in_=result[:])
 
         cast(0, VECTOR_SHARE)
         quant_q(0)
+        values0 = dequantize(0, 4)
         cast(1, VECTOR_SHARE)
         quant_q(1)
-        values0 = dequantize(0)
-        cast(2, 0)
-        cast(3, 0)
-        subtract(0, values0)
-        quant_q(2)
-        regroup(0)
-        subtract(1, values0)
-        quant_q(3)
-        values1 = dequantize(1)
+        values1 = dequantize(CHUNK, 0)
+        cast(2, 0, 128)
+        subtract(0, values0, CHUNK)
+        cast(3, 0, 128)
         acc0 = first_tier(0)
-        regroup(1)
+        regroup(0, 96)
+        subtract(1, values1, CHUNK, (0, 1))
+        quant_q(2)
+        quant_q(3)
+        subtract(1, values1, CHUNK, (2, 3))
+        regroup(1, 96)
+        values2 = dequantize(CHUNK + HALF, 0)
         quant_r(0)
         second_tier(0, acc0)
-        subtract(2, values1)
-        regroup(2)
+        subtract(2, values2, 0)
+        regroup(2, 96)
         quant_r(1)
         second_tier(1, acc0)
-        subtract(3, values1)
-        regroup(3)
+        subtract(3, values2, CHUNK)
+        regroup(3, 96)
         acc1 = first_tier(1)
-        quant_r(2)
-        second_tier(2, acc1)
         finish(0, 0, acc0)
         finish(0, 1, acc0)
+        quant_r(2)
+        second_tier(2, acc1)
         quant_r(3)
         second_tier(3, acc1)
         finish(0, 2, acc0)
         finish(0, 3, acc0)
-        for m in range(n_tiles):
-            finish(1, m, acc1)
+        finish(1, 0, acc1)
+        finish(1, 1, acc1)
+        finish(1, 2, acc1)
+        finish(1, 3, acc1, 0, CHUNK)
+        finish(1, 3, acc1, CHUNK, HALF)

@@ -161,10 +161,18 @@ def tile_mix_tierg_mul_kernel(tc, g, w8_words, w8_scales, d, out):
                     out=r_rows[c][:, j, :], in0=g_raw[c][:, j, :], in1=banks[j][:, lo : lo + CHUNK], op=ALU.subtract
                 )
 
-        def regroup(c, pool_share=0):
+        def regroup(c, pool_share=0, share=0):
             if pool_share > 0:
                 interleave_pool(r_bf[c], r_rows[c], 0, pool_share)
-            interleave(nc.scalar.copy, r_bf[c], r_rows[c], pool_share, CHUNK)
+            if share > 0:
+                interleave(nc.vector.tensor_copy, r_bf[c], r_rows[c], 0, share)
+            interleave(nc.scalar.copy, r_bf[c], r_rows[c], pool_share + share, CHUNK)
+
+        def subtract_pool(c, values):
+            lo = (c % 2) * CHUNK
+            nc.gpsimd.tensor_tensor(
+                out=r_rows[c][:, 0, :], in0=g_raw[c][:, 0, :], in1=values[:, lo : lo + CHUNK], op=ALU.subtract
+            )
 
         def regroup_pool(c):
             nc.gpsimd.tensor_scalar(
@@ -202,10 +210,10 @@ def tile_mix_tierg_mul_kernel(tc, g, w8_words, w8_scales, d, out):
                     stop=(c % 2 == 1),
                 )
 
-        def finish(h, m, banks, lo=0, hi=HALF):
+        def finish(h, m, banks, lo=0, hi=HALF, queue=nc.sync):
             result = sb.tile([P, hi - lo], F32, name="result%d_%d_%d" % (h, m, lo), align_bytes=64)
             nc.vector.tensor_tensor(out=result[:], in0=d_sb[h][:, m, lo:hi], in1=banks[m][:, lo:hi], op=ALU.mult)
-            nc.sync.dma_start(out=out[m * P : (m + 1) * P, h * HALF + lo : h * HALF + hi], in_=result[:])
+            queue.dma_start(out=out[m * P : (m + 1) * P, h * HALF + lo : h * HALF + hi], in_=result[:])
 
         def finish_pool(h, m, banks):
             sums = sb.tile([P, HALF], F32, name="sums%d_%d" % (h, m), align_bytes=64)
@@ -222,34 +230,37 @@ def tile_mix_tierg_mul_kernel(tc, g, w8_words, w8_scales, d, out):
         values1 = dequantize(CHUNK, 0)
         cast(2, 0, 128)
         subtract(0, values0, CHUNK)
-        cast(3, 0, 128)
-        acc0 = first_tier(0)
-        regroup(0, 96)
-        subtract(1, values1, CHUNK, (0, 1))
         quant_q(2)
+        cast(3, 0, 96)
+        acc0 = first_tier(0)
+        subtract(1, values1, CHUNK)
         quant_q(3)
-        subtract(1, values1, CHUNK, (2, 3))
-        regroup(1, 96)
+        regroup(0, 0, 128)
+        regroup(1, 0, 128)
         values2 = dequantize(CHUNK + HALF, 0)
         quant_r(0)
         second_tier(0, acc0)
-        subtract(2, values2, 0)
-        regroup(2, 96)
+        row0 = sb.tile([P, HALF], F32, name="row0", align_bytes=64)
+        nc.scalar.copy(out=row0[:], in_=values2[0][:])
         quant_r(1)
         second_tier(1, acc0)
-        subtract(3, values2, CHUNK)
+        subtract_pool(2, row0)
+        subtract_pool(3, row0)
+        subtract(2, values2, 0, (1, 2, 3))
+        regroup(2)
+        subtract(3, values2, CHUNK, (1, 2, 3))
         regroup(3, 96)
         acc1 = first_tier(1)
         finish(0, 0, acc0)
         finish(0, 1, acc0)
         quant_r(2)
         second_tier(2, acc1)
+        finish(0, 2, acc0)
         quant_r(3)
         second_tier(3, acc1)
-        finish(0, 2, acc0)
         finish(0, 3, acc0)
         finish(1, 0, acc1)
-        finish(1, 1, acc1)
+        finish(1, 1, acc1, 0, HALF, nc.scalar)
         finish(1, 2, acc1)
-        finish(1, 3, acc1, 0, CHUNK)
+        finish(1, 3, acc1, 0, CHUNK, nc.scalar)
         finish(1, 3, acc1, CHUNK, HALF)

@@ -20,7 +20,13 @@ CHUNK = 256
 HALF = 512
 RUN = 4
 VECTOR_SHARE = 160
-WARMUP = 7
+WARMUP = 3
+D_TILES = 2
+X = 192
+PC2 = 128
+PC3 = 144
+R0 = 64
+RAMP = 256
 
 
 def tile_mix_tierg_mul_kernel(tc, g, w8_words, w8_scales, d, out):
@@ -36,20 +42,20 @@ def tile_mix_tierg_mul_kernel(tc, g, w8_words, w8_scales, d, out):
         g_raw = [sb.tile([P, PACK, CHUNK], F32, name="g_raw%d" % c, align_bytes=64) for c in range(n_chunks)]
         g_bf = [sb.tile([P, CHUNK, PACK], BF16, name="g_bf%d" % c, align_bytes=64) for c in range(n_chunks)]
         r_rows = [sb.tile([P, PACK, CHUNK], BF16, name="r_rows%d" % c, align_bytes=64) for c in range(n_chunks)]
-        r_bf = [sb.tile([P, CHUNK, PACK], BF16, name="r_bf%d" % c, align_bytes=64) for c in range(n_chunks)]
-        q_codes = sb.tile([P, CHUNK + T], U32, name="q_codes", align_bytes=64)
-        q_scales = sb.tile([P, CHUNK + T], U8, name="q_scales", align_bytes=64)
+        r_bf = [sb.tile([P, CHUNK, PACK], BF16, name="r_bf%d" % c, align_bytes=64) for c in range(n_chunks - 1)]
+        r_bf.insert(2, r_bf[1])
+        codes = sb.tile([P, K + T], U32, name="codes", align_bytes=64)
+        scales = sb.tile([P, K + T], U8, name="scales", align_bytes=64)
+        eye_codes, eye_scales = codes[:, 0:K], scales[:, 0:K]
+        q_codes, q_scales = codes[:, K - CHUNK :], scales[:, K - CHUNK :]
         r_codes = sb.tile([P, T], U32, name="r_codes", align_bytes=64)
         r_scales = sb.tile([P, T], U8, name="r_scales", align_bytes=64)
         w_codes = sb.tile([P, N], I32, name="w_codes", align_bytes=64)
         w_scales = sb.tile([P, N], U8, name="w_scales", align_bytes=64)
-        d_sb = [sb.tile([P, n_tiles, HALF], F32, name="d_sb%d" % h, align_bytes=64) for h in range(2)]
-        ramp = sb.tile([P, K], BF16, name="ramp", align_bytes=64)
+        d_sb = [[sb.tile([P, D_TILES, HALF], F32, name="d_sb%d_%d" % (h, u), align_bytes=64) for u in range(n_tiles // D_TILES)] for h in range(2)]
+        ramp = sb.tile([P, RAMP], BF16, name="ramp", align_bytes=64)
         eye_bf = sb.tile([P, PACK * K], BF16, name="eye_bf", align_bytes=64)
-        eye_codes = sb.tile([P, K], U32, name="eye_codes", align_bytes=64)
-        eye_scales = sb.tile([P, K], U8, name="eye_scales", align_bytes=64)
-        warm_in = sb.tile([P, 8], F32, name="warm_in")
-        warm_out = sb.tile([P, 8], F32, name="warm_out")
+        q_rows = sb.tile([P, PACK, CHUNK], F32, name="q_rows", align_bytes=64)
 
         def bank(b):
             return psum.tile([P, HALF], F32, name="bank%d" % b, tag="bank%d" % b)
@@ -57,26 +63,17 @@ def tile_mix_tierg_mul_kernel(tc, g, w8_words, w8_scales, d, out):
         g_view = g.rearrange("(p j) t -> p j t", j=PACK)
         for c in range(n_chunks):
             nc.sync.dma_start(out=g_raw[c][:], in_=g_view[:, :, c * CHUNK : (c + 1) * CHUNK])
-        nc.gpsimd.iota(ramp[:], pattern=[[1, K]], base=0, channel_multiplier=-PACK, allow_small_or_imprecise_dtypes=True)
-        nc.vector.memset(warm_in[:], 0.0)
-        nc.scalar.copy(out=warm_out[:], in_=warm_in[:])
-        nc.vector.memset(w_scales[:].bitcast(I32), 0)
-        nc.vector.memset(q_codes[:, 0:CHUNK], 0)
-        nc.vector.memset(q_scales[:, 0:CHUNK].bitcast(I32), 0)
-        for q in range(4):
-            nc.sync.dma_start(
-                out=w_scales[32 * q : 32 * q + 4, :].bitcast(I32),
-                in_=w8_scales[0, 4 * q : 4 * q + 4, :].bitcast(I32),
-            )
-        nc.sync.dma_start(out=w_codes[:], in_=w8_words[0].rearrange("p n i -> p (n i)").bitcast(I32))
-        d_view = d.rearrange("(m p) t -> p m t", p=P)
-        for h in range(2):
-            nc.sync.dma_start(out=d_sb[h][:], in_=d_view[:, :, h * HALF : (h + 1) * HALF])
+        nc.gpsimd.iota(ramp[:], pattern=[[1, RAMP]], base=RAMP // 2, channel_multiplier=-PACK, allow_small_or_imprecise_dtypes=True)
 
         def eye_rows(j):
-            nc.vector.tensor_scalar(
-                out=eye_bf[:, j * K : (j + 1) * K], in0=ramp[:], scalar1=float(j), scalar2=None, op0=ALU.is_equal
-            )
+            for lo in range(0, K, RAMP):
+                nc.vector.tensor_scalar(
+                    out=eye_bf[:, j * K + lo : j * K + lo + RAMP],
+                    in0=ramp[:],
+                    scalar1=float(RAMP // 2 + j - lo),
+                    scalar2=None,
+                    op0=ALU.is_equal,
+                )
 
         def eye_quantize(u):
             nc.vector.quantize_mx(
@@ -85,51 +82,61 @@ def tile_mix_tierg_mul_kernel(tc, g, w8_words, w8_scales, d, out):
                 in_=eye_bf[:, u * 1024 : (u + 1) * 1024],
             )
 
-        eye_rows(0)
-        eye_rows(1)
-        eye_rows(2)
+        for j in range(PACK):
+            eye_rows(j)
         eye_quantize(0)
-        eye_rows(3)
         eye_quantize(1)
+        nc.vector.memset(w_scales[:].bitcast(I32), 0)
+        for q in range(4):
+            nc.sync.dma_start(
+                out=w_scales[32 * q : 32 * q + 4, :].bitcast(I32),
+                in_=w8_scales[0, 4 * q : 4 * q + 4, :].bitcast(I32),
+            )
+        nc.sync.dma_start(out=w_codes[:], in_=w8_words[0].rearrange("p n i -> p (n i)").bitcast(I32))
+        out_view = out.rearrange("(m p) t -> p m t", p=P)
+        d_view = d.rearrange("(m p) t -> p m t", p=P)
+        for h in range(2):
+            for u in range(n_tiles // D_TILES):
+                nc.sync.dma_start(out=d_sb[h][u][:], in_=d_view[:, u * D_TILES : (u + 1) * D_TILES, h * HALF : (h + 1) * HALF])
+
         warm_bank = bank(0)
-        for i in range(WARMUP):
+        for width in [CHUNK] + [HALF] * WARMUP:
             nc.tensor.matmul_mx(
-                out=warm_bank[:, 0:256],
+                out=warm_bank[:, 0:width],
                 lhsT=eye_codes[:, 0:P].bitcast(E4M3),
                 lhsT_scale=eye_scales[:, 0:P],
-                rhs=eye_codes[:, 0:256].bitcast(E4M3),
-                rhs_scale=eye_scales[:, 0:256],
+                rhs=eye_codes[:, 0:width].bitcast(E4M3),
+                rhs_scale=eye_scales[:, 0:width],
                 start=True,
                 stop=True,
             )
 
-        def interleave(copy, dst, src, lo, hi):
-            copy(
-                out=dst[:, lo:hi, :].rearrange("p (c i) j -> p c j i", i=RUN),
-                in_=src[:, :, lo:hi].rearrange("p j (c i) -> p c j i", i=RUN),
-            )
+        def grouped(tile, lo, hi):
+            return tile[:, lo:hi, :].rearrange("p (c i) j -> p c j i", i=RUN)
 
-        def interleave_pool(dst, src, lo, hi):
+        def rows(tile, lo, hi):
+            return tile[:, :, lo:hi].rearrange("p j (c i) -> p c j i", i=RUN)
+
+        def cast_vector(c, lo, hi):
+            nc.vector.tensor_copy(out=grouped(g_bf[c], lo, hi), in_=rows(g_raw[c], lo, hi))
+
+        def cast_scalar(c, lo, hi):
+            nc.scalar.copy(out=grouped(g_bf[c], lo, hi), in_=rows(g_raw[c], lo, hi))
+
+        def cast_pool(c, lo, hi):
             nc.gpsimd.tensor_scalar(
-                out=dst[:, lo:hi, :],
-                in0=src[:, :, lo:hi].rearrange("p j t -> p t j"),
+                out=g_bf[c][:, lo:hi, :],
+                in0=g_raw[c][:, :, lo:hi].rearrange("p j t -> p t j"),
                 scalar1=1.0,
                 scalar2=0.0,
                 op0=ALU.mult,
                 op1=ALU.add,
             )
 
-        def cast(c, share, pool_share=0):
-            if share > 0:
-                interleave(nc.vector.tensor_copy, g_bf[c], g_raw[c], 0, share)
-            if pool_share > 0:
-                interleave_pool(g_bf[c], g_raw[c], 0, pool_share)
-            interleave(nc.scalar.copy, g_bf[c], g_raw[c], share + pool_share, CHUNK)
-
-        def quantize(codes, scales, fmt, src, c, first):
+        def quantize(words, plane, fmt, src, c, first):
             cols = slice(first + c * CHUNK, first + (c + 1) * CHUNK)
             nc.vector.quantize_mx(
-                out=codes[:, cols].bitcast(fmt), scales=scales[:, cols], in_=src[c][:].rearrange("p t j -> p (t j)")
+                out=words[:, cols].bitcast(fmt), scales=plane[:, cols], in_=src[c][:].rearrange("p t j -> p (t j)")
             )
 
         def quant_q(c):
@@ -138,129 +145,171 @@ def tile_mix_tierg_mul_kernel(tc, g, w8_words, w8_scales, d, out):
         def quant_r(c):
             quantize(r_codes, r_scales, E4M3, r_bf, c, 0)
 
-        def dequantize(first, first_bank):
-            cols = slice(first, first + HALF)
-            banks = []
-            for j in range(PACK):
-                values = bank(first_bank + j)
-                nc.tensor.matmul_mx(
-                    out=values[:],
-                    lhsT=eye_codes[:, j * P : (j + 1) * P].bitcast(E4M3),
-                    lhsT_scale=eye_scales[:, j * P : (j + 1) * P],
-                    rhs=q_codes[:, cols].bitcast(E5M2),
-                    rhs_scale=q_scales[:, cols],
-                    start=True,
-                    stop=True,
-                )
-                banks.append(values)
-            return banks
+        def dequantize(last, j, b):
+            cols = slice(last * CHUNK, last * CHUNK + HALF)
+            values = bank(b)
+            nc.tensor.matmul_mx(
+                out=values[:],
+                lhsT=eye_codes[:, j * P : (j + 1) * P].bitcast(E4M3),
+                lhsT_scale=eye_scales[:, j * P : (j + 1) * P],
+                rhs=q_codes[:, cols].bitcast(E5M2),
+                rhs_scale=q_scales[:, cols],
+                start=True,
+                stop=True,
+            )
+            return values
 
-        def subtract(c, banks, lo, rows=(0, 1, 2, 3)):
-            for j in rows:
-                nc.vector.tensor_tensor(
-                    out=r_rows[c][:, j, :], in0=g_raw[c][:, j, :], in1=banks[j][:, lo : lo + CHUNK], op=ALU.subtract
-                )
-
-        def regroup(c, pool_share=0, share=0):
-            if pool_share > 0:
-                interleave_pool(r_bf[c], r_rows[c], 0, pool_share)
-            if share > 0:
-                interleave(nc.vector.tensor_copy, r_bf[c], r_rows[c], 0, share)
-            interleave(nc.scalar.copy, r_bf[c], r_rows[c], pool_share + share, CHUNK)
-
-        def subtract_pool(c, values):
-            lo = (c % 2) * CHUNK
-            nc.gpsimd.tensor_tensor(
-                out=r_rows[c][:, 0, :], in0=g_raw[c][:, 0, :], in1=values[:, lo : lo + CHUNK], op=ALU.subtract
+        def subtract(c, j, values, at, lo=0, hi=CHUNK):
+            nc.vector.tensor_tensor(
+                out=r_rows[c][:, j, lo:hi], in0=g_raw[c][:, j, lo:hi], in1=values[:, at + lo : at + hi], op=ALU.subtract
             )
 
-        def regroup_pool(c):
+        def regroup(c, lo=0, hi=CHUNK):
+            nc.scalar.copy(out=grouped(r_bf[c], lo, hi), in_=rows(r_rows[c], lo, hi))
+
+        def regroup_vector(c, lo, hi):
+            nc.vector.tensor_copy(out=grouped(r_bf[c], lo, hi), in_=rows(r_rows[c], lo, hi))
+
+        def regroup_pool(c, lo, hi):
             nc.gpsimd.tensor_scalar(
-                out=r_bf[c][:], in0=r_rows[c][:].rearrange("p j t -> p t j"), scalar1=1.0, scalar2=0.0, op0=ALU.mult, op1=ALU.add
+                out=r_bf[c][:, lo:hi, :],
+                in0=r_rows[c][:, :, lo:hi].rearrange("p j t -> p t j"),
+                scalar1=1.0,
+                scalar2=0.0,
+                op0=ALU.mult,
+                op1=ALU.add,
             )
 
-        def first_tier(h):
-            cols = slice(CHUNK + h * HALF, CHUNK + (h + 1) * HALF)
-            banks = []
-            for m in range(n_tiles):
-                acc = bank(4 * (1 - h) + m)
-                nc.tensor.matmul_mx(
-                    out=acc[:],
-                    lhsT=w_codes[:, m * P : (m + 1) * P].bitcast(E4M3),
-                    lhsT_scale=w_scales[:, m * P : (m + 1) * P],
-                    rhs=q_codes[:, cols].bitcast(E5M2),
-                    rhs_scale=q_scales[:, cols],
-                    start=True,
-                    stop=False,
-                )
-                banks.append(acc)
-            return banks
+        def copy_values(j, values, at, hi):
+            nc.scalar.copy(out=q_rows[:, j, 0:hi], in_=values[:, at : at + hi])
 
-        def second_tier(c, banks):
-            cols = slice(c * CHUNK, (c + 1) * CHUNK)
-            lo = (c % 2) * CHUNK
-            for m in range(n_tiles):
-                nc.tensor.matmul_mx(
-                    out=banks[m][:, lo : lo + CHUNK],
-                    lhsT=w_codes[:, m * P : (m + 1) * P].bitcast(E4M3),
-                    lhsT_scale=w_scales[:, m * P : (m + 1) * P],
-                    rhs=r_codes[:, cols].bitcast(E4M3),
-                    rhs_scale=r_scales[:, cols],
-                    start=False,
-                    stop=(c % 2 == 1),
-                )
+        def subtract_pool(c, lo, hi):
+            nc.gpsimd.tensor_tensor(
+                out=grouped(r_bf[c], lo, hi), in0=rows(g_raw[c], lo, hi), in1=rows(q_rows, lo, hi), op=ALU.subtract
+            )
 
-        def finish(h, m, banks, lo=0, hi=HALF, queue=nc.sync):
-            result = sb.tile([P, hi - lo], F32, name="result%d_%d_%d" % (h, m, lo), align_bytes=64)
-            nc.vector.tensor_tensor(out=result[:], in0=d_sb[h][:, m, lo:hi], in1=banks[m][:, lo:hi], op=ALU.mult)
-            queue.dma_start(out=out[m * P : (m + 1) * P, h * HALF + lo : h * HALF + hi], in_=result[:])
+        def subtract_pool_into(dst, c, lo, hi):
+            nc.gpsimd.tensor_tensor(
+                out=grouped(dst, 0, hi - lo), in0=rows(g_raw[c], lo, hi), in1=rows(q_rows, lo, hi), op=ALU.subtract
+            )
 
-        def finish_pool(h, m, banks):
-            sums = sb.tile([P, HALF], F32, name="sums%d_%d" % (h, m), align_bytes=64)
-            nc.scalar.copy(out=sums[:], in_=banks[m][:])
-            result = sb.tile([P, HALF], F32, name="result%d_%d" % (h, m), align_bytes=64)
-            nc.gpsimd.tensor_tensor(out=result[:], in0=sums[:], in1=d_sb[h][:, m, :], op=ALU.mult)
-            nc.sync.dma_start(out=out[m * P : (m + 1) * P, h * HALF : (h + 1) * HALF], in_=result[:])
+        def quant_r_part(src, at, t0, width):
+            nc.vector.quantize_mx(
+                out=r_codes[:, t0 : t0 + width].bitcast(E4M3),
+                scales=r_scales[:, t0 : t0 + width],
+                in_=src[:, at : at + width, :].rearrange("p t j -> p (t j)"),
+            )
 
-        cast(0, VECTOR_SHARE)
+        def finish_pair(u, accs, t0, queue):
+            result = sb.tile([P, 2, CHUNK], F32, name="pair%d_%d" % (u, t0), align_bytes=64)
+            for i in range(2):
+                m = 2 * u + i
+                nc.vector.tensor_tensor(out=result[:, i, :], in0=d_cols(m, t0, CHUNK), in1=accs[m][:, CHUNK:HALF], op=ALU.mult)
+            queue.dma_start(out=out_view[:, 2 * u : 2 * u + 2, t0 : t0 + CHUNK], in_=result[:])
+
+        def first_tier(last, m, b):
+            cols = slice(last * CHUNK, last * CHUNK + HALF)
+            acc = bank(b)
+            nc.tensor.matmul_mx(
+                out=acc[:],
+                lhsT=w_codes[:, m * P : (m + 1) * P].bitcast(E4M3),
+                lhsT_scale=w_scales[:, m * P : (m + 1) * P],
+                rhs=q_codes[:, cols].bitcast(E5M2),
+                rhs_scale=q_scales[:, cols],
+                start=True,
+                stop=False,
+            )
+            return acc
+
+        def second_tier(c, m, acc, at, stop, width=CHUNK):
+            cols = slice(c * CHUNK, c * CHUNK + width)
+            nc.tensor.matmul_mx(
+                out=acc[:, at : at + width],
+                lhsT=w_codes[:, m * P : (m + 1) * P].bitcast(E4M3),
+                lhsT_scale=w_scales[:, m * P : (m + 1) * P],
+                rhs=r_codes[:, cols].bitcast(E4M3),
+                rhs_scale=r_scales[:, cols],
+                start=False,
+                stop=stop,
+            )
+
+        def d_cols(m, t0, width):
+            return d_sb[t0 // HALF][m // D_TILES][:, m % D_TILES, t0 % HALF : t0 % HALF + width]
+
+        def store(m, t0, width, result, queue):
+            queue.dma_start(out=out[m * P : (m + 1) * P, t0 : t0 + width], in_=result)
+
+        def finish(m, acc, at, t0, width, queue=nc.sync):
+            result = sb.tile([P, width], F32, name="result%d_%d" % (m, t0), align_bytes=64)
+            nc.vector.tensor_tensor(out=result[:], in0=d_cols(m, t0, width), in1=acc[:, at : at + width], op=ALU.mult)
+            store(m, t0, width, result[:], queue)
+
+        def copy_sums(m, acc, at, t0, width):
+            sums = sb.tile([P, width], F32, name="sums%d_%d" % (m, t0), align_bytes=64)
+            nc.scalar.copy(out=sums[:], in_=acc[:, at : at + width])
+            return sums
+
+        def finish_pool(m, sums, t0, width):
+            result = sb.tile([P, width], F32, name="result%d_%d" % (m, t0), align_bytes=64)
+            nc.gpsimd.tensor_tensor(out=result[:], in0=sums[:], in1=d_cols(m, t0, width), op=ALU.mult)
+            return result
+
+        cast_vector(0, 0, VECTOR_SHARE)
+        cast_scalar(0, VECTOR_SHARE, CHUNK)
         quant_q(0)
-        values0 = dequantize(0, 4)
-        cast(1, VECTOR_SHARE)
+        values0 = [dequantize(0, j, j) for j in range(PACK)]
+        cast_vector(1, 0, VECTOR_SHARE)
+        cast_scalar(1, VECTOR_SHARE, CHUNK)
         quant_q(1)
-        values1 = dequantize(CHUNK, 0)
-        cast(2, 0, 128)
-        subtract(0, values0, CHUNK)
+        values1 = [dequantize(1, j, 4 + j) for j in range(PACK)]
+        cast_pool(2, 0, PC2)
+        cast_scalar(2, PC2, CHUNK)
+        for j in range(PACK):
+            subtract(0, j, values0[j], CHUNK)
         quant_q(2)
-        cast(3, 0, 96)
-        acc0 = first_tier(0)
-        subtract(1, values1, CHUNK)
+        values2 = [dequantize(2, j, j) for j in range(PACK)]
+        regroup(0, 0, R0)
+        cast_pool(3, 0, PC3)
+        cast_scalar(3, PC3, CHUNK)
+        for j in range(PACK):
+            subtract(1, j, values1[j], CHUNK)
+        regroup(0, R0, CHUNK)
         quant_q(3)
-        regroup(0, 0, 128)
-        regroup(1, 0, 128)
-        values2 = dequantize(CHUNK + HALF, 0)
+        values3 = [dequantize(3, j, 4 + j) for j in range(PACK)]
+        regroup_vector(1, 0, CHUNK)
+        for j in range(PACK):
+            copy_values(j, values2[j], CHUNK, CHUNK)
         quant_r(0)
-        second_tier(0, acc0)
-        row0 = sb.tile([P, HALF], F32, name="row0", align_bytes=64)
-        nc.scalar.copy(out=row0[:], in_=values2[0][:])
         quant_r(1)
-        second_tier(1, acc0)
-        subtract_pool(2, row0)
-        subtract_pool(3, row0)
-        subtract(2, values2, 0, (1, 2, 3))
-        regroup(2)
-        subtract(3, values2, CHUNK, (1, 2, 3))
-        regroup(3, 96)
-        acc1 = first_tier(1)
-        finish(0, 0, acc0)
-        finish(0, 1, acc0)
-        quant_r(2)
-        second_tier(2, acc1)
-        finish(0, 2, acc0)
+        acc0 = []
+        for m in range(n_tiles):
+            acc0.append(first_tier(1, m, m))
+            second_tier(0, m, acc0[m], 0, True, HALF)
+        subtract_pool(2, 0, X // 2)
+        subtract_pool(2, X // 2, X)
+        for lo in (0, 128):
+            for j in range(PACK):
+                subtract(3, j, values3[j], CHUNK, lo, lo + 128)
+            regroup(3, lo, lo + 128)
+        acc3 = [first_tier(3, m, 4 + m) for m in range(n_tiles)]
+        finish(0, acc0[0], 0, 0, HALF)
+        finish(1, acc0[1], 0, 0, HALF)
+        finish(2, acc0[2], 0, 0, HALF)
         quant_r(3)
-        second_tier(3, acc1)
-        finish(0, 3, acc0)
-        finish(1, 0, acc1)
-        finish(1, 1, acc1, 0, HALF, nc.scalar)
-        finish(1, 2, acc1)
-        finish(1, 3, acc1, 0, CHUNK, nc.scalar)
-        finish(1, 3, acc1, CHUNK, HALF)
+        for m in range(n_tiles):
+            second_tier(3, m, acc3[m], CHUNK, True)
+        subtract_pool_into(r_bf[3], 2, X, CHUNK)
+        quant_r_part(r_bf[2], 0, 2 * CHUNK, 128)
+        quant_r_part(r_bf[2], 128, 2 * CHUNK + 128, 64)
+        finish(3, acc0[3], 0, 0, HALF)
+        acc2 = [first_tier(2, m, m) for m in range(2)]
+        finish_pair(0, acc3, 3 * CHUNK, nc.scalar)
+        quant_r_part(r_bf[3], 0, 2 * CHUNK + X, 64)
+        for m in range(n_tiles):
+            if m >= 2:
+                acc2.append(first_tier(2, m, m))
+            second_tier(2, m, acc2[m], CHUNK, True)
+        finish_pair(1, acc3, 3 * CHUNK, nc.sync)
+        finish_pair(0, acc2, 2 * CHUNK, nc.scalar)
+        finish(2, acc2[2], CHUNK, 2 * CHUNK, CHUNK, nc.sync)
+        finish(3, acc2[3], CHUNK, 2 * CHUNK, CHUNK, nc.scalar)

@@ -22,11 +22,14 @@ RUN = 4
 VECTOR_SHARE = 160
 WARMUP = 3
 D_TILES = 2
-X = 192
+X = 208
 PC2 = 128
 PC3 = 144
 R0 = 64
 RAMP = 256
+GATE = 0
+NW = 3
+NB = 3
 
 
 def tile_mix_tierg_mul_kernel(tc, g, w8_words, w8_scales, d, out):
@@ -43,7 +46,7 @@ def tile_mix_tierg_mul_kernel(tc, g, w8_words, w8_scales, d, out):
         g_bf = [sb.tile([P, CHUNK, PACK], BF16, name="g_bf%d" % c, align_bytes=64) for c in range(n_chunks)]
         r_rows = [sb.tile([P, PACK, CHUNK], BF16, name="r_rows%d" % c, align_bytes=64) for c in range(n_chunks)]
         r_bf = [sb.tile([P, CHUNK, PACK], BF16, name="r_bf%d" % c, align_bytes=64) for c in range(n_chunks - 1)]
-        r_bf.insert(2, r_bf[1])
+        r_bf.insert(2, r_bf[GATE])
         codes = sb.tile([P, K + T], U32, name="codes", align_bytes=64)
         scales = sb.tile([P, K + T], U8, name="scales", align_bytes=64)
         eye_codes, eye_scales = codes[:, 0:K], scales[:, 0:K]
@@ -278,38 +281,37 @@ def tile_mix_tierg_mul_kernel(tc, g, w8_words, w8_scales, d, out):
         values3 = [dequantize(3, j, 4 + j) for j in range(PACK)]
         regroup_vector(1, 0, CHUNK)
         for j in range(PACK):
-            copy_values(j, values2[j], CHUNK, CHUNK)
+            copy_values(j, values2[j], CHUNK, X)
         quant_r(0)
         quant_r(1)
+        for j in range(PACK):
+            subtract(2, j, values2[j], CHUNK, X, CHUNK)
+        regroup(2, X, CHUNK)
         acc0 = []
         for m in range(n_tiles):
             acc0.append(first_tier(1, m, m))
             second_tier(0, m, acc0[m], 0, True, HALF)
-        subtract_pool(2, 0, X // 2)
-        subtract_pool(2, X // 2, X)
+        subtract_pool(2, 0, X)
+        for j in range(NW):
+            subtract(3, j, values3[j], CHUNK)
         for lo in (0, 128):
-            for j in range(PACK):
+            for j in range(NW, PACK):
                 subtract(3, j, values3[j], CHUNK, lo, lo + 128)
             regroup(3, lo, lo + 128)
-        acc3 = [first_tier(3, m, 4 + m) for m in range(n_tiles)]
+        acc1 = [first_tier(3, m, 4 + m) for m in range(NB)]
         finish(0, acc0[0], 0, 0, HALF)
         finish(1, acc0[1], 0, 0, HALF)
         finish(2, acc0[2], 0, 0, HALF)
         quant_r(3)
+        quant_r(2)
         for m in range(n_tiles):
-            second_tier(3, m, acc3[m], CHUNK, True)
-        subtract_pool_into(r_bf[3], 2, X, CHUNK)
-        quant_r_part(r_bf[2], 0, 2 * CHUNK, 128)
-        quant_r_part(r_bf[2], 128, 2 * CHUNK + 128, 64)
-        finish(3, acc0[3], 0, 0, HALF)
-        acc2 = [first_tier(2, m, m) for m in range(2)]
-        finish_pair(0, acc3, 3 * CHUNK, nc.scalar)
-        quant_r_part(r_bf[3], 0, 2 * CHUNK + X, 64)
-        for m in range(n_tiles):
-            if m >= 2:
-                acc2.append(first_tier(2, m, m))
-            second_tier(2, m, acc2[m], CHUNK, True)
-        finish_pair(1, acc3, 3 * CHUNK, nc.sync)
-        finish_pair(0, acc2, 2 * CHUNK, nc.scalar)
-        finish(2, acc2[2], CHUNK, 2 * CHUNK, CHUNK, nc.sync)
-        finish(3, acc2[3], CHUNK, 2 * CHUNK, CHUNK, nc.scalar)
+            if m >= NB:
+                acc1.append(first_tier(3, m, 4 + m))
+            second_tier(3, m, acc1[m], CHUNK, False)
+            second_tier(2, m, acc1[m], 0, True)
+        finish(3, acc0[3], 0, 0, HALF, nc.scalar)
+        finish(0, acc1[0], 0, HALF, HALF)
+        finish(1, acc1[1], 0, HALF, HALF, nc.scalar)
+        finish(2, acc1[2], 0, HALF, HALF)
+        finish(3, acc1[3], 0, HALF, CHUNK, nc.scalar)
+        finish(3, acc1[3], CHUNK, HALF + CHUNK, CHUNK)

@@ -17,19 +17,16 @@ ALU = mybir.AluOpType
 P = 128
 PACK = 4
 CHUNK = 256
-HALF = 512
+WINDOW = 512
 RUN = 4
-VECTOR_SHARE = 160
-WARMUP = 3
-D_TILES = 2
-X = 208
-PC2 = 128
-PC3 = 144
-R0 = 64
 RAMP = 256
-GATE = 0
-NW = 3
-NB = 3
+WARMUPS = 3
+
+CAST_VECTOR = 160
+CAST_POOL_2 = 128
+CAST_POOL_3 = 144
+REGROUP_EARLY = 64
+SUBTRACT_POOL = 224
 
 
 def tile_mix_tierg_mul_kernel(tc, g, w8_words, w8_scales, d, out):
@@ -42,74 +39,66 @@ def tile_mix_tierg_mul_kernel(tc, g, w8_words, w8_scales, d, out):
         psum = ctx.enter_context(tc.psum_pool(name="psum", bufs=1))
         ctx.enter_context(tc.manual_schedule())
 
-        g_raw = [sb.tile([P, PACK, CHUNK], F32, name="g_raw%d" % c, align_bytes=64) for c in range(n_chunks)]
-        g_bf = [sb.tile([P, CHUNK, PACK], BF16, name="g_bf%d" % c, align_bytes=64) for c in range(n_chunks)]
-        r_rows = [sb.tile([P, PACK, CHUNK], BF16, name="r_rows%d" % c, align_bytes=64) for c in range(n_chunks)]
-        r_bf = [sb.tile([P, CHUNK, PACK], BF16, name="r_bf%d" % c, align_bytes=64) for c in range(n_chunks - 1)]
-        r_bf.insert(2, r_bf[GATE])
-        codes = sb.tile([P, K + T], U32, name="codes", align_bytes=64)
-        scales = sb.tile([P, K + T], U8, name="scales", align_bytes=64)
-        eye_codes, eye_scales = codes[:, 0:K], scales[:, 0:K]
-        q_codes, q_scales = codes[:, K - CHUNK :], scales[:, K - CHUNK :]
-        r_codes = sb.tile([P, T], U32, name="r_codes", align_bytes=64)
-        r_scales = sb.tile([P, T], U8, name="r_scales", align_bytes=64)
-        w_codes = sb.tile([P, N], I32, name="w_codes", align_bytes=64)
-        w_scales = sb.tile([P, N], U8, name="w_scales", align_bytes=64)
-        d_sb = [[sb.tile([P, D_TILES, HALF], F32, name="d_sb%d_%d" % (h, u), align_bytes=64) for u in range(n_tiles // D_TILES)] for h in range(2)]
+        g_rows = [sb.tile([P, PACK, CHUNK], F32, name="g_rows%d" % c, align_bytes=64) for c in range(n_chunks)]
+        g_grouped = [sb.tile([P, CHUNK, PACK], BF16, name="g_grouped%d" % c, align_bytes=64) for c in range(n_chunks)]
+        r_rows = {c: sb.tile([P, PACK, CHUNK], BF16, name="r_rows%d" % c, align_bytes=64) for c in range(n_chunks)}
+        r_grouped = {c: sb.tile([P, CHUNK, PACK], BF16, name="r_grouped%d" % c, align_bytes=64) for c in (0, 1, 3)}
+        r_grouped[2] = r_grouped[0]
+        q2_rows = sb.tile([P, PACK, SUBTRACT_POOL], F32, name="q2_rows", align_bytes=64)
+
+        words = sb.tile([P, K + T], U32, name="words", align_bytes=64)
+        plane = sb.tile([P, K + T], U8, name="plane", align_bytes=64)
+        eye_words, eye_plane = words[:, 0:K], plane[:, 0:K]
+        r_words = sb.tile([P, T], U32, name="r_words", align_bytes=64)
+        r_plane = sb.tile([P, T], U8, name="r_plane", align_bytes=64)
+        w_words = sb.tile([P, N], I32, name="w_words", align_bytes=64)
+        w_plane = sb.tile([P, N], U8, name="w_plane", align_bytes=64)
+        d_sb = [sb.tile([P, T], F32, name="d_sb%d" % m, align_bytes=64) for m in range(n_tiles)]
         ramp = sb.tile([P, RAMP], BF16, name="ramp", align_bytes=64)
-        eye_bf = sb.tile([P, PACK * K], BF16, name="eye_bf", align_bytes=64)
-        q_rows = sb.tile([P, PACK, CHUNK], F32, name="q_rows", align_bytes=64)
+        eye_grouped = sb.tile([P, PACK * K], BF16, name="eye_grouped", align_bytes=64)
 
         def bank(b):
-            return psum.tile([P, HALF], F32, name="bank%d" % b, tag="bank%d" % b)
+            return psum.tile([P, WINDOW], F32, name="bank%d" % b, tag="bank%d" % b)
 
         g_view = g.rearrange("(p j) t -> p j t", j=PACK)
         for c in range(n_chunks):
-            nc.sync.dma_start(out=g_raw[c][:], in_=g_view[:, :, c * CHUNK : (c + 1) * CHUNK])
-        nc.gpsimd.iota(ramp[:], pattern=[[1, RAMP]], base=RAMP // 2, channel_multiplier=-PACK, allow_small_or_imprecise_dtypes=True)
+            nc.sync.dma_start(out=g_rows[c][:], in_=g_view[:, :, c * CHUNK : (c + 1) * CHUNK])
 
-        def eye_rows(j):
-            for lo in range(0, K, RAMP):
+        nc.gpsimd.iota(ramp[:], pattern=[[1, RAMP]], base=RAMP // 2, channel_multiplier=-PACK, allow_small_or_imprecise_dtypes=True)
+        for j in range(PACK):
+            for x in range(0, K, RAMP):
                 nc.vector.tensor_scalar(
-                    out=eye_bf[:, j * K + lo : j * K + lo + RAMP],
+                    out=eye_grouped[:, j * K + x : j * K + x + RAMP],
                     in0=ramp[:],
-                    scalar1=float(RAMP // 2 + j - lo),
+                    scalar1=float(RAMP // 2 + j - x),
                     scalar2=None,
                     op0=ALU.is_equal,
                 )
-
-        def eye_quantize(u):
+        for first in range(0, K, CHUNK):
             nc.vector.quantize_mx(
-                out=eye_codes[:, u * 256 : (u + 1) * 256].bitcast(E4M3),
-                scales=eye_scales[:, u * 256 : (u + 1) * 256],
-                in_=eye_bf[:, u * 1024 : (u + 1) * 1024],
+                out=eye_words[:, first : first + CHUNK].bitcast(E4M3),
+                scales=eye_plane[:, first : first + CHUNK],
+                in_=eye_grouped[:, PACK * first : PACK * (first + CHUNK)],
             )
 
-        for j in range(PACK):
-            eye_rows(j)
-        eye_quantize(0)
-        eye_quantize(1)
-        nc.vector.memset(w_scales[:].bitcast(I32), 0)
+        nc.vector.memset(w_plane[:].bitcast(I32), 0)
         for q in range(4):
             nc.sync.dma_start(
-                out=w_scales[32 * q : 32 * q + 4, :].bitcast(I32),
+                out=w_plane[32 * q : 32 * q + 4, :].bitcast(I32),
                 in_=w8_scales[0, 4 * q : 4 * q + 4, :].bitcast(I32),
             )
-        nc.sync.dma_start(out=w_codes[:], in_=w8_words[0].rearrange("p n i -> p (n i)").bitcast(I32))
-        out_view = out.rearrange("(m p) t -> p m t", p=P)
-        d_view = d.rearrange("(m p) t -> p m t", p=P)
-        for h in range(2):
-            for u in range(n_tiles // D_TILES):
-                nc.sync.dma_start(out=d_sb[h][u][:], in_=d_view[:, u * D_TILES : (u + 1) * D_TILES, h * HALF : (h + 1) * HALF])
+        nc.sync.dma_start(out=w_words[:], in_=w8_words[0].rearrange("p n i -> p (n i)").bitcast(I32))
+        for m in range(n_tiles):
+            nc.sync.dma_start(out=d_sb[m][:], in_=d[m * P : (m + 1) * P, :])
 
         warm_bank = bank(0)
-        for width in [CHUNK] + [HALF] * WARMUP:
+        for i in range(WARMUPS):
             nc.tensor.matmul_mx(
-                out=warm_bank[:, 0:width],
-                lhsT=eye_codes[:, 0:P].bitcast(E4M3),
-                lhsT_scale=eye_scales[:, 0:P],
-                rhs=eye_codes[:, 0:width].bitcast(E4M3),
-                rhs_scale=eye_scales[:, 0:width],
+                out=warm_bank[:],
+                lhsT=eye_words[:, 0:P].bitcast(E4M3),
+                lhsT_scale=eye_plane[:, 0:P],
+                rhs=eye_words.bitcast(E4M3),
+                rhs_scale=eye_plane,
                 start=True,
                 stop=True,
             )
@@ -120,198 +109,130 @@ def tile_mix_tierg_mul_kernel(tc, g, w8_words, w8_scales, d, out):
         def rows(tile, lo, hi):
             return tile[:, :, lo:hi].rearrange("p j (c i) -> p c j i", i=RUN)
 
-        def cast_vector(c, lo, hi):
-            nc.vector.tensor_copy(out=grouped(g_bf[c], lo, hi), in_=rows(g_raw[c], lo, hi))
+        def cast(copy, c, lo, hi):
+            copy(out=grouped(g_grouped[c], lo, hi), in_=rows(g_rows[c], lo, hi))
 
-        def cast_scalar(c, lo, hi):
-            nc.scalar.copy(out=grouped(g_bf[c], lo, hi), in_=rows(g_raw[c], lo, hi))
-
-        def cast_pool(c, lo, hi):
+        def cast_pool(c, hi):
             nc.gpsimd.tensor_scalar(
-                out=g_bf[c][:, lo:hi, :],
-                in0=g_raw[c][:, :, lo:hi].rearrange("p j t -> p t j"),
+                out=g_grouped[c][:, 0:hi, :],
+                in0=g_rows[c][:, :, 0:hi].rearrange("p j t -> p t j"),
                 scalar1=1.0,
                 scalar2=0.0,
                 op0=ALU.mult,
                 op1=ALU.add,
             )
 
-        def quantize(words, plane, fmt, src, c, first):
-            cols = slice(first + c * CHUNK, first + (c + 1) * CHUNK)
+        def quantise_q(c):
+            cols = slice(K + c * CHUNK, K + (c + 1) * CHUNK)
             nc.vector.quantize_mx(
-                out=words[:, cols].bitcast(fmt), scales=plane[:, cols], in_=src[c][:].rearrange("p t j -> p (t j)")
+                out=words[:, cols].bitcast(E5M2), scales=plane[:, cols], in_=g_grouped[c][:].rearrange("p t j -> p (t j)")
             )
 
-        def quant_q(c):
-            quantize(q_codes, q_scales, E5M2, g_bf, c, CHUNK)
-
-        def quant_r(c):
-            quantize(r_codes, r_scales, E4M3, r_bf, c, 0)
-
-        def dequantize(last, j, b):
-            cols = slice(last * CHUNK, last * CHUNK + HALF)
-            values = bank(b)
-            nc.tensor.matmul_mx(
-                out=values[:],
-                lhsT=eye_codes[:, j * P : (j + 1) * P].bitcast(E4M3),
-                lhsT_scale=eye_scales[:, j * P : (j + 1) * P],
-                rhs=q_codes[:, cols].bitcast(E5M2),
-                rhs_scale=q_scales[:, cols],
-                start=True,
-                stop=True,
-            )
-            return values
-
-        def subtract(c, j, values, at, lo=0, hi=CHUNK):
-            nc.vector.tensor_tensor(
-                out=r_rows[c][:, j, lo:hi], in0=g_raw[c][:, j, lo:hi], in1=values[:, at + lo : at + hi], op=ALU.subtract
-            )
-
-        def regroup(c, lo=0, hi=CHUNK):
-            nc.scalar.copy(out=grouped(r_bf[c], lo, hi), in_=rows(r_rows[c], lo, hi))
-
-        def regroup_vector(c, lo, hi):
-            nc.vector.tensor_copy(out=grouped(r_bf[c], lo, hi), in_=rows(r_rows[c], lo, hi))
-
-        def regroup_pool(c, lo, hi):
-            nc.gpsimd.tensor_scalar(
-                out=r_bf[c][:, lo:hi, :],
-                in0=r_rows[c][:, :, lo:hi].rearrange("p j t -> p t j"),
-                scalar1=1.0,
-                scalar2=0.0,
-                op0=ALU.mult,
-                op1=ALU.add,
-            )
-
-        def copy_values(j, values, at, hi):
-            nc.scalar.copy(out=q_rows[:, j, 0:hi], in_=values[:, at : at + hi])
-
-        def subtract_pool(c, lo, hi):
-            nc.gpsimd.tensor_tensor(
-                out=grouped(r_bf[c], lo, hi), in0=rows(g_raw[c], lo, hi), in1=rows(q_rows, lo, hi), op=ALU.subtract
-            )
-
-        def subtract_pool_into(dst, c, lo, hi):
-            nc.gpsimd.tensor_tensor(
-                out=grouped(dst, 0, hi - lo), in0=rows(g_raw[c], lo, hi), in1=rows(q_rows, lo, hi), op=ALU.subtract
-            )
-
-        def quant_r_part(src, at, t0, width):
+        def quantise_r(c):
+            cols = slice(c * CHUNK, (c + 1) * CHUNK)
             nc.vector.quantize_mx(
-                out=r_codes[:, t0 : t0 + width].bitcast(E4M3),
-                scales=r_scales[:, t0 : t0 + width],
-                in_=src[:, at : at + width, :].rearrange("p t j -> p (t j)"),
+                out=r_words[:, cols].bitcast(E4M3), scales=r_plane[:, cols], in_=r_grouped[c][:].rearrange("p t j -> p (t j)")
             )
 
-        def finish_pair(u, accs, t0, queue):
-            result = sb.tile([P, 2, CHUNK], F32, name="pair%d_%d" % (u, t0), align_bytes=64)
-            for i in range(2):
-                m = 2 * u + i
-                nc.vector.tensor_tensor(out=result[:, i, :], in0=d_cols(m, t0, CHUNK), in1=accs[m][:, CHUNK:HALF], op=ALU.mult)
-            queue.dma_start(out=out_view[:, 2 * u : 2 * u + 2, t0 : t0 + CHUNK], in_=result[:])
-
-        def first_tier(last, m, b):
-            cols = slice(last * CHUNK, last * CHUNK + HALF)
+        def q_pass(stationary, stationary_plane, i, c, b, stop):
+            cols = slice(K + (c + 1) * CHUNK - WINDOW, K + (c + 1) * CHUNK)
             acc = bank(b)
             nc.tensor.matmul_mx(
                 out=acc[:],
-                lhsT=w_codes[:, m * P : (m + 1) * P].bitcast(E4M3),
-                lhsT_scale=w_scales[:, m * P : (m + 1) * P],
-                rhs=q_codes[:, cols].bitcast(E5M2),
-                rhs_scale=q_scales[:, cols],
+                lhsT=stationary[:, i * P : (i + 1) * P].bitcast(E4M3),
+                lhsT_scale=stationary_plane[:, i * P : (i + 1) * P],
+                rhs=words[:, cols].bitcast(E5M2),
+                rhs_scale=plane[:, cols],
                 start=True,
-                stop=False,
+                stop=stop,
             )
             return acc
 
-        def second_tier(c, m, acc, at, stop, width=CHUNK):
-            cols = slice(c * CHUNK, c * CHUNK + width)
+        def dequantise(c):
+            return [q_pass(eye_words, eye_plane, j, c, PACK * (c % 2) + j, True) for j in range(PACK)]
+
+        def first_tier(m, c, b):
+            return q_pass(w_words, w_plane, m, c, b, False)
+
+        def second_tier(m, acc, t0, width, stop):
             nc.tensor.matmul_mx(
-                out=acc[:, at : at + width],
-                lhsT=w_codes[:, m * P : (m + 1) * P].bitcast(E4M3),
-                lhsT_scale=w_scales[:, m * P : (m + 1) * P],
-                rhs=r_codes[:, cols].bitcast(E4M3),
-                rhs_scale=r_scales[:, cols],
+                out=acc[:, t0 % WINDOW : t0 % WINDOW + width],
+                lhsT=w_words[:, m * P : (m + 1) * P].bitcast(E4M3),
+                lhsT_scale=w_plane[:, m * P : (m + 1) * P],
+                rhs=r_words[:, t0 : t0 + width].bitcast(E4M3),
+                rhs_scale=r_plane[:, t0 : t0 + width],
                 start=False,
                 stop=stop,
             )
 
-        def d_cols(m, t0, width):
-            return d_sb[t0 // HALF][m // D_TILES][:, m % D_TILES, t0 % HALF : t0 % HALF + width]
+        def subtract(c, js, lo, hi):
+            for j in js:
+                nc.vector.tensor_tensor(
+                    out=r_rows[c][:, j, lo:hi], in0=g_rows[c][:, j, lo:hi], in1=values[c][j][:, CHUNK + lo : CHUNK + hi], op=ALU.subtract
+                )
 
-        def store(m, t0, width, result, queue):
-            queue.dma_start(out=out[m * P : (m + 1) * P, t0 : t0 + width], in_=result)
+        def regroup(copy, c, lo, hi):
+            copy(out=grouped(r_grouped[c], lo, hi), in_=rows(r_rows[c], lo, hi))
 
-        def finish(m, acc, at, t0, width, queue=nc.sync):
-            result = sb.tile([P, width], F32, name="result%d_%d" % (m, t0), align_bytes=64)
-            nc.vector.tensor_tensor(out=result[:], in0=d_cols(m, t0, width), in1=acc[:, at : at + width], op=ALU.mult)
-            store(m, t0, width, result[:], queue)
+        def finish(m, h, acc, queue):
+            cols = slice(h * WINDOW, (h + 1) * WINDOW)
+            result = sb.tile([P, WINDOW], F32, name="result%d_%d" % (m, h), align_bytes=64)
+            nc.vector.tensor_tensor(out=result[:], in0=d_sb[m][:, cols], in1=acc[:], op=ALU.mult)
+            queue.dma_start(out=out[m * P : (m + 1) * P, cols], in_=result[:])
 
-        def copy_sums(m, acc, at, t0, width):
-            sums = sb.tile([P, width], F32, name="sums%d_%d" % (m, t0), align_bytes=64)
-            nc.scalar.copy(out=sums[:], in_=acc[:, at : at + width])
-            return sums
+        values = {}
+        for c in range(2):
+            cast(nc.vector.tensor_copy, c, 0, CAST_VECTOR)
+            cast(nc.scalar.copy, c, CAST_VECTOR, CHUNK)
+            quantise_q(c)
+            values[c] = dequantise(c)
+        cast_pool(2, CAST_POOL_2)
+        cast(nc.scalar.copy, 2, CAST_POOL_2, CHUNK)
+        subtract(0, range(PACK), 0, CHUNK)
+        quantise_q(2)
+        values[2] = dequantise(2)
+        regroup(nc.scalar.copy, 0, 0, REGROUP_EARLY)
+        cast_pool(3, CAST_POOL_3)
+        cast(nc.scalar.copy, 3, CAST_POOL_3, CHUNK)
+        subtract(1, range(PACK), 0, CHUNK)
+        regroup(nc.scalar.copy, 0, REGROUP_EARLY, CHUNK)
+        quantise_q(3)
+        values[3] = dequantise(3)
 
-        def finish_pool(m, sums, t0, width):
-            result = sb.tile([P, width], F32, name="result%d_%d" % (m, t0), align_bytes=64)
-            nc.gpsimd.tensor_tensor(out=result[:], in0=sums[:], in1=d_cols(m, t0, width), op=ALU.mult)
-            return result
-
-        cast_vector(0, 0, VECTOR_SHARE)
-        cast_scalar(0, VECTOR_SHARE, CHUNK)
-        quant_q(0)
-        values0 = [dequantize(0, j, j) for j in range(PACK)]
-        cast_vector(1, 0, VECTOR_SHARE)
-        cast_scalar(1, VECTOR_SHARE, CHUNK)
-        quant_q(1)
-        values1 = [dequantize(1, j, 4 + j) for j in range(PACK)]
-        cast_pool(2, 0, PC2)
-        cast_scalar(2, PC2, CHUNK)
+        regroup(nc.vector.tensor_copy, 1, 0, CHUNK)
         for j in range(PACK):
-            subtract(0, j, values0[j], CHUNK)
-        quant_q(2)
-        values2 = [dequantize(2, j, j) for j in range(PACK)]
-        regroup(0, 0, R0)
-        cast_pool(3, 0, PC3)
-        cast_scalar(3, PC3, CHUNK)
-        for j in range(PACK):
-            subtract(1, j, values1[j], CHUNK)
-        regroup(0, R0, CHUNK)
-        quant_q(3)
-        values3 = [dequantize(3, j, 4 + j) for j in range(PACK)]
-        regroup_vector(1, 0, CHUNK)
-        for j in range(PACK):
-            copy_values(j, values2[j], CHUNK, X)
-        quant_r(0)
-        quant_r(1)
-        for j in range(PACK):
-            subtract(2, j, values2[j], CHUNK, X, CHUNK)
-        regroup(2, X, CHUNK)
-        acc0 = []
+            nc.scalar.copy(out=q2_rows[:, j, :], in_=values[2][j][:, CHUNK : CHUNK + SUBTRACT_POOL])
+        quantise_r(0)
+        quantise_r(1)
+
+        subtract(2, range(PACK), SUBTRACT_POOL, CHUNK)
+        regroup(nc.scalar.copy, 2, SUBTRACT_POOL, CHUNK)
+        last = n_tiles - 1
+        first_half = []
         for m in range(n_tiles):
-            acc0.append(first_tier(1, m, m))
-            second_tier(0, m, acc0[m], 0, True, HALF)
-        subtract_pool(2, 0, X)
-        for j in range(NW):
-            subtract(3, j, values3[j], CHUNK)
-        for lo in (0, 128):
-            for j in range(NW, PACK):
-                subtract(3, j, values3[j], CHUNK, lo, lo + 128)
-            regroup(3, lo, lo + 128)
-        acc1 = [first_tier(3, m, 4 + m) for m in range(NB)]
-        finish(0, acc0[0], 0, 0, HALF)
-        finish(1, acc0[1], 0, 0, HALF)
-        finish(2, acc0[2], 0, 0, HALF)
-        quant_r(3)
-        quant_r(2)
+            first_half.append(first_tier(m, 1, m))
+            second_tier(m, first_half[m], 0, WINDOW, True)
+        nc.gpsimd.tensor_tensor(
+            out=grouped(r_grouped[2], 0, SUBTRACT_POOL),
+            in0=rows(g_rows[2], 0, SUBTRACT_POOL),
+            in1=rows(q2_rows, 0, SUBTRACT_POOL),
+            op=ALU.subtract,
+        )
+        subtract(3, range(PACK - 1), 0, CHUNK)
+        for lo in range(0, CHUNK, CHUNK // 2):
+            subtract(3, [PACK - 1], lo, lo + CHUNK // 2)
+            regroup(nc.scalar.copy, 3, lo, lo + CHUNK // 2)
+        second_half = [first_tier(m, 3, PACK + m) for m in range(last)]
+        for m in range(last):
+            finish(m, 0, first_half[m], nc.sync)
+
+        quantise_r(3)
+        quantise_r(2)
         for m in range(n_tiles):
-            if m >= NB:
-                acc1.append(first_tier(3, m, 4 + m))
-            second_tier(3, m, acc1[m], CHUNK, False)
-            second_tier(2, m, acc1[m], 0, True)
-        finish(3, acc0[3], 0, 0, HALF, nc.scalar)
-        finish(0, acc1[0], 0, HALF, HALF)
-        finish(1, acc1[1], 0, HALF, HALF, nc.scalar)
-        finish(2, acc1[2], 0, HALF, HALF)
-        finish(3, acc1[3], 0, HALF, CHUNK, nc.scalar)
-        finish(3, acc1[3], CHUNK, HALF + CHUNK, CHUNK)
+            if m == last:
+                second_half.append(first_tier(m, 3, PACK + m))
+            second_tier(m, second_half[m], 3 * CHUNK, CHUNK, False)
+            second_tier(m, second_half[m], 2 * CHUNK, CHUNK, True)
+        finish(last, 0, first_half[last], nc.scalar)
+        for m in range(n_tiles):
+            finish(m, 1, second_half[m], nc.scalar if m % 2 else nc.sync)

@@ -26,7 +26,6 @@ CAST_VECTOR = 160
 CAST_POOL_2 = 128
 CAST_POOL_3 = 144
 REGROUP_EARLY = 64
-SUBTRACT_POOL = 224
 
 
 def tile_mix_tierg_mul_kernel(tc, g, w8_words, w8_scales, d, out):
@@ -41,10 +40,10 @@ def tile_mix_tierg_mul_kernel(tc, g, w8_words, w8_scales, d, out):
 
         g_rows = [sb.tile([P, PACK, CHUNK], F32, name="g_rows%d" % c, align_bytes=64) for c in range(n_chunks)]
         g_grouped = [sb.tile([P, CHUNK, PACK], BF16, name="g_grouped%d" % c, align_bytes=64) for c in range(n_chunks)]
-        r_rows = {c: sb.tile([P, PACK, CHUNK], BF16, name="r_rows%d" % c, align_bytes=64) for c in range(n_chunks)}
+        r_rows = {c: sb.tile([P, PACK, CHUNK], BF16, name="r_rows%d" % c, align_bytes=64) for c in (0, 1, 3)}
         r_grouped = {c: sb.tile([P, CHUNK, PACK], BF16, name="r_grouped%d" % c, align_bytes=64) for c in (0, 1, 3)}
         r_grouped[2] = r_grouped[0]
-        q2_rows = sb.tile([P, PACK, SUBTRACT_POOL], F32, name="q2_rows", align_bytes=64)
+        q2_rows = sb.tile([P, PACK, CHUNK], F32, name="q2_rows", align_bytes=64)
 
         words = sb.tile([P, K + T], U32, name="words", align_bytes=64)
         plane = sb.tile([P, K + T], U8, name="plane", align_bytes=64)
@@ -201,21 +200,19 @@ def tile_mix_tierg_mul_kernel(tc, g, w8_words, w8_scales, d, out):
 
         regroup(nc.vector.tensor_copy, 1, 0, CHUNK)
         for j in range(PACK):
-            nc.scalar.copy(out=q2_rows[:, j, :], in_=values[2][j][:, CHUNK : CHUNK + SUBTRACT_POOL])
+            nc.scalar.copy(out=q2_rows[:, j, :], in_=values[2][j][:, CHUNK:WINDOW])
         quantise_r(0)
         quantise_r(1)
 
-        subtract(2, range(PACK), SUBTRACT_POOL, CHUNK)
-        regroup(nc.scalar.copy, 2, SUBTRACT_POOL, CHUNK)
         last = n_tiles - 1
         first_half = []
         for m in range(n_tiles):
             first_half.append(first_tier(m, 1, m))
             second_tier(m, first_half[m], 0, WINDOW, True)
         nc.gpsimd.tensor_tensor(
-            out=grouped(r_grouped[2], 0, SUBTRACT_POOL),
-            in0=rows(g_rows[2], 0, SUBTRACT_POOL),
-            in1=rows(q2_rows, 0, SUBTRACT_POOL),
+            out=grouped(r_grouped[2], 0, CHUNK),
+            in0=rows(g_rows[2], 0, CHUNK),
+            in1=rows(q2_rows, 0, CHUNK),
             op=ALU.subtract,
         )
         subtract(3, range(PACK - 1), 0, CHUNK)

@@ -43,7 +43,7 @@ def tile_mix_tierg_mul_kernel(tc, g, w8_words, w8_scales, d, out):
         r_rows = {c: sb.tile([P, PACK, CHUNK], BF16, name="r_rows%d" % c, align_bytes=64) for c in (0, 1, 3)}
         r_grouped = {c: sb.tile([P, CHUNK, PACK], BF16, name="r_grouped%d" % c, align_bytes=64) for c in (0, 1, 3)}
         r_grouped[2] = r_grouped[0]
-        q2_rows = sb.tile([P, PACK, CHUNK], F32, name="q2_rows", align_bytes=64)
+        q2_walk = sb.tile([P, CHUNK // RUN, PACK, RUN], F32, name="q2_walk", align_bytes=64)
 
         words = sb.tile([P, K + T], U32, name="words", align_bytes=64)
         plane = sb.tile([P, K + T], U8, name="plane", align_bytes=64)
@@ -200,7 +200,7 @@ def tile_mix_tierg_mul_kernel(tc, g, w8_words, w8_scales, d, out):
 
         regroup(nc.vector.tensor_copy, 1, 0, CHUNK)
         for j in range(PACK):
-            nc.scalar.copy(out=q2_rows[:, j, :], in_=values[2][j][:, CHUNK:WINDOW])
+            nc.scalar.copy(out=q2_walk[:, :, j, :], in_=values[2][j][:, CHUNK:WINDOW].rearrange("p (c i) -> p c i", i=RUN))
         quantise_r(0)
         quantise_r(1)
 
@@ -212,7 +212,7 @@ def tile_mix_tierg_mul_kernel(tc, g, w8_words, w8_scales, d, out):
         nc.gpsimd.tensor_tensor(
             out=grouped(r_grouped[2], 0, CHUNK),
             in0=rows(g_rows[2], 0, CHUNK),
-            in1=rows(q2_rows, 0, CHUNK),
+            in1=q2_walk[:],
             op=ALU.subtract,
         )
         subtract(3, range(PACK - 1), 0, CHUNK)

@@ -17,20 +17,23 @@ ALU = mybir.AluOpType
 P = 128
 PACK = 4
 CHUNK = 256
-WINDOW = 512
-RUN = 4
+UNIT = 128
+BANK = 512
+RUN = 2
 RAMP = 256
-WARMUPS = 3
-
-CAST_VECTOR = 160
-CAST_POOL_2 = 128
-CAST_POOL_3 = 144
-REGROUP_EARLY = 64
+CAST_VECTOR = 88
+CAST_VECTOR_1 = 168
+SLOT = PACK * UNIT
+G_SLOT = [0, 1, 2, 3, 4, 5, 6, 7]
+R_SLOT = [8, 9, 10, 11, 12, 13, 14, 15]
+VALUE_BANK = [4, 5, 6, 7, 4, 5, 6, 7]
+SUM_BANK = [[0, 1, 2, 3], [4, 5, 6, 7]]
 
 
 def tile_mix_tierg_mul_kernel(tc, g, w8_words, w8_scales, d, out):
     nc = tc.nc
     n_chunks = T // CHUNK
+    n_units = T // UNIT
     n_tiles = N // P
 
     with ExitStack() as ctx:
@@ -39,15 +42,11 @@ def tile_mix_tierg_mul_kernel(tc, g, w8_words, w8_scales, d, out):
         ctx.enter_context(tc.manual_schedule())
 
         g_rows = [sb.tile([P, PACK, CHUNK], F32, name="g_rows%d" % c, align_bytes=64) for c in range(n_chunks)]
-        g_grouped = [sb.tile([P, CHUNK, PACK], BF16, name="g_grouped%d" % c, align_bytes=64) for c in range(n_chunks)]
-        r_rows = {c: sb.tile([P, PACK, CHUNK], BF16, name="r_rows%d" % c, align_bytes=64) for c in (0, 1, 3)}
-        r_grouped = {c: sb.tile([P, CHUNK, PACK], BF16, name="r_grouped%d" % c, align_bytes=64) for c in (0, 1, 3)}
-        r_grouped[2] = r_grouped[0]
-        q2_walk = sb.tile([P, CHUNK // RUN, PACK, RUN], F32, name="q2_walk", align_bytes=64)
-
-        words = sb.tile([P, K + T], U32, name="words", align_bytes=64)
-        plane = sb.tile([P, K + T], U8, name="plane", align_bytes=64)
-        eye_words, eye_plane = words[:, 0:K], plane[:, 0:K]
+        slots = sb.tile([P, 16 * SLOT], BF16, name="slots", align_bytes=64)
+        eye_words = sb.tile([P, K], U32, name="eye_words", align_bytes=64)
+        eye_plane = sb.tile([P, K], U8, name="eye_plane", align_bytes=64)
+        q_words = sb.tile([P, T], U32, name="q_words", align_bytes=64)
+        q_plane = sb.tile([P, T], U8, name="q_plane", align_bytes=64)
         r_words = sb.tile([P, T], U32, name="r_words", align_bytes=64)
         r_plane = sb.tile([P, T], U8, name="r_plane", align_bytes=64)
         w_words = sb.tile([P, N], I32, name="w_words", align_bytes=64)
@@ -57,12 +56,17 @@ def tile_mix_tierg_mul_kernel(tc, g, w8_words, w8_scales, d, out):
         eye_grouped = sb.tile([P, PACK * K], BF16, name="eye_grouped", align_bytes=64)
 
         def bank(b):
-            return psum.tile([P, WINDOW], F32, name="bank%d" % b, tag="bank%d" % b)
+            return psum.tile([P, BANK], F32, name="bank%d" % b, tag="bank%d" % b)
 
         g_view = g.rearrange("(p j) t -> p j t", j=PACK)
-        for c in range(n_chunks):
+
+        def load_g(c):
             nc.sync.dma_start(out=g_rows[c][:], in_=g_view[:, :, c * CHUNK : (c + 1) * CHUNK])
 
+        load_g(0)
+        load_g(1)
+
+        nc.vector.memset(w_plane[:].bitcast(I32), 0)
         nc.gpsimd.iota(ramp[:], pattern=[[1, RAMP]], base=RAMP // 2, channel_multiplier=-PACK, allow_small_or_imprecise_dtypes=True)
         for j in range(PACK):
             for x in range(0, K, RAMP):
@@ -80,156 +84,129 @@ def tile_mix_tierg_mul_kernel(tc, g, w8_words, w8_scales, d, out):
                 in_=eye_grouped[:, PACK * first : PACK * (first + CHUNK)],
             )
 
-        nc.vector.memset(w_plane[:].bitcast(I32), 0)
         for q in range(4):
             nc.sync.dma_start(
                 out=w_plane[32 * q : 32 * q + 4, :].bitcast(I32),
                 in_=w8_scales[0, 4 * q : 4 * q + 4, :].bitcast(I32),
             )
         nc.sync.dma_start(out=w_words[:], in_=w8_words[0].rearrange("p n i -> p (n i)").bitcast(I32))
+        load_g(2)
+        load_g(3)
         for m in range(n_tiles):
             nc.sync.dma_start(out=d_sb[m][:], in_=d[m * P : (m + 1) * P, :])
 
-        warm_bank = bank(0)
-        for i in range(WARMUPS):
-            nc.tensor.matmul_mx(
-                out=warm_bank[:],
-                lhsT=eye_words[:, 0:P].bitcast(E4M3),
-                lhsT_scale=eye_plane[:, 0:P],
-                rhs=eye_words.bitcast(E4M3),
-                rhs_scale=eye_plane,
-                start=True,
-                stop=True,
-            )
+        def grouped(slot, lo, hi, run):
+            return slots[:, slot * SLOT + PACK * lo : slot * SLOT + PACK * hi].rearrange("p (c i j) -> p c j i", i=run, j=PACK)
 
-        def grouped(tile, lo, hi):
-            return tile[:, lo:hi, :].rearrange("p (c i) j -> p c j i", i=RUN)
+        def g_cols(u, lo, hi):
+            first = (u * UNIT) % CHUNK
+            return g_rows[u * UNIT // CHUNK][:, :, first + lo : first + hi]
 
-        def rows(tile, lo, hi):
-            return tile[:, :, lo:hi].rearrange("p j (c i) -> p c j i", i=RUN)
+        def g_walk(u, lo, hi, run):
+            return g_cols(u, lo, hi).rearrange("p j (c i) -> p c j i", i=run)
 
-        def cast(copy, c, lo, hi):
-            copy(out=grouped(g_grouped[c], lo, hi), in_=rows(g_rows[c], lo, hi))
+        def cast(copy, u, lo, hi):
+            copy(out=grouped(G_SLOT[u], lo, hi, RUN), in_=g_walk(u, lo, hi, RUN))
 
-        def cast_pool(c, hi):
-            nc.gpsimd.tensor_scalar(
-                out=g_grouped[c][:, 0:hi, :],
-                in0=g_rows[c][:, :, 0:hi].rearrange("p j t -> p t j"),
-                scalar1=1.0,
-                scalar2=0.0,
-                op0=ALU.mult,
-                op1=ALU.add,
-            )
-
-        def quantise_q(c):
-            cols = slice(K + c * CHUNK, K + (c + 1) * CHUNK)
+        def quantise(words, plane, fmt, slot, u, count):
+            cols = slice(u * UNIT, (u + count) * UNIT)
             nc.vector.quantize_mx(
-                out=words[:, cols].bitcast(E5M2), scales=plane[:, cols], in_=g_grouped[c][:].rearrange("p t j -> p (t j)")
+                out=words[:, cols].bitcast(fmt), scales=plane[:, cols], in_=slots[:, slot * SLOT : (slot + count) * SLOT]
             )
 
-        def quantise_r(c):
-            cols = slice(c * CHUNK, (c + 1) * CHUNK)
-            nc.vector.quantize_mx(
-                out=r_words[:, cols].bitcast(E4M3), scales=r_plane[:, cols], in_=r_grouped[c][:].rearrange("p t j -> p (t j)")
-            )
+        def quantise_q(u, count):
+            quantise(q_words, q_plane, E5M2, G_SLOT[u], u, count)
+            for v in range(u, u + count):
+                values[v] = dequantise(v)
 
-        def q_pass(stationary, stationary_plane, i, c, b, stop):
-            cols = slice(K + (c + 1) * CHUNK - WINDOW, K + (c + 1) * CHUNK)
-            acc = bank(b)
-            nc.tensor.matmul_mx(
-                out=acc[:],
-                lhsT=stationary[:, i * P : (i + 1) * P].bitcast(E4M3),
-                lhsT_scale=stationary_plane[:, i * P : (i + 1) * P],
-                rhs=words[:, cols].bitcast(E5M2),
-                rhs_scale=plane[:, cols],
-                start=True,
-                stop=stop,
-            )
+        def quantise_r(u, count):
+            quantise(r_words, r_plane, E4M3, R_SLOT[u], u, count)
+
+        def dequantise(u):
+            cols = slice(u * UNIT, (u + 1) * UNIT)
+            acc = bank(VALUE_BANK[u])
+            for j in range(PACK):
+                nc.tensor.matmul_mx(
+                    out=acc[:, j * UNIT : (j + 1) * UNIT],
+                    lhsT=eye_words[:, j * P : (j + 1) * P].bitcast(E4M3),
+                    lhsT_scale=eye_plane[:, j * P : (j + 1) * P],
+                    rhs=q_words[:, cols].bitcast(E5M2),
+                    rhs_scale=q_plane[:, cols],
+                    start=True,
+                    stop=True,
+                )
             return acc
 
-        def dequantise(c):
-            return [q_pass(eye_words, eye_plane, j, c, PACK * (c % 2) + j, True) for j in range(PACK)]
+        def subtract(u):
+            nc.vector.tensor_tensor(
+                out=grouped(R_SLOT[u], 0, UNIT, RUN),
+                in0=g_walk(u, 0, UNIT, RUN),
+                in1=values[u][:].rearrange("p (j c i) -> p c j i", j=PACK, i=RUN),
+                op=ALU.subtract,
+            )
 
-        def first_tier(m, c, b):
-            return q_pass(w_words, w_plane, m, c, b, False)
-
-        def second_tier(m, acc, t0, width, stop):
+        def product(acc, m, words, plane, fmt, t0, width, start, stop):
             nc.tensor.matmul_mx(
-                out=acc[:, t0 % WINDOW : t0 % WINDOW + width],
+                out=acc[:, t0 % BANK : t0 % BANK + width],
                 lhsT=w_words[:, m * P : (m + 1) * P].bitcast(E4M3),
                 lhsT_scale=w_plane[:, m * P : (m + 1) * P],
-                rhs=r_words[:, t0 : t0 + width].bitcast(E4M3),
-                rhs_scale=r_plane[:, t0 : t0 + width],
-                start=False,
+                rhs=words[:, t0 : t0 + width].bitcast(fmt),
+                rhs_scale=plane[:, t0 : t0 + width],
+                start=start,
                 stop=stop,
             )
 
-        def subtract(c, js, lo, hi):
-            for j in js:
-                nc.vector.tensor_tensor(
-                    out=r_rows[c][:, j, lo:hi], in0=g_rows[c][:, j, lo:hi], in1=values[c][j][:, CHUNK + lo : CHUNK + hi], op=ALU.subtract
-                )
+        def first_tier(m, h):
+            sums[m, h] = bank(SUM_BANK[h][m])
+            product(sums[m, h], m, q_words, q_plane, E5M2, h * BANK, BANK, True, False)
 
-        def regroup(copy, c, lo, hi):
-            copy(out=grouped(r_grouped[c], lo, hi), in_=rows(r_rows[c], lo, hi))
+        def second_tier(m, c):
+            product(sums[m, c // 2], m, r_words, r_plane, E4M3, c * CHUNK, CHUNK, False, c % 2 == 1)
 
-        def finish(m, h, acc, queue):
-            cols = slice(h * WINDOW, (h + 1) * WINDOW)
-            result = sb.tile([P, WINDOW], F32, name="result%d_%d" % (m, h), align_bytes=64)
-            nc.vector.tensor_tensor(out=result[:], in0=d_sb[m][:, cols], in1=acc[:], op=ALU.mult)
+        def finish(m, h, queue):
+            cols = slice(h * BANK, (h + 1) * BANK)
+            result = sb.tile([P, BANK], F32, name="result%d_%d" % (m, h), align_bytes=64)
+            nc.vector.tensor_tensor(out=result[:], in0=d_sb[m][:, cols], in1=sums[m, h][:], op=ALU.mult)
             queue.dma_start(out=out[m * P : (m + 1) * P, cols], in_=result[:])
 
         values = {}
-        for c in range(2):
-            cast(nc.vector.tensor_copy, c, 0, CAST_VECTOR)
-            cast(nc.scalar.copy, c, CAST_VECTOR, CHUNK)
-            quantise_q(c)
-            values[c] = dequantise(c)
-        cast_pool(2, CAST_POOL_2)
-        cast(nc.scalar.copy, 2, CAST_POOL_2, CHUNK)
-        subtract(0, range(PACK), 0, CHUNK)
-        quantise_q(2)
-        values[2] = dequantise(2)
-        regroup(nc.scalar.copy, 0, 0, REGROUP_EARLY)
-        cast_pool(3, CAST_POOL_3)
-        cast(nc.scalar.copy, 3, CAST_POOL_3, CHUNK)
-        subtract(1, range(PACK), 0, CHUNK)
-        regroup(nc.scalar.copy, 0, REGROUP_EARLY, CHUNK)
-        quantise_q(3)
-        values[3] = dequantise(3)
-
-        regroup(nc.vector.tensor_copy, 1, 0, CHUNK)
-        for j in range(PACK):
-            nc.scalar.copy(out=q2_walk[:, :, j, :], in_=values[2][j][:, CHUNK:WINDOW].rearrange("p (c i) -> p c i", i=RUN))
-        quantise_r(0)
-        quantise_r(1)
-
-        last = n_tiles - 1
-        first_half = []
+        sums = {}
+        for u in range(2):
+            cast(nc.vector.tensor_copy, u, 0, CAST_VECTOR)
+            cast(nc.scalar.copy, u, CAST_VECTOR, UNIT)
+        for u in range(2):
+            quantise_q(u, 1)
+        cast(nc.vector.tensor_copy, 2, 0, CAST_VECTOR_1)
+        cast(nc.scalar.copy, 2, CAST_VECTOR_1, CHUNK)
+        quantise_q(2, 2)
         for m in range(n_tiles):
-            first_half.append(first_tier(m, 1, m))
-            second_tier(m, first_half[m], 0, WINDOW, True)
-        nc.gpsimd.tensor_tensor(
-            out=grouped(r_grouped[2], 0, CHUNK),
-            in0=rows(g_rows[2], 0, CHUNK),
-            in1=q2_walk[:],
-            op=ALU.subtract,
-        )
-        subtract(3, range(PACK - 1), 0, CHUNK)
-        for lo in range(0, CHUNK, CHUNK // 2):
-            subtract(3, [PACK - 1], lo, lo + CHUNK // 2)
-            regroup(nc.scalar.copy, 3, lo, lo + CHUNK // 2)
-        second_half = [first_tier(m, 3, PACK + m) for m in range(last)]
-        for m in range(last):
-            finish(m, 0, first_half[m], nc.sync)
+            first_tier(m, 0)
 
-        quantise_r(3)
-        quantise_r(2)
+        cast(nc.scalar.copy, 4, 0, CHUNK)
+        cast(nc.scalar.copy, 6, 0, CHUNK)
+        subtract(0)
+        subtract(1)
+        subtract(2)
+        quantise_r(0, 2)
+        quantise_q(4, 2)
         for m in range(n_tiles):
-            if m == last:
-                second_half.append(first_tier(m, 3, PACK + m))
-            second_tier(m, second_half[m], 3 * CHUNK, CHUNK, False)
-            second_tier(m, second_half[m], 2 * CHUNK, CHUNK, True)
-        finish(last, 0, first_half[last], nc.scalar)
+            second_tier(m, 0)
+        subtract(3)
+        subtract(4)
+        quantise_r(2, 2)
+        quantise_q(6, 2)
         for m in range(n_tiles):
-            finish(m, 1, second_half[m], nc.scalar if m % 2 else nc.sync)
+            second_tier(m, 1)
+        subtract(5)
+        subtract(6)
+        quantise_r(4, 2)
+        subtract(7)
+        for m in range(n_tiles):
+            first_tier(m, 1)
+            second_tier(m, 2)
+        finish(0, 0, nc.sync)
+        quantise_r(6, 2)
+        for m in range(n_tiles):
+            second_tier(m, 3)
+        for i in range(1, 2 * n_tiles):
+            finish(i % n_tiles, i // n_tiles, nc.scalar if i % 2 else nc.sync)

@@ -22,12 +22,13 @@ BANK = 512
 RUN = 2
 RAMP = 256
 CAST_VECTOR = 88
-CAST_VECTOR_1 = 168
+POOL_RUN = 4
 SLOT = PACK * UNIT
-G_SLOT = [0, 1, 2, 3, 4, 5, 6, 7]
-R_SLOT = [8, 9, 10, 11, 12, 13, 14, 15]
+G_SLOT = [0, 1, 6, 7, 8, 9, 10, 11]
+R_SLOT = [2, 3, 4, 5, 9, 10, 11, 12]
+WARMUPS = 2
 VALUE_BANK = [4, 5, 6, 7, 4, 5, 6, 7]
-SUM_BANK = [[0, 1, 2, 3], [4, 5, 6, 7]]
+SUM_BANK = [[0, 1, 2, 3], [5, 4, 0, 6]]
 
 
 def tile_mix_tierg_mul_kernel(tc, g, w8_words, w8_scales, d, out):
@@ -42,7 +43,7 @@ def tile_mix_tierg_mul_kernel(tc, g, w8_words, w8_scales, d, out):
         ctx.enter_context(tc.manual_schedule())
 
         g_rows = [sb.tile([P, PACK, CHUNK], F32, name="g_rows%d" % c, align_bytes=64) for c in range(n_chunks)]
-        slots = sb.tile([P, 16 * SLOT], BF16, name="slots", align_bytes=64)
+        slots = sb.tile([P, 13 * SLOT], BF16, name="slots", align_bytes=64)
         eye_words = sb.tile([P, K], U32, name="eye_words", align_bytes=64)
         eye_plane = sb.tile([P, K], U8, name="eye_plane", align_bytes=64)
         q_words = sb.tile([P, T], U32, name="q_words", align_bytes=64)
@@ -63,8 +64,8 @@ def tile_mix_tierg_mul_kernel(tc, g, w8_words, w8_scales, d, out):
         def load_g(c):
             nc.sync.dma_start(out=g_rows[c][:], in_=g_view[:, :, c * CHUNK : (c + 1) * CHUNK])
 
-        load_g(0)
-        load_g(1)
+        for c in range(n_chunks):
+            load_g(c)
 
         nc.vector.memset(w_plane[:].bitcast(I32), 0)
         nc.gpsimd.iota(ramp[:], pattern=[[1, RAMP]], base=RAMP // 2, channel_multiplier=-PACK, allow_small_or_imprecise_dtypes=True)
@@ -90,10 +91,20 @@ def tile_mix_tierg_mul_kernel(tc, g, w8_words, w8_scales, d, out):
                 in_=w8_scales[0, 4 * q : 4 * q + 4, :].bitcast(I32),
             )
         nc.sync.dma_start(out=w_words[:], in_=w8_words[0].rearrange("p n i -> p (n i)").bitcast(I32))
-        load_g(2)
-        load_g(3)
         for m in range(n_tiles):
             nc.sync.dma_start(out=d_sb[m][:], in_=d[m * P : (m + 1) * P, :])
+
+        warm_bank = bank(0)
+        for i in range(WARMUPS):
+            nc.tensor.matmul_mx(
+                out=warm_bank[:],
+                lhsT=eye_words[:, 0:P].bitcast(E4M3),
+                lhsT_scale=eye_plane[:, 0:P],
+                rhs=eye_words[:].bitcast(E4M3),
+                rhs_scale=eye_plane[:],
+                start=True,
+                stop=True,
+            )
 
         def grouped(slot, lo, hi, run):
             return slots[:, slot * SLOT + PACK * lo : slot * SLOT + PACK * hi].rearrange("p (c i j) -> p c j i", i=run, j=PACK)
@@ -116,8 +127,6 @@ def tile_mix_tierg_mul_kernel(tc, g, w8_words, w8_scales, d, out):
 
         def quantise_q(u, count):
             quantise(q_words, q_plane, E5M2, G_SLOT[u], u, count)
-            for v in range(u, u + count):
-                values[v] = dequantise(v)
 
         def quantise_r(u, count):
             quantise(r_words, r_plane, E4M3, R_SLOT[u], u, count)
@@ -135,13 +144,28 @@ def tile_mix_tierg_mul_kernel(tc, g, w8_words, w8_scales, d, out):
                     start=True,
                     stop=True,
                 )
-            return acc
+            values[u] = acc
 
         def subtract(u):
             nc.vector.tensor_tensor(
                 out=grouped(R_SLOT[u], 0, UNIT, RUN),
                 in0=g_walk(u, 0, UNIT, RUN),
                 in1=values[u][:].rearrange("p (j c i) -> p c j i", j=PACK, i=RUN),
+                op=ALU.subtract,
+            )
+
+        def stage_values(u):
+            staged[u] = sb.tile([P, BANK], F32, name="staged%d" % u, align_bytes=64)
+            nc.scalar.copy(
+                out=staged[u][:].rearrange("p (c j i) -> p c j i", j=PACK, i=POOL_RUN),
+                in_=values[u][:].rearrange("p (j c i) -> p c j i", j=PACK, i=POOL_RUN),
+            )
+
+        def subtract_pool(u):
+            nc.gpsimd.tensor_tensor(
+                out=grouped(R_SLOT[u], 0, UNIT, POOL_RUN),
+                in0=g_walk(u, 0, UNIT, POOL_RUN),
+                in1=staged[u][:].rearrange("p (c j i) -> p c j i", j=PACK, i=POOL_RUN),
                 op=ALU.subtract,
             )
 
@@ -160,8 +184,17 @@ def tile_mix_tierg_mul_kernel(tc, g, w8_words, w8_scales, d, out):
             sums[m, h] = bank(SUM_BANK[h][m])
             product(sums[m, h], m, q_words, q_plane, E5M2, h * BANK, BANK, True, False)
 
-        def second_tier(m, c):
-            product(sums[m, c // 2], m, r_words, r_plane, E4M3, c * CHUNK, CHUNK, False, c % 2 == 1)
+        def second_tier(m, h):
+            product(sums[m, h], m, r_words, r_plane, E4M3, h * BANK, BANK, False, True)
+
+        def stage_sums(m, h):
+            staged[m, h] = sb.tile([P, BANK], F32, name="staged%d_%d" % (m, h), align_bytes=64)
+            nc.scalar.copy(out=staged[m, h][:], in_=sums[m, h][:])
+
+        def finish_pool(m, h, result, queue):
+            cols = slice(h * BANK, (h + 1) * BANK)
+            nc.gpsimd.tensor_tensor(out=result, in0=d_sb[m][:, cols], in1=staged[m, h][:], op=ALU.mult)
+            queue.dma_start(out=out[m * P : (m + 1) * P, cols], in_=result)
 
         def finish(m, h, queue):
             cols = slice(h * BANK, (h + 1) * BANK)
@@ -169,44 +202,64 @@ def tile_mix_tierg_mul_kernel(tc, g, w8_words, w8_scales, d, out):
             nc.vector.tensor_tensor(out=result[:], in0=d_sb[m][:, cols], in1=sums[m, h][:], op=ALU.mult)
             queue.dma_start(out=out[m * P : (m + 1) * P, cols], in_=result[:])
 
+        def fresh(m, h):
+            result = sb.tile([P, BANK], F32, name="result%d_%d" % (m, h), align_bytes=64)
+            return result[:]
+
+        def reused(slot):
+            return slots[:, slot * SLOT : (slot + 2) * SLOT].bitcast(F32)
+
         values = {}
         sums = {}
+        staged = {}
         for u in range(2):
             cast(nc.vector.tensor_copy, u, 0, CAST_VECTOR)
             cast(nc.scalar.copy, u, CAST_VECTOR, UNIT)
         for u in range(2):
             quantise_q(u, 1)
-        cast(nc.vector.tensor_copy, 2, 0, CAST_VECTOR_1)
-        cast(nc.scalar.copy, 2, CAST_VECTOR_1, CHUNK)
-        quantise_q(2, 2)
-        for m in range(n_tiles):
-            first_tier(m, 0)
-
+            dequantise(u)
+        for u in (2, 3):
+            cast(nc.scalar.copy, u, 0, UNIT)
+            subtract(u - 2)
+            quantise_q(u, 1)
+            dequantise(u)
         cast(nc.scalar.copy, 4, 0, CHUNK)
         cast(nc.scalar.copy, 6, 0, CHUNK)
-        subtract(0)
-        subtract(1)
         subtract(2)
-        quantise_r(0, 2)
         quantise_q(4, 2)
-        for m in range(n_tiles):
-            second_tier(m, 0)
+        dequantise(4)
+        dequantise(5)
+        stage_values(5)
+        first_tier(0, 0)
+        first_tier(1, 0)
         subtract(3)
-        subtract(4)
-        quantise_r(2, 2)
         quantise_q(6, 2)
-        for m in range(n_tiles):
-            second_tier(m, 1)
-        subtract(5)
-        subtract(6)
-        quantise_r(4, 2)
-        subtract(7)
+        dequantise(6)
+        dequantise(7)
+        quantise_r(0, 4)
+        second_tier(0, 0)
+        second_tier(1, 0)
+        for m in (2, 3):
+            first_tier(m, 0)
+            second_tier(m, 0)
+
+        subtract_pool(5)
+        stage_sums(0, 0)
+        stage_sums(2, 0)
+        finish_pool(0, 0, fresh(0, 0), nc.scalar)
+        for u in (4, 6, 7):
+            subtract(u)
         for m in range(n_tiles):
             first_tier(m, 1)
-            second_tier(m, 2)
-        finish(0, 0, nc.sync)
-        quantise_r(6, 2)
-        for m in range(n_tiles):
-            second_tier(m, 3)
-        for i in range(1, 2 * n_tiles):
-            finish(i % n_tiles, i // n_tiles, nc.scalar if i % 2 else nc.sync)
+        finish(1, 0, nc.sync)
+        quantise_r(4, 4)
+        for m in (0, 3, 1, 2):
+            second_tier(m, 1)
+        stage_sums(3, 1)
+
+        finish(3, 0, nc.sync)
+        finish_pool(2, 0, reused(R_SLOT[4]), nc.scalar)
+        finish(0, 1, nc.sync)
+        finish(1, 1, nc.sync)
+        finish_pool(3, 1, fresh(3, 1), nc.scalar)
+        finish(2, 1, nc.sync)

@@ -19,7 +19,7 @@ PACK = 4
 CHUNK = 256
 UNIT = 128
 BANK = 512
-RUN = 2
+RUN = 4
 RAMP = 256
 CAST_VECTOR = 88
 POOL_RUN = 4

@@ -19,16 +19,16 @@ PACK = 4
 CHUNK = 256
 UNIT = 128
 BANK = 512
+SLOT = PACK * UNIT
 RUN = 4
 RAMP = 256
-CAST_VECTOR = 88
-POOL_RUN = 4
-SLOT = PACK * UNIT
-G_SLOT = [0, 1, 6, 7, 8, 9, 10, 11]
-R_SLOT = [2, 3, 4, 5, 9, 10, 11, 12]
 WARMUPS = 2
-VALUE_BANK = [4, 5, 6, 7, 4, 5, 6, 7]
-SUM_BANK = [[0, 1, 2, 3], [5, 4, 0, 6]]
+
+CAST_VECTOR_0 = 88
+CAST_VECTOR_1 = 168
+CAST_VECTOR_2 = 160
+CAST_POOL_3 = 96
+SUBTRACT_VECTOR_4 = 64
 
 
 def tile_mix_tierg_mul_kernel(tc, g, w8_words, w8_scales, d, out):
@@ -43,7 +43,8 @@ def tile_mix_tierg_mul_kernel(tc, g, w8_words, w8_scales, d, out):
         ctx.enter_context(tc.manual_schedule())
 
         g_rows = [sb.tile([P, PACK, CHUNK], F32, name="g_rows%d" % c, align_bytes=64) for c in range(n_chunks)]
-        slots = sb.tile([P, 13 * SLOT], BF16, name="slots", align_bytes=64)
+        slots = sb.tile([P, (2 * n_units - 2) * SLOT], BF16, name="slots", align_bytes=64)
+        r_slot = [u + 10 if u < 4 else u + 2 for u in range(n_units)]
         eye_words = sb.tile([P, K], U32, name="eye_words", align_bytes=64)
         eye_plane = sb.tile([P, K], U8, name="eye_plane", align_bytes=64)
         q_words = sb.tile([P, T], U32, name="q_words", align_bytes=64)
@@ -60,14 +61,11 @@ def tile_mix_tierg_mul_kernel(tc, g, w8_words, w8_scales, d, out):
             return psum.tile([P, BANK], F32, name="bank%d" % b, tag="bank%d" % b)
 
         g_view = g.rearrange("(p j) t -> p j t", j=PACK)
-
-        def load_g(c):
+        for c in range(n_chunks):
             nc.sync.dma_start(out=g_rows[c][:], in_=g_view[:, :, c * CHUNK : (c + 1) * CHUNK])
 
-        for c in range(n_chunks):
-            load_g(c)
-
         nc.vector.memset(w_plane[:].bitcast(I32), 0)
+
         nc.gpsimd.iota(ramp[:], pattern=[[1, RAMP]], base=RAMP // 2, channel_multiplier=-PACK, allow_small_or_imprecise_dtypes=True)
         for j in range(PACK):
             for x in range(0, K, RAMP):
@@ -106,18 +104,29 @@ def tile_mix_tierg_mul_kernel(tc, g, w8_words, w8_scales, d, out):
                 stop=True,
             )
 
-        def grouped(slot, lo, hi, run):
-            return slots[:, slot * SLOT + PACK * lo : slot * SLOT + PACK * hi].rearrange("p (c i j) -> p c j i", i=run, j=PACK)
+        values = {}
+        staged = {}
+        sums = {}
+
+        def grouped(slot, lo, hi):
+            return slots[:, slot * SLOT + PACK * lo : slot * SLOT + PACK * hi].rearrange("p (c i j) -> p c j i", i=RUN, j=PACK)
 
         def g_cols(u, lo, hi):
             first = (u * UNIT) % CHUNK
             return g_rows[u * UNIT // CHUNK][:, :, first + lo : first + hi]
 
-        def g_walk(u, lo, hi, run):
-            return g_cols(u, lo, hi).rearrange("p j (c i) -> p c j i", i=run)
+        def g_walk(u, lo, hi):
+            return g_cols(u, lo, hi).rearrange("p j (c i) -> p c j i", i=RUN)
 
-        def cast(copy, u, lo, hi):
-            copy(out=grouped(G_SLOT[u], lo, hi, RUN), in_=g_walk(u, lo, hi, RUN))
+        def value_walk(u, lo, hi):
+            return values[u][:].rearrange("p (j t) -> p j t", j=PACK)[:, :, lo:hi].rearrange("p j (c i) -> p c j i", i=RUN)
+
+        def staged_walk(u, lo):
+            return staged[u][:, PACK * lo :].rearrange("p (c j i) -> p c j i", j=PACK, i=RUN)
+
+        def cast_shared(u, split, width):
+            nc.vector.tensor_copy(out=grouped(u, 0, split), in_=g_walk(u, 0, split))
+            nc.scalar.copy(out=grouped(u, split, width), in_=g_walk(u, split, width))
 
         def quantise(words, plane, fmt, slot, u, count):
             cols = slice(u * UNIT, (u + count) * UNIT)
@@ -125,18 +134,12 @@ def tile_mix_tierg_mul_kernel(tc, g, w8_words, w8_scales, d, out):
                 out=words[:, cols].bitcast(fmt), scales=plane[:, cols], in_=slots[:, slot * SLOT : (slot + count) * SLOT]
             )
 
-        def quantise_q(u, count):
-            quantise(q_words, q_plane, E5M2, G_SLOT[u], u, count)
-
-        def quantise_r(u, count):
-            quantise(r_words, r_plane, E4M3, R_SLOT[u], u, count)
-
         def dequantise(u):
             cols = slice(u * UNIT, (u + 1) * UNIT)
-            acc = bank(VALUE_BANK[u])
+            values[u] = bank(n_tiles + u % n_tiles)
             for j in range(PACK):
                 nc.tensor.matmul_mx(
-                    out=acc[:, j * UNIT : (j + 1) * UNIT],
+                    out=values[u][:, j * UNIT : (j + 1) * UNIT],
                     lhsT=eye_words[:, j * P : (j + 1) * P].bitcast(E4M3),
                     lhsT_scale=eye_plane[:, j * P : (j + 1) * P],
                     rhs=q_words[:, cols].bitcast(E5M2),
@@ -144,122 +147,101 @@ def tile_mix_tierg_mul_kernel(tc, g, w8_words, w8_scales, d, out):
                     start=True,
                     stop=True,
                 )
-            values[u] = acc
 
-        def subtract(u):
-            nc.vector.tensor_tensor(
-                out=grouped(R_SLOT[u], 0, UNIT, RUN),
-                in0=g_walk(u, 0, UNIT, RUN),
-                in1=values[u][:].rearrange("p (j c i) -> p c j i", j=PACK, i=RUN),
-                op=ALU.subtract,
-            )
+        def quantise_q(u, count):
+            quantise(q_words, q_plane, E5M2, u, u, count)
+            for v in range(u, u + count):
+                dequantise(v)
 
-        def stage_values(u):
+        def quantise_r(h):
+            first = h * n_units // 2
+            quantise(r_words, r_plane, E4M3, r_slot[first], first, n_units // 2)
+
+        def subtract(u, hi):
+            nc.vector.tensor_tensor(out=grouped(r_slot[u], 0, hi), in0=g_walk(u, 0, hi), in1=value_walk(u, 0, hi), op=ALU.subtract)
+
+        def stage(u, lo):
             staged[u] = sb.tile([P, BANK], F32, name="staged%d" % u, align_bytes=64)
-            nc.scalar.copy(
-                out=staged[u][:].rearrange("p (c j i) -> p c j i", j=PACK, i=POOL_RUN),
-                in_=values[u][:].rearrange("p (j c i) -> p c j i", j=PACK, i=POOL_RUN),
-            )
+            nc.scalar.copy(out=staged_walk(u, lo), in_=value_walk(u, lo, UNIT))
 
-        def subtract_pool(u):
+        def subtract_pool(u, lo):
             nc.gpsimd.tensor_tensor(
-                out=grouped(R_SLOT[u], 0, UNIT, POOL_RUN),
-                in0=g_walk(u, 0, UNIT, POOL_RUN),
-                in1=staged[u][:].rearrange("p (c j i) -> p c j i", j=PACK, i=POOL_RUN),
-                op=ALU.subtract,
+                out=grouped(r_slot[u], lo, UNIT), in0=g_walk(u, lo, UNIT), in1=staged_walk(u, lo), op=ALU.subtract
             )
 
-        def product(acc, m, words, plane, fmt, t0, width, start, stop):
+        def product(m, h, words, plane, fmt, first):
+            cols = slice(h * BANK, (h + 1) * BANK)
             nc.tensor.matmul_mx(
-                out=acc[:, t0 % BANK : t0 % BANK + width],
+                out=sums[m, h][:],
                 lhsT=w_words[:, m * P : (m + 1) * P].bitcast(E4M3),
                 lhsT_scale=w_plane[:, m * P : (m + 1) * P],
-                rhs=words[:, t0 : t0 + width].bitcast(fmt),
-                rhs_scale=plane[:, t0 : t0 + width],
-                start=start,
-                stop=stop,
+                rhs=words[:, cols].bitcast(fmt),
+                rhs_scale=plane[:, cols],
+                start=first,
+                stop=not first,
             )
 
-        def first_tier(m, h):
-            sums[m, h] = bank(SUM_BANK[h][m])
-            product(sums[m, h], m, q_words, q_plane, E5M2, h * BANK, BANK, True, False)
+        def first_tier(m, h, b):
+            sums[m, h] = bank(b)
+            product(m, h, q_words, q_plane, E5M2, True)
 
         def second_tier(m, h):
-            product(sums[m, h], m, r_words, r_plane, E4M3, h * BANK, BANK, False, True)
+            product(m, h, r_words, r_plane, E4M3, False)
 
-        def stage_sums(m, h):
-            staged[m, h] = sb.tile([P, BANK], F32, name="staged%d_%d" % (m, h), align_bytes=64)
-            nc.scalar.copy(out=staged[m, h][:], in_=sums[m, h][:])
-
-        def finish_pool(m, h, result, queue):
-            cols = slice(h * BANK, (h + 1) * BANK)
-            nc.gpsimd.tensor_tensor(out=result, in0=d_sb[m][:, cols], in1=staged[m, h][:], op=ALU.mult)
-            queue.dma_start(out=out[m * P : (m + 1) * P, cols], in_=result)
-
-        def finish(m, h, queue):
+        def finish(m, h):
             cols = slice(h * BANK, (h + 1) * BANK)
             result = sb.tile([P, BANK], F32, name="result%d_%d" % (m, h), align_bytes=64)
             nc.vector.tensor_tensor(out=result[:], in0=d_sb[m][:, cols], in1=sums[m, h][:], op=ALU.mult)
+            queue = nc.scalar if m % 2 else nc.sync
             queue.dma_start(out=out[m * P : (m + 1) * P, cols], in_=result[:])
 
-        def fresh(m, h):
-            result = sb.tile([P, BANK], F32, name="result%d_%d" % (m, h), align_bytes=64)
-            return result[:]
-
-        def reused(slot):
-            return slots[:, slot * SLOT : (slot + 2) * SLOT].bitcast(F32)
-
-        values = {}
-        sums = {}
-        staged = {}
         for u in range(2):
-            cast(nc.vector.tensor_copy, u, 0, CAST_VECTOR)
-            cast(nc.scalar.copy, u, CAST_VECTOR, UNIT)
+            cast_shared(u, CAST_VECTOR_0, UNIT)
         for u in range(2):
             quantise_q(u, 1)
-            dequantise(u)
-        for u in (2, 3):
-            cast(nc.scalar.copy, u, 0, UNIT)
-            subtract(u - 2)
-            quantise_q(u, 1)
-            dequantise(u)
-        cast(nc.scalar.copy, 4, 0, CHUNK)
-        cast(nc.scalar.copy, 6, 0, CHUNK)
-        subtract(2)
-        quantise_q(4, 2)
-        dequantise(4)
-        dequantise(5)
-        stage_values(5)
-        first_tier(0, 0)
-        first_tier(1, 0)
-        subtract(3)
+        for c, split in ((1, CAST_VECTOR_1), (2, CAST_VECTOR_2)):
+            cast_shared(2 * c, split, CHUNK)
+            subtract(c - 1, UNIT)
+            quantise_q(2 * c, 2)
+
+        nc.gpsimd.tensor_scalar(
+            out=slots[:, 6 * SLOT : 6 * SLOT + PACK * CAST_POOL_3].rearrange("p (t j) -> p t j", j=PACK),
+            in0=g_cols(6, 0, CAST_POOL_3).rearrange("p j t -> p t j"),
+            scalar1=1.0,
+            scalar2=0.0,
+            op0=ALU.mult,
+            op1=ALU.add,
+        )
+        nc.scalar.copy(out=grouped(6, CAST_POOL_3, CHUNK), in_=g_walk(6, CAST_POOL_3, CHUNK))
+        subtract(2, UNIT)
+        subtract(3, UNIT)
+        stage(4, SUBTRACT_VECTOR_4)
+        stage(5, 0)
+
+        early = n_tiles // 2
+        for m in range(early):
+            first_tier(m, 0, m)
         quantise_q(6, 2)
-        dequantise(6)
-        dequantise(7)
-        quantise_r(0, 4)
-        second_tier(0, 0)
-        second_tier(1, 0)
-        for m in (2, 3):
-            first_tier(m, 0)
+        quantise_r(0)
+        for m in range(n_tiles):
+            if m >= early:
+                first_tier(m, 0, m)
             second_tier(m, 0)
 
-        subtract_pool(5)
-        stage_sums(0, 0)
-        stage_sums(2, 0)
-        finish_pool(0, 0, fresh(0, 0), nc.scalar)
-        for u in (4, 6, 7):
-            subtract(u)
+        subtract_pool(4, SUBTRACT_VECTOR_4)
+        subtract_pool(5, 0)
+        subtract(4, SUBTRACT_VECTOR_4)
+        subtract(6, UNIT)
+        subtract(7, UNIT)
         for m in range(n_tiles):
-            first_tier(m, 1)
-        finish(1, 0, nc.sync)
-        quantise_r(4, 4)
-        for m in (0, 3, 1, 2):
-            second_tier(m, 1)
-        stage_sums(3, 1)
+            first_tier(m, 1, n_tiles + m)
+        for m in range(early):
+            finish(m, 0)
 
-        finish(3, 0, nc.sync)
-        finish_pool(2, 0, reused(R_SLOT[4]), nc.scalar)
-        finish(0, 1, nc.sync)
-        finish(1, 1, nc.sync)
-        finish_pool(3, 1, fresh(3, 1), nc.scalar)
-        finish(2, 1, nc.sync)
+        quantise_r(1)
+        for m in range(n_tiles):
+            second_tier(m, 1)
+        for m in range(early, n_tiles):
+            finish(m, 0)
+        for m in range(n_tiles):
+            finish(m, 1)

@@ -19,8 +19,8 @@ PACK = 4
 CHUNK = 256
 UNIT = 128
 BANK = 512
-SLOT = PACK * UNIT
 RUN = 4
+RUN_WIDE = 2
 RAMP = 256
 WARMUPS = 2
 
@@ -43,8 +43,10 @@ def tile_mix_tierg_mul_kernel(tc, g, w8_words, w8_scales, d, out):
         ctx.enter_context(tc.manual_schedule())
 
         g_rows = [sb.tile([P, PACK, CHUNK], F32, name="g_rows%d" % c, align_bytes=64) for c in range(n_chunks)]
-        slots = sb.tile([P, (2 * n_units - 2) * SLOT], BF16, name="slots", align_bytes=64)
-        r_slot = [u + 10 if u < 4 else u + 2 for u in range(n_units)]
+        late = 6 * UNIT - CAST_POOL_3
+        g_at = [u * UNIT if u < 6 else late + (u - 6) * UNIT for u in range(n_units)]
+        r_at = [T + CHUNK + u * UNIT if u < 4 else late + (u - 4) * UNIT for u in range(n_units)]
+        grouped_all = sb.tile([P, PACK * (r_at[3] + UNIT)], BF16, name="grouped_all", align_bytes=64)
         eye_words = sb.tile([P, K], U32, name="eye_words", align_bytes=64)
         eye_plane = sb.tile([P, K], U8, name="eye_plane", align_bytes=64)
         q_words = sb.tile([P, T], U32, name="q_words", align_bytes=64)
@@ -53,7 +55,9 @@ def tile_mix_tierg_mul_kernel(tc, g, w8_words, w8_scales, d, out):
         r_plane = sb.tile([P, T], U8, name="r_plane", align_bytes=64)
         w_words = sb.tile([P, N], I32, name="w_words", align_bytes=64)
         w_plane = sb.tile([P, N], U8, name="w_plane", align_bytes=64)
-        d_sb = [sb.tile([P, T], F32, name="d_sb%d" % m, align_bytes=64) for m in range(n_tiles)]
+        early = n_tiles // 2
+        d_early = [sb.tile([P, T], F32, name="d_early%d" % m, align_bytes=64) for m in range(early)]
+        d_late = [sb.tile([P, n_tiles - early, BANK], F32, name="d_late%d" % h, align_bytes=64) for h in range(2)]
         ramp = sb.tile([P, RAMP], BF16, name="ramp", align_bytes=64)
         eye_grouped = sb.tile([P, PACK * K], BF16, name="eye_grouped", align_bytes=64)
 
@@ -89,8 +93,11 @@ def tile_mix_tierg_mul_kernel(tc, g, w8_words, w8_scales, d, out):
                 in_=w8_scales[0, 4 * q : 4 * q + 4, :].bitcast(I32),
             )
         nc.sync.dma_start(out=w_words[:], in_=w8_words[0].rearrange("p n i -> p (n i)").bitcast(I32))
-        for m in range(n_tiles):
-            nc.sync.dma_start(out=d_sb[m][:], in_=d[m * P : (m + 1) * P, :])
+        for m in range(early):
+            nc.sync.dma_start(out=d_early[m][:], in_=d[m * P : (m + 1) * P, :])
+        d_view = d[early * P :, :].rearrange("(m p) t -> p m t", p=P)
+        for h in range(2):
+            nc.sync.dma_start(out=d_late[h][:], in_=d_view[:, :, h * BANK : (h + 1) * BANK])
 
         warm_bank = bank(0)
         for i in range(WARMUPS):
@@ -105,34 +112,45 @@ def tile_mix_tierg_mul_kernel(tc, g, w8_words, w8_scales, d, out):
             )
 
         values = {}
+        g_wide = {}
         staged = {}
         sums = {}
 
-        def grouped(slot, lo, hi):
-            return slots[:, slot * SLOT + PACK * lo : slot * SLOT + PACK * hi].rearrange("p (c i j) -> p c j i", i=RUN, j=PACK)
+        def flat(at, lo, hi):
+            return grouped_all[:, PACK * (at + lo) : PACK * (at + hi)]
+
+        def grouped_walk(at, lo, hi):
+            return flat(at, lo, hi).rearrange("p (c i j) -> p c j i", i=RUN, j=PACK)
+
+        def rows_walk(rows, run):
+            return rows.rearrange("p j (c i) -> p c j i", i=run)
 
         def g_cols(u, lo, hi):
             first = (u * UNIT) % CHUNK
             return g_rows[u * UNIT // CHUNK][:, :, first + lo : first + hi]
 
-        def g_walk(u, lo, hi):
-            return g_cols(u, lo, hi).rearrange("p j (c i) -> p c j i", i=RUN)
-
-        def value_walk(u, lo, hi):
-            return values[u][:].rearrange("p (j t) -> p j t", j=PACK)[:, :, lo:hi].rearrange("p j (c i) -> p c j i", i=RUN)
+        def value_rows(u):
+            return values[u][:].rearrange("p (j t) -> p j t", j=PACK)
 
         def staged_walk(u, lo):
             return staged[u][:, PACK * lo :].rearrange("p (c j i) -> p c j i", j=PACK, i=RUN)
 
-        def cast_shared(u, split, width):
-            nc.vector.tensor_copy(out=grouped(u, 0, split), in_=g_walk(u, 0, split))
-            nc.scalar.copy(out=grouped(u, split, width), in_=g_walk(u, split, width))
+        def cast(copy, u, lo, hi):
+            copy(out=grouped_walk(g_at[u], lo, hi), in_=rows_walk(g_cols(u, lo, hi), RUN))
 
-        def quantise(words, plane, fmt, slot, u, count):
-            cols = slice(u * UNIT, (u + count) * UNIT)
-            nc.vector.quantize_mx(
-                out=words[:, cols].bitcast(fmt), scales=plane[:, cols], in_=slots[:, slot * SLOT : (slot + count) * SLOT]
+        def cast_shared(u, split, width):
+            cast(nc.vector.tensor_copy, u, 0, split)
+            cast(nc.scalar.copy, u, split, width)
+
+        def widen(u, hi):
+            g_wide[u] = sb.tile([P, UNIT, PACK], F32, name="g_wide%d" % u, align_bytes=64)
+            nc.scalar.copy(
+                out=g_wide[u][:, 0:hi, :].rearrange("p (c i) j -> p c j i", i=RUN_WIDE), in_=rows_walk(g_cols(u, 0, hi), RUN_WIDE)
             )
+
+        def quantise(words, plane, fmt, at, u, count):
+            cols = slice(u * UNIT, (u + count) * UNIT)
+            nc.vector.quantize_mx(out=words[:, cols].bitcast(fmt), scales=plane[:, cols], in_=flat(at, 0, count * UNIT))
 
         def dequantise(u):
             cols = slice(u * UNIT, (u + 1) * UNIT)
@@ -149,24 +167,37 @@ def tile_mix_tierg_mul_kernel(tc, g, w8_words, w8_scales, d, out):
                 )
 
         def quantise_q(u, count):
-            quantise(q_words, q_plane, E5M2, u, u, count)
+            quantise(q_words, q_plane, E5M2, g_at[u], u, count)
             for v in range(u, u + count):
                 dequantise(v)
 
         def quantise_r(h):
             first = h * n_units // 2
-            quantise(r_words, r_plane, E4M3, r_slot[first], first, n_units // 2)
+            quantise(r_words, r_plane, E4M3, r_at[first], first, n_units // 2)
 
-        def subtract(u, hi):
-            nc.vector.tensor_tensor(out=grouped(r_slot[u], 0, hi), in0=g_walk(u, 0, hi), in1=value_walk(u, 0, hi), op=ALU.subtract)
+        def subtract_wide(u, hi):
+            nc.vector.tensor_tensor(
+                out=flat(r_at[u], 0, hi).rearrange("p (t j) -> p t j", j=PACK),
+                in0=g_wide[u][:, 0:hi, :],
+                in1=value_rows(u)[:, :, 0:hi].rearrange("p j t -> p t j"),
+                op=ALU.subtract,
+            )
+
+        def subtract_rows(u):
+            r_rows = sb.tile([P, PACK, UNIT], BF16, name="r_rows%d" % u, align_bytes=64)
+            nc.vector.tensor_tensor(out=r_rows[:], in0=g_cols(u, 0, UNIT), in1=value_rows(u), op=ALU.subtract)
+            nc.scalar.copy(out=grouped_walk(r_at[u], 0, UNIT), in_=rows_walk(r_rows[:], RUN))
 
         def stage(u, lo):
             staged[u] = sb.tile([P, BANK], F32, name="staged%d" % u, align_bytes=64)
-            nc.scalar.copy(out=staged_walk(u, lo), in_=value_walk(u, lo, UNIT))
+            nc.scalar.copy(out=staged_walk(u, lo), in_=rows_walk(value_rows(u)[:, :, lo:UNIT], RUN))
 
         def subtract_pool(u, lo):
             nc.gpsimd.tensor_tensor(
-                out=grouped(r_slot[u], lo, UNIT), in0=g_walk(u, lo, UNIT), in1=staged_walk(u, lo), op=ALU.subtract
+                out=grouped_walk(r_at[u], lo, UNIT),
+                in0=rows_walk(g_cols(u, lo, UNIT), RUN),
+                in1=staged_walk(u, lo),
+                op=ALU.subtract,
             )
 
         def product(m, h, words, plane, fmt, first):
@@ -191,48 +222,54 @@ def tile_mix_tierg_mul_kernel(tc, g, w8_words, w8_scales, d, out):
         def finish(m, h):
             cols = slice(h * BANK, (h + 1) * BANK)
             result = sb.tile([P, BANK], F32, name="result%d_%d" % (m, h), align_bytes=64)
-            nc.vector.tensor_tensor(out=result[:], in0=d_sb[m][:, cols], in1=sums[m, h][:], op=ALU.mult)
+            factor = d_early[m][:, cols] if m < early else d_late[h][:, m - early, :]
+            nc.vector.tensor_tensor(out=result[:], in0=factor, in1=sums[m, h][:], op=ALU.mult)
             queue = nc.scalar if m % 2 else nc.sync
             queue.dma_start(out=out[m * P : (m + 1) * P, cols], in_=result[:])
 
         for u in range(2):
             cast_shared(u, CAST_VECTOR_0, UNIT)
         for u in range(2):
+            widen(u, UNIT)
             quantise_q(u, 1)
-        for c, split in ((1, CAST_VECTOR_1), (2, CAST_VECTOR_2)):
-            cast_shared(2 * c, split, CHUNK)
-            subtract(c - 1, UNIT)
-            quantise_q(2 * c, 2)
+        cast_shared(2, CAST_VECTOR_1, CHUNK)
+        widen(2, UNIT)
+        subtract_wide(0, UNIT)
+        quantise_q(2, 2)
+        cast_shared(4, CAST_VECTOR_2, CHUNK)
+        widen(3, UNIT)
+        subtract_wide(1, UNIT)
+        quantise_q(4, 2)
 
         nc.gpsimd.tensor_scalar(
-            out=slots[:, 6 * SLOT : 6 * SLOT + PACK * CAST_POOL_3].rearrange("p (t j) -> p t j", j=PACK),
+            out=flat(g_at[6], 0, CAST_POOL_3).rearrange("p (t j) -> p t j", j=PACK),
             in0=g_cols(6, 0, CAST_POOL_3).rearrange("p j t -> p t j"),
             scalar1=1.0,
             scalar2=0.0,
             op0=ALU.mult,
             op1=ALU.add,
         )
-        nc.scalar.copy(out=grouped(6, CAST_POOL_3, CHUNK), in_=g_walk(6, CAST_POOL_3, CHUNK))
-        subtract(2, UNIT)
-        subtract(3, UNIT)
+        cast(nc.scalar.copy, 6, CAST_POOL_3, CHUNK)
+        subtract_wide(2, UNIT)
+        subtract_wide(3, UNIT)
+        widen(4, SUBTRACT_VECTOR_4)
         stage(4, SUBTRACT_VECTOR_4)
         stage(5, 0)
+        widen(7, UNIT)
 
-        early = n_tiles // 2
-        for m in range(early):
-            first_tier(m, 0, m)
+        first_tier(0, 0, 0)
         quantise_q(6, 2)
         quantise_r(0)
         for m in range(n_tiles):
-            if m >= early:
+            if m > 0:
                 first_tier(m, 0, m)
             second_tier(m, 0)
 
         subtract_pool(4, SUBTRACT_VECTOR_4)
         subtract_pool(5, 0)
-        subtract(4, SUBTRACT_VECTOR_4)
-        subtract(6, UNIT)
-        subtract(7, UNIT)
+        subtract_wide(4, SUBTRACT_VECTOR_4)
+        subtract_rows(6)
+        subtract_wide(7, UNIT)
         for m in range(n_tiles):
             first_tier(m, 1, n_tiles + m)
         for m in range(early):

@@ -16,37 +16,31 @@ ALU = mybir.AluOpType
 
 P = 128
 PACK = 4
-CHUNK = 256
 UNIT = 128
 BANK = 512
+PAIR = 2
 RUN = 4
-RUN_WIDE = 2
 RAMP = 256
 WARMUPS = 2
-
-CAST_VECTOR_0 = 88
-CAST_VECTOR_1 = 168
-CAST_VECTOR_2 = 160
-CAST_POOL_3 = 96
-SUBTRACT_VECTOR_4 = 64
+LOADS = (256, 256, 256, 256)
 
 
 def tile_mix_tierg_mul_kernel(tc, g, w8_words, w8_scales, d, out):
     nc = tc.nc
-    n_chunks = T // CHUNK
     n_units = T // UNIT
     n_tiles = N // P
+    starts = [sum(LOADS[:c]) for c in range(len(LOADS))]
 
     with ExitStack() as ctx:
         sb = ctx.enter_context(tc.tile_pool(name="sb", bufs=1))
         psum = ctx.enter_context(tc.psum_pool(name="psum", bufs=1))
         ctx.enter_context(tc.manual_schedule())
 
-        g_rows = [sb.tile([P, PACK, CHUNK], F32, name="g_rows%d" % c, align_bytes=64) for c in range(n_chunks)]
-        late = 6 * UNIT - CAST_POOL_3
+        g_rows = [sb.tile([P, PACK, w], F32, name="g_rows%d" % c, align_bytes=64) for c, w in enumerate(LOADS)]
+        late = 6 * UNIT - 64
         g_at = [u * UNIT if u < 6 else late + (u - 6) * UNIT for u in range(n_units)]
-        r_at = [T + CHUNK + u * UNIT if u < 4 else late + (u - 4) * UNIT for u in range(n_units)]
-        grouped_all = sb.tile([P, PACK * (r_at[3] + UNIT)], BF16, name="grouped_all", align_bytes=64)
+        r_at = [(10 + u) * UNIT for u in range(4)] + [late, 8 * UNIT, 9 * UNIT, late]
+        grouped_all = sb.tile([P, PACK * 14 * UNIT], BF16, name="grouped_all", align_bytes=64)
         eye_words = sb.tile([P, K], U32, name="eye_words", align_bytes=64)
         eye_plane = sb.tile([P, K], U8, name="eye_plane", align_bytes=64)
         q_words = sb.tile([P, T], U32, name="q_words", align_bytes=64)
@@ -55,9 +49,6 @@ def tile_mix_tierg_mul_kernel(tc, g, w8_words, w8_scales, d, out):
         r_plane = sb.tile([P, T], U8, name="r_plane", align_bytes=64)
         w_words = sb.tile([P, N], I32, name="w_words", align_bytes=64)
         w_plane = sb.tile([P, N], U8, name="w_plane", align_bytes=64)
-        early = n_tiles // 2
-        d_early = [sb.tile([P, T], F32, name="d_early%d" % m, align_bytes=64) for m in range(early)]
-        d_late = [sb.tile([P, n_tiles - early, BANK], F32, name="d_late%d" % h, align_bytes=64) for h in range(2)]
         ramp = sb.tile([P, RAMP], BF16, name="ramp", align_bytes=64)
         eye_grouped = sb.tile([P, PACK * K], BF16, name="eye_grouped", align_bytes=64)
 
@@ -65,8 +56,12 @@ def tile_mix_tierg_mul_kernel(tc, g, w8_words, w8_scales, d, out):
             return psum.tile([P, BANK], F32, name="bank%d" % b, tag="bank%d" % b)
 
         g_view = g.rearrange("(p j) t -> p j t", j=PACK)
-        for c in range(n_chunks):
-            nc.sync.dma_start(out=g_rows[c][:], in_=g_view[:, :, c * CHUNK : (c + 1) * CHUNK])
+
+        def load_g(c):
+            nc.sync.dma_start(out=g_rows[c][:], in_=g_view[:, :, starts[c] : starts[c] + LOADS[c]])
+
+        for c in range(len(LOADS)):
+            load_g(c)
 
         nc.vector.memset(w_plane[:].bitcast(I32), 0)
 
@@ -80,11 +75,11 @@ def tile_mix_tierg_mul_kernel(tc, g, w8_words, w8_scales, d, out):
                     scalar2=None,
                     op0=ALU.is_equal,
                 )
-        for first in range(0, K, CHUNK):
+        for first in range(0, K, K // 2):
             nc.vector.quantize_mx(
-                out=eye_words[:, first : first + CHUNK].bitcast(E4M3),
-                scales=eye_plane[:, first : first + CHUNK],
-                in_=eye_grouped[:, PACK * first : PACK * (first + CHUNK)],
+                out=eye_words[:, first : first + K // 2].bitcast(E4M3),
+                scales=eye_plane[:, first : first + K // 2],
+                in_=eye_grouped[:, PACK * first : PACK * (first + K // 2)],
             )
 
         for q in range(4):
@@ -93,11 +88,15 @@ def tile_mix_tierg_mul_kernel(tc, g, w8_words, w8_scales, d, out):
                 in_=w8_scales[0, 4 * q : 4 * q + 4, :].bitcast(I32),
             )
         nc.sync.dma_start(out=w_words[:], in_=w8_words[0].rearrange("p n i -> p (n i)").bitcast(I32))
-        for m in range(early):
-            nc.sync.dma_start(out=d_early[m][:], in_=d[m * P : (m + 1) * P, :])
-        d_view = d[early * P :, :].rearrange("(m p) t -> p m t", p=P)
+        d_view = d.rearrange("(m p) t -> p m t", p=P)
+        d_pair = [sb.tile([P, 2, T], F32, name="d_pair%d" % i, align_bytes=64) for i in range(2)]
+        for m in range(2):
+            nc.sync.dma_start(out=d_pair[0][:, m, :], in_=d_view[:, m, :])
         for h in range(2):
-            nc.sync.dma_start(out=d_late[h][:], in_=d_view[:, :, h * BANK : (h + 1) * BANK])
+            nc.sync.dma_start(out=d_pair[1][:, :, h * BANK : (h + 1) * BANK], in_=d_view[:, 2:4, h * BANK : (h + 1) * BANK])
+
+        def factor(m, h):
+            return d_pair[m // 2][:, m % 2, h * BANK : (h + 1) * BANK]
 
         warm_bank = bank(0)
         for i in range(WARMUPS):
@@ -112,22 +111,22 @@ def tile_mix_tierg_mul_kernel(tc, g, w8_words, w8_scales, d, out):
             )
 
         values = {}
-        g_wide = {}
         staged = {}
         sums = {}
 
         def flat(at, lo, hi):
             return grouped_all[:, PACK * (at + lo) : PACK * (at + hi)]
 
-        def grouped_walk(at, lo, hi):
-            return flat(at, lo, hi).rearrange("p (c i j) -> p c j i", i=RUN, j=PACK)
+        def grouped_walk(at, lo, hi, run):
+            return flat(at, lo, hi).rearrange("p (c i j) -> p c j i", i=run, j=PACK)
 
         def rows_walk(rows, run):
             return rows.rearrange("p j (c i) -> p c j i", i=run)
 
         def g_cols(u, lo, hi):
-            first = (u * UNIT) % CHUNK
-            return g_rows[u * UNIT // CHUNK][:, :, first + lo : first + hi]
+            c = max(x for x in range(len(LOADS)) if starts[x] <= u * UNIT)
+            first = u * UNIT - starts[c]
+            return g_rows[c][:, :, first + lo : first + hi]
 
         def value_rows(u):
             return values[u][:].rearrange("p (j t) -> p j t", j=PACK)
@@ -136,16 +135,16 @@ def tile_mix_tierg_mul_kernel(tc, g, w8_words, w8_scales, d, out):
             return staged[u][:, PACK * lo :].rearrange("p (c j i) -> p c j i", j=PACK, i=RUN)
 
         def cast(copy, u, lo, hi):
-            copy(out=grouped_walk(g_at[u], lo, hi), in_=rows_walk(g_cols(u, lo, hi), RUN))
+            copy(out=grouped_walk(g_at[u], lo, hi, RUN), in_=rows_walk(g_cols(u, lo, hi), RUN))
 
-        def cast_shared(u, split, width):
-            cast(nc.vector.tensor_copy, u, 0, split)
-            cast(nc.scalar.copy, u, split, width)
-
-        def widen(u, hi):
-            g_wide[u] = sb.tile([P, UNIT, PACK], F32, name="g_wide%d" % u, align_bytes=64)
-            nc.scalar.copy(
-                out=g_wide[u][:, 0:hi, :].rearrange("p (c i) j -> p c j i", i=RUN_WIDE), in_=rows_walk(g_cols(u, 0, hi), RUN_WIDE)
+        def cast_pool(u, lo, hi):
+            nc.gpsimd.tensor_scalar(
+                out=flat(g_at[u], lo, hi).rearrange("p (t j) -> p t j", j=PACK),
+                in0=g_cols(u, lo, hi).rearrange("p j t -> p t j"),
+                scalar1=1.0,
+                scalar2=0.0,
+                op0=ALU.mult,
+                op1=ALU.add,
             )
 
         def quantise(words, plane, fmt, at, u, count):
@@ -171,22 +170,16 @@ def tile_mix_tierg_mul_kernel(tc, g, w8_words, w8_scales, d, out):
             for v in range(u, u + count):
                 dequantise(v)
 
-        def quantise_r(h):
-            first = h * n_units // 2
-            quantise(r_words, r_plane, E4M3, r_at[first], first, n_units // 2)
+        def quantise_r(u, count):
+            quantise(r_words, r_plane, E4M3, r_at[u], u, count)
 
-        def subtract_wide(u, hi):
+        def subtract(u, lo=0, hi=UNIT):
             nc.vector.tensor_tensor(
-                out=flat(r_at[u], 0, hi).rearrange("p (t j) -> p t j", j=PACK),
-                in0=g_wide[u][:, 0:hi, :],
-                in1=value_rows(u)[:, :, 0:hi].rearrange("p j t -> p t j"),
+                out=grouped_walk(r_at[u], lo, hi, PAIR),
+                in0=rows_walk(g_cols(u, lo, hi), PAIR),
+                in1=rows_walk(value_rows(u)[:, :, lo:hi], PAIR),
                 op=ALU.subtract,
             )
-
-        def subtract_rows(u):
-            r_rows = sb.tile([P, PACK, UNIT], BF16, name="r_rows%d" % u, align_bytes=64)
-            nc.vector.tensor_tensor(out=r_rows[:], in0=g_cols(u, 0, UNIT), in1=value_rows(u), op=ALU.subtract)
-            nc.scalar.copy(out=grouped_walk(r_at[u], 0, UNIT), in_=rows_walk(r_rows[:], RUN))
 
         def stage(u, lo):
             staged[u] = sb.tile([P, BANK], F32, name="staged%d" % u, align_bytes=64)
@@ -194,7 +187,7 @@ def tile_mix_tierg_mul_kernel(tc, g, w8_words, w8_scales, d, out):
 
         def subtract_pool(u, lo):
             nc.gpsimd.tensor_tensor(
-                out=grouped_walk(r_at[u], lo, UNIT),
+                out=grouped_walk(r_at[u], lo, UNIT, RUN),
                 in0=rows_walk(g_cols(u, lo, UNIT), RUN),
                 in1=staged_walk(u, lo),
                 op=ALU.subtract,
@@ -219,66 +212,91 @@ def tile_mix_tierg_mul_kernel(tc, g, w8_words, w8_scales, d, out):
         def second_tier(m, h):
             product(m, h, r_words, r_plane, E4M3, False)
 
-        def finish(m, h):
+        def finish(m, h, queue):
             cols = slice(h * BANK, (h + 1) * BANK)
             result = sb.tile([P, BANK], F32, name="result%d_%d" % (m, h), align_bytes=64)
-            factor = d_early[m][:, cols] if m < early else d_late[h][:, m - early, :]
-            nc.vector.tensor_tensor(out=result[:], in0=factor, in1=sums[m, h][:], op=ALU.mult)
-            queue = nc.scalar if m % 2 else nc.sync
+            nc.vector.tensor_tensor(out=result[:], in0=factor(m, h), in1=sums[m, h][:], op=ALU.mult)
             queue.dma_start(out=out[m * P : (m + 1) * P, cols], in_=result[:])
 
+        QUARTER = 2 * UNIT
+        out_view = out.rearrange("(m p) t -> p m t", p=P)
+
+        def narrow_tier(i, u, words, plane, fmt, first):
+            cols = slice(u * UNIT, u * UNIT + QUARTER)
+            if first:
+                sums[i, u, 2] = bank(n_tiles + (u + i) % n_tiles)
+            for s in range(2):
+                m = 2 * i + s
+                nc.tensor.matmul_mx(
+                    out=sums[i, u, 2][:, s * QUARTER : (s + 1) * QUARTER],
+                    lhsT=w_words[:, m * P : (m + 1) * P].bitcast(E4M3),
+                    lhsT_scale=w_plane[:, m * P : (m + 1) * P],
+                    rhs=words[:, cols].bitcast(fmt),
+                    rhs_scale=plane[:, cols],
+                    start=first and s == 0,
+                    stop=not first and s == 1,
+                )
+
+        def narrow_first(i, u):
+            narrow_tier(i, u, q_words, q_plane, E5M2, True)
+
+        def narrow_second(i, u):
+            narrow_tier(i, u, r_words, r_plane, E4M3, False)
+
+        def narrow_finish(i, u, queue):
+            cols = slice(u * UNIT, u * UNIT + QUARTER)
+            result = sb.tile([P, 2, QUARTER], F32, name="narrow%d_%d" % (i, u), align_bytes=64)
+            nc.vector.tensor_tensor(
+                out=result[:], in0=d_pair[i][:, :, cols], in1=sums[i, u, 2][:].rearrange("p (s t) -> p s t", s=2), op=ALU.mult
+            )
+            queue.dma_start(out=out_view[:, 2 * i : 2 * i + 2, cols], in_=result[:])
+
+
         for u in range(2):
-            cast_shared(u, CAST_VECTOR_0, UNIT)
+            cast(nc.vector.tensor_copy, u, 0, 88)
+            cast(nc.scalar.copy, u, 88, UNIT)
         for u in range(2):
-            widen(u, UNIT)
             quantise_q(u, 1)
-        cast_shared(2, CAST_VECTOR_1, CHUNK)
-        widen(2, UNIT)
-        subtract_wide(0, UNIT)
+        cast(nc.vector.tensor_copy, 2, 0, 168)
+        cast(nc.scalar.copy, 2, 168, 2 * UNIT)
+        subtract(0)
         quantise_q(2, 2)
-        cast_shared(4, CAST_VECTOR_2, CHUNK)
-        widen(3, UNIT)
-        subtract_wide(1, UNIT)
+        cast(nc.vector.tensor_copy, 4, 0, 96)
+        cast(nc.scalar.copy, 4, 96, 2 * UNIT)
+        subtract(1)
         quantise_q(4, 2)
-
-        nc.gpsimd.tensor_scalar(
-            out=flat(g_at[6], 0, CAST_POOL_3).rearrange("p (t j) -> p t j", j=PACK),
-            in0=g_cols(6, 0, CAST_POOL_3).rearrange("p j t -> p t j"),
-            scalar1=1.0,
-            scalar2=0.0,
-            op0=ALU.mult,
-            op1=ALU.add,
-        )
-        cast(nc.scalar.copy, 6, CAST_POOL_3, CHUNK)
-        subtract_wide(2, UNIT)
-        subtract_wide(3, UNIT)
-        widen(4, SUBTRACT_VECTOR_4)
-        stage(4, SUBTRACT_VECTOR_4)
-        stage(5, 0)
-        widen(7, UNIT)
-
+        cast_pool(6, 0, 64)
+        cast(nc.scalar.copy, 6, 64, 2 * UNIT)
+        subtract(2)
+        subtract(3)
+        stage(4, 0)
         first_tier(0, 0, 0)
         quantise_q(6, 2)
-        quantise_r(0)
-        for m in range(n_tiles):
-            if m > 0:
-                first_tier(m, 0, m)
+        quantise_r(0, 4)
+        stage(7, 0)
+        second_tier(0, 0)
+        subtract_pool(4, 0)
+        subtract(5)
+        subtract(6)
+        for m in range(1, n_tiles):
+            first_tier(m, 0, m)
             second_tier(m, 0)
-
-        subtract_pool(4, SUBTRACT_VECTOR_4)
-        subtract_pool(5, 0)
-        subtract_wide(4, SUBTRACT_VECTOR_4)
-        subtract_rows(6)
-        subtract_wide(7, UNIT)
-        for m in range(n_tiles):
-            first_tier(m, 1, n_tiles + m)
-        for m in range(early):
-            finish(m, 0)
-
-        quantise_r(1)
-        for m in range(n_tiles):
-            second_tier(m, 1)
-        for m in range(early, n_tiles):
-            finish(m, 0)
-        for m in range(n_tiles):
-            finish(m, 1)
+        finish(0, 0, nc.sync)
+        quantise_r(4, 1)
+        quantise_r(5, 2)
+        subtract_pool(7, 0)
+        for i in range(2):
+            narrow_first(i, 4)
+            narrow_second(i, 4)
+        for i in range(2):
+            narrow_first(i, 6)
+        finish(1, 0, nc.scalar)
+        finish(2, 0, nc.sync)
+        finish(3, 0, nc.scalar)
+        quantise_r(7, 1)
+        for i in range(2):
+            narrow_second(i, 6)
+        narrow_finish(0, 4, nc.sync)
+        narrow_finish(1, 4, nc.scalar)
+        narrow_finish(0, 6, nc.sync)
+        narrow_finish(1, 6, nc.scalar)

@@ -37,7 +37,7 @@ def tile_mix_tierg_mul_kernel(tc, g, w8_words, w8_scales, d, out):
         ctx.enter_context(tc.manual_schedule())
 
         g_rows = [sb.tile([P, PACK, w], F32, name="g_rows%d" % c, align_bytes=64) for c, w in enumerate(LOADS)]
-        late = 6 * UNIT - 64
+        late = 6 * UNIT - 96
         g_at = [u * UNIT if u < 6 else late + (u - 6) * UNIT for u in range(n_units)]
         r_at = [(10 + u) * UNIT for u in range(4)] + [late, 8 * UNIT, 9 * UNIT, late]
         grouped_all = sb.tile([P, PACK * 14 * UNIT], BF16, name="grouped_all", align_bytes=64)
@@ -90,10 +90,8 @@ def tile_mix_tierg_mul_kernel(tc, g, w8_words, w8_scales, d, out):
         nc.sync.dma_start(out=w_words[:], in_=w8_words[0].rearrange("p n i -> p (n i)").bitcast(I32))
         d_view = d.rearrange("(m p) t -> p m t", p=P)
         d_pair = [sb.tile([P, 2, T], F32, name="d_pair%d" % i, align_bytes=64) for i in range(2)]
-        for m in range(2):
-            nc.sync.dma_start(out=d_pair[0][:, m, :], in_=d_view[:, m, :])
-        for h in range(2):
-            nc.sync.dma_start(out=d_pair[1][:, :, h * BANK : (h + 1) * BANK], in_=d_view[:, 2:4, h * BANK : (h + 1) * BANK])
+        for m in range(n_tiles):
+            nc.sync.dma_start(out=d_pair[m // 2][:, m % 2, :], in_=d_view[:, m, :])
 
         def factor(m, h):
             return d_pair[m // 2][:, m % 2, h * BANK : (h + 1) * BANK]
@@ -251,33 +249,53 @@ def tile_mix_tierg_mul_kernel(tc, g, w8_words, w8_scales, d, out):
             )
             queue.dma_start(out=out_view[:, 2 * i : 2 * i + 2, cols], in_=result[:])
 
+        g_wide = {}
+
+        def widen(u):
+            g_wide[u] = sb.tile([P, UNIT, PACK], F32, name="g_wide%d" % u, align_bytes=64)
+            nc.scalar.copy(out=g_wide[u][:].rearrange("p (c i) j -> p c j i", i=PAIR), in_=rows_walk(g_cols(u, 0, UNIT), PAIR))
+
+        def subtract_wide(u):
+            nc.vector.tensor_tensor(
+                out=flat(r_at[u], 0, UNIT).rearrange("p (t j) -> p t j", j=PACK),
+                in0=g_wide[u][:],
+                in1=value_rows(u).rearrange("p j t -> p t j"),
+                op=ALU.subtract,
+            )
+
 
         for u in range(2):
             cast(nc.vector.tensor_copy, u, 0, 88)
             cast(nc.scalar.copy, u, 88, UNIT)
-        for u in range(2):
-            quantise_q(u, 1)
-        cast(nc.vector.tensor_copy, 2, 0, 168)
-        cast(nc.scalar.copy, 2, 168, 2 * UNIT)
-        subtract(0)
+        widen(0)
+        quantise_q(0, 1)
+        widen(1)
+        quantise_q(1, 1)
+        cast(nc.vector.tensor_copy, 2, 0, 192)
+        cast(nc.scalar.copy, 2, 192, 2 * UNIT)
+        widen(2)
+        subtract_wide(0)
         quantise_q(2, 2)
-        cast(nc.vector.tensor_copy, 4, 0, 96)
-        cast(nc.scalar.copy, 4, 96, 2 * UNIT)
-        subtract(1)
+        cast(nc.vector.tensor_copy, 4, 0, 128)
+        cast(nc.scalar.copy, 4, 128, 2 * UNIT)
+        widen(3)
+        subtract_wide(1)
         quantise_q(4, 2)
-        cast_pool(6, 0, 64)
-        cast(nc.scalar.copy, 6, 64, 2 * UNIT)
-        subtract(2)
-        subtract(3)
+        cast_pool(6, 0, 96)
+        cast(nc.scalar.copy, 6, 96, 2 * UNIT)
+        subtract_wide(2)
+        subtract_wide(3)
+        widen(5)
         stage(4, 0)
+        widen(6)
         first_tier(0, 0, 0)
         quantise_q(6, 2)
         quantise_r(0, 4)
         stage(7, 0)
         second_tier(0, 0)
         subtract_pool(4, 0)
-        subtract(5)
-        subtract(6)
+        subtract_wide(5)
+        subtract_wide(6)
         for m in range(1, n_tiles):
             first_tier(m, 0, m)
             second_tier(m, 0)
@@ -292,11 +310,11 @@ def tile_mix_tierg_mul_kernel(tc, g, w8_words, w8_scales, d, out):
             narrow_first(i, 6)
         finish(1, 0, nc.scalar)
         finish(2, 0, nc.sync)
-        finish(3, 0, nc.scalar)
+        narrow_finish(0, 4, nc.scalar)
         quantise_r(7, 1)
         for i in range(2):
             narrow_second(i, 6)
-        narrow_finish(0, 4, nc.sync)
+        finish(3, 0, nc.sync)
         narrow_finish(1, 4, nc.scalar)
         narrow_finish(0, 6, nc.sync)
         narrow_finish(1, 6, nc.scalar)

@@ -36,21 +36,21 @@ def tile_mix_tierg_mul_kernel(tc, g, w8_words, w8_scales, d, out):
         psum = ctx.enter_context(tc.psum_pool(name="psum", bufs=1))
         ctx.enter_context(tc.manual_schedule())
 
-        g_rows = [sb.tile([P, PACK, w], F32, name="g_rows%d" % c, align_bytes=64) for c, w in enumerate(LOADS)]
-        late = 6 * UNIT - 96
-        g_at = [u * UNIT if u < 6 else late + (u - 6) * UNIT for u in range(n_units)]
+        g_rows = [sb.tile([P, PACK, w], F32, name="g_rows%d" % c, align_bytes=256) for c, w in enumerate(LOADS)]
+        late = 6 * UNIT - 104
+        g_at = [u * UNIT for u in range(6)] + [14 * UNIT, late]
         r_at = [(10 + u) * UNIT for u in range(4)] + [late, 8 * UNIT, 9 * UNIT, late]
-        grouped_all = sb.tile([P, PACK * 14 * UNIT], BF16, name="grouped_all", align_bytes=64)
-        eye_words = sb.tile([P, K], U32, name="eye_words", align_bytes=64)
-        eye_plane = sb.tile([P, K], U8, name="eye_plane", align_bytes=64)
-        q_words = sb.tile([P, T], U32, name="q_words", align_bytes=64)
-        q_plane = sb.tile([P, T], U8, name="q_plane", align_bytes=64)
-        r_words = sb.tile([P, T], U32, name="r_words", align_bytes=64)
-        r_plane = sb.tile([P, T], U8, name="r_plane", align_bytes=64)
-        w_words = sb.tile([P, N], I32, name="w_words", align_bytes=64)
-        w_plane = sb.tile([P, N], U8, name="w_plane", align_bytes=64)
-        ramp = sb.tile([P, RAMP], BF16, name="ramp", align_bytes=64)
-        eye_grouped = sb.tile([P, PACK * K], BF16, name="eye_grouped", align_bytes=64)
+        grouped_all = sb.tile([P, PACK * 15 * UNIT], BF16, name="grouped_all", align_bytes=256)
+        eye_words = sb.tile([P, K], U32, name="eye_words", align_bytes=256)
+        eye_plane = sb.tile([P, K], U8, name="eye_plane", align_bytes=256)
+        q_words = sb.tile([P, T], U32, name="q_words", align_bytes=256)
+        q_plane = sb.tile([P, T], U8, name="q_plane", align_bytes=256)
+        r_words = sb.tile([P, T], U32, name="r_words", align_bytes=256)
+        r_plane = sb.tile([P, T], U8, name="r_plane", align_bytes=256)
+        w_words = sb.tile([P, N], I32, name="w_words", align_bytes=256)
+        w_plane = sb.tile([P, N], U8, name="w_plane", align_bytes=256)
+        ramp = sb.tile([P, RAMP], BF16, name="ramp", align_bytes=256)
+        eye_grouped = sb.tile([P, PACK * K], BF16, name="eye_grouped", align_bytes=256)
 
         def bank(b):
             return psum.tile([P, BANK], F32, name="bank%d" % b, tag="bank%d" % b)
@@ -82,14 +82,11 @@ def tile_mix_tierg_mul_kernel(tc, g, w8_words, w8_scales, d, out):
                 in_=eye_grouped[:, PACK * first : PACK * (first + K // 2)],
             )
 
-        for q in range(4):
-            nc.sync.dma_start(
-                out=w_plane[32 * q : 32 * q + 4, :].bitcast(I32),
-                in_=w8_scales[0, 4 * q : 4 * q + 4, :].bitcast(I32),
-            )
+        for r in range(4):
+            nc.sync.dma_start(out=w_plane[r:P:32, :].bitcast(I32), in_=w8_scales[0, r:16:4, :].bitcast(I32))
         nc.sync.dma_start(out=w_words[:], in_=w8_words[0].rearrange("p n i -> p (n i)").bitcast(I32))
         d_view = d.rearrange("(m p) t -> p m t", p=P)
-        d_pair = [sb.tile([P, 2, T], F32, name="d_pair%d" % i, align_bytes=64) for i in range(2)]
+        d_pair = [sb.tile([P, 2, T], F32, name="d_pair%d" % i, align_bytes=256) for i in range(2)]
         for m in range(n_tiles):
             nc.sync.dma_start(out=d_pair[m // 2][:, m % 2, :], in_=d_view[:, m, :])
 
@@ -180,7 +177,7 @@ def tile_mix_tierg_mul_kernel(tc, g, w8_words, w8_scales, d, out):
             )
 
         def stage(u, lo):
-            staged[u] = sb.tile([P, BANK], F32, name="staged%d" % u, align_bytes=64)
+            staged[u] = sb.tile([P, BANK], F32, name="staged%d" % u, align_bytes=256)
             nc.scalar.copy(out=staged_walk(u, lo), in_=rows_walk(value_rows(u)[:, :, lo:UNIT], RUN))
 
         def subtract_pool(u, lo):
@@ -212,7 +209,7 @@ def tile_mix_tierg_mul_kernel(tc, g, w8_words, w8_scales, d, out):
 
         def finish(m, h, queue):
             cols = slice(h * BANK, (h + 1) * BANK)
-            result = sb.tile([P, BANK], F32, name="result%d_%d" % (m, h), align_bytes=64)
+            result = sb.tile([P, BANK], F32, name="result%d_%d" % (m, h), align_bytes=256)
             nc.vector.tensor_tensor(out=result[:], in0=factor(m, h), in1=sums[m, h][:], op=ALU.mult)
             queue.dma_start(out=out[m * P : (m + 1) * P, cols], in_=result[:])
 
@@ -243,7 +240,7 @@ def tile_mix_tierg_mul_kernel(tc, g, w8_words, w8_scales, d, out):
 
         def narrow_finish(i, u, queue):
             cols = slice(u * UNIT, u * UNIT + QUARTER)
-            result = sb.tile([P, 2, QUARTER], F32, name="narrow%d_%d" % (i, u), align_bytes=64)
+            result = sb.tile([P, 2, QUARTER], F32, name="narrow%d_%d" % (i, u), align_bytes=256)
             nc.vector.tensor_tensor(
                 out=result[:], in0=d_pair[i][:, :, cols], in1=sums[i, u, 2][:].rearrange("p (s t) -> p s t", s=2), op=ALU.mult
             )
@@ -252,7 +249,7 @@ def tile_mix_tierg_mul_kernel(tc, g, w8_words, w8_scales, d, out):
         g_wide = {}
 
         def widen(u):
-            g_wide[u] = sb.tile([P, UNIT, PACK], F32, name="g_wide%d" % u, align_bytes=64)
+            g_wide[u] = sb.tile([P, UNIT, PACK], F32, name="g_wide%d" % u, align_bytes=256)
             nc.scalar.copy(out=g_wide[u][:].rearrange("p (c i) j -> p c j i", i=PAIR), in_=rows_walk(g_cols(u, 0, UNIT), PAIR))
 
         def subtract_wide(u):
@@ -271,33 +268,36 @@ def tile_mix_tierg_mul_kernel(tc, g, w8_words, w8_scales, d, out):
         quantise_q(0, 1)
         widen(1)
         quantise_q(1, 1)
-        cast(nc.vector.tensor_copy, 2, 0, 192)
-        cast(nc.scalar.copy, 2, 192, 2 * UNIT)
+        cast(nc.vector.tensor_copy, 2, 0, 168)
+        cast(nc.scalar.copy, 2, 168, 2 * UNIT)
         widen(2)
         subtract_wide(0)
         quantise_q(2, 2)
-        cast(nc.vector.tensor_copy, 4, 0, 128)
-        cast(nc.scalar.copy, 4, 128, 2 * UNIT)
+        cast(nc.vector.tensor_copy, 4, 0, 160)
+        cast(nc.scalar.copy, 4, 160, 2 * UNIT)
         widen(3)
         subtract_wide(1)
         quantise_q(4, 2)
-        cast_pool(6, 0, 96)
-        cast(nc.scalar.copy, 6, 96, 2 * UNIT)
+        cast_pool(7, 0, 104)
+        cast(nc.scalar.copy, 6, 0, UNIT)
+        cast(nc.scalar.copy, 7, 104, UNIT)
         subtract_wide(2)
         subtract_wide(3)
-        widen(5)
         stage(4, 0)
         widen(6)
-        first_tier(0, 0, 0)
-        quantise_q(6, 2)
+        for m in range(2):
+            first_tier(m, 0, m)
+        quantise_q(6, 1)
+        quantise_q(7, 1)
         quantise_r(0, 4)
         stage(7, 0)
         second_tier(0, 0)
         subtract_pool(4, 0)
-        subtract_wide(5)
+        subtract(5)
         subtract_wide(6)
         for m in range(1, n_tiles):
-            first_tier(m, 0, m)
+            if m >= 2:
+                first_tier(m, 0, m)
             second_tier(m, 0)
         finish(0, 0, nc.sync)
         quantise_r(4, 1)

@@ -37,7 +37,7 @@ def tile_mix_tierg_mul_kernel(tc, g, w8_words, w8_scales, d, out):
         ctx.enter_context(tc.manual_schedule())
 
         g_rows = [sb.tile([P, PACK, w], F32, name="g_rows%d" % c, align_bytes=256) for c, w in enumerate(LOADS)]
-        late = 6 * UNIT - 104
+        late = 6 * UNIT - 80
         g_at = [u * UNIT for u in range(6)] + [14 * UNIT, late]
         r_at = [(10 + u) * UNIT for u in range(4)] + [late, 8 * UNIT, 9 * UNIT, late]
         grouped_all = sb.tile([P, PACK * 15 * UNIT], BF16, name="grouped_all", align_bytes=256)
@@ -130,7 +130,7 @@ def tile_mix_tierg_mul_kernel(tc, g, w8_words, w8_scales, d, out):
             return staged[u][:, PACK * lo :].rearrange("p (c j i) -> p c j i", j=PACK, i=RUN)
 
         def cast(copy, u, lo, hi):
-            copy(out=grouped_walk(g_at[u], lo, hi, RUN), in_=rows_walk(g_cols(u, lo, hi), RUN))
+            copy(out=grouped_walk(g_at[u], lo, hi, PAIR), in_=rows_walk(g_cols(u, lo, hi), PAIR))
 
         def cast_pool(u, lo, hi):
             nc.gpsimd.tensor_scalar(
@@ -268,19 +268,19 @@ def tile_mix_tierg_mul_kernel(tc, g, w8_words, w8_scales, d, out):
         quantise_q(0, 1)
         widen(1)
         quantise_q(1, 1)
-        cast(nc.vector.tensor_copy, 2, 0, 168)
-        cast(nc.scalar.copy, 2, 168, 2 * UNIT)
+        cast(nc.vector.tensor_copy, 2, 0, 184)
+        cast(nc.scalar.copy, 2, 184, 2 * UNIT)
         widen(2)
         subtract_wide(0)
         quantise_q(2, 2)
-        cast(nc.vector.tensor_copy, 4, 0, 160)
-        cast(nc.scalar.copy, 4, 160, 2 * UNIT)
+        cast(nc.vector.tensor_copy, 4, 0, 144)
+        cast(nc.scalar.copy, 4, 144, 2 * UNIT)
         widen(3)
         subtract_wide(1)
         quantise_q(4, 2)
-        cast_pool(7, 0, 104)
+        cast_pool(7, 0, 80)
         cast(nc.scalar.copy, 6, 0, UNIT)
-        cast(nc.scalar.copy, 7, 104, UNIT)
+        cast(nc.scalar.copy, 7, 80, UNIT)
         subtract_wide(2)
         subtract_wide(3)
         stage(4, 0)

@@ -21,96 +21,99 @@ BANK = 512
 PAIR = 2
 RUN = 4
 RAMP = 256
-WARMUPS = 2
-LOADS = (256, 256, 256, 256)
+ALIGN = 256
+SLOTS = 12
+G_AT = [s * UNIT for s in (0, 1, 0, 1, 4, 5, 3, 4)]
+R_AT = [s * UNIT for s in (6, 7, 8, 9, 3, 10, 11, 3)]
 
 
 def tile_mix_tierg_mul_kernel(tc, g, w8_words, w8_scales, d, out):
     nc = tc.nc
-    n_units = T // UNIT
     n_tiles = N // P
-    starts = [sum(LOADS[:c]) for c in range(len(LOADS))]
 
     with ExitStack() as ctx:
         sb = ctx.enter_context(tc.tile_pool(name="sb", bufs=1))
         psum = ctx.enter_context(tc.psum_pool(name="psum", bufs=1))
         ctx.enter_context(tc.manual_schedule())
 
-        g_rows = [sb.tile([P, PACK, w], F32, name="g_rows%d" % c, align_bytes=256) for c, w in enumerate(LOADS)]
-        late = 6 * UNIT - 80
-        g_at = [u * UNIT for u in range(6)] + [14 * UNIT, late]
-        r_at = [(10 + u) * UNIT for u in range(4)] + [late, 8 * UNIT, 9 * UNIT, late]
-        grouped_all = sb.tile([P, PACK * 15 * UNIT], BF16, name="grouped_all", align_bytes=256)
-        eye_words = sb.tile([P, K], U32, name="eye_words", align_bytes=256)
-        eye_plane = sb.tile([P, K], U8, name="eye_plane", align_bytes=256)
-        q_words = sb.tile([P, T], U32, name="q_words", align_bytes=256)
-        q_plane = sb.tile([P, T], U8, name="q_plane", align_bytes=256)
-        r_words = sb.tile([P, T], U32, name="r_words", align_bytes=256)
-        r_plane = sb.tile([P, T], U8, name="r_plane", align_bytes=256)
-        w_words = sb.tile([P, N], I32, name="w_words", align_bytes=256)
-        w_plane = sb.tile([P, N], U8, name="w_plane", align_bytes=256)
-        ramp = sb.tile([P, RAMP], BF16, name="ramp", align_bytes=256)
-        eye_grouped = sb.tile([P, PACK * K], BF16, name="eye_grouped", align_bytes=256)
+        grouped = sb.tile([P, PACK * SLOTS * UNIT], BF16, name="grouped", align_bytes=ALIGN)
+        eye_words = sb.tile([P, K], U32, name="eye_words", align_bytes=ALIGN)
+        eye_plane = sb.tile([P, K], U8, name="eye_plane", align_bytes=ALIGN)
+        q_words = sb.tile([P, T], U32, name="q_words", align_bytes=ALIGN)
+        q_plane = sb.tile([P, T], U8, name="q_plane", align_bytes=ALIGN)
+        r_words = sb.tile([P, T], U32, name="r_words", align_bytes=ALIGN)
+        r_plane = sb.tile([P, T], U8, name="r_plane", align_bytes=ALIGN)
+        w_words = sb.tile([P, N], I32, name="w_words", align_bytes=ALIGN)
+        w_plane = sb.tile([P, N], U8, name="w_plane", align_bytes=ALIGN)
+        ramp = sb.tile([P, RAMP], BF16, name="ramp", align_bytes=ALIGN)
+        eye_grouped = sb.tile([P, PACK * K], BF16, name="eye_grouped", align_bytes=ALIGN)
+
+        g_view = g.rearrange("(p j) t -> p j t", j=PACK)
+        d_view = d.rearrange("(m p) t -> p m t", p=P)
+        out_view = out.rearrange("(m p) t -> p m t", p=P)
+        g_rows = {}
+        d_part = {}
+        values = {}
+        staged = {}
+        g_wide = {}
+        sums = {}
+        results = {}
 
         def bank(b):
             return psum.tile([P, BANK], F32, name="bank%d" % b, tag="bank%d" % b)
 
-        g_view = g.rearrange("(p j) t -> p j t", j=PACK)
+        def load_g(first, count, queue=nc.sync):
+            rows = sb.tile([P, PACK, count * UNIT], F32, name="g_rows%d" % first, align_bytes=ALIGN)
+            queue.dma_start(out=rows[:], in_=g_view[:, :, first * UNIT : (first + count) * UNIT])
+            for u in range(first, first + count):
+                g_rows[u] = (rows, (u - first) * UNIT)
 
-        def load_g(c):
-            nc.sync.dma_start(out=g_rows[c][:], in_=g_view[:, :, starts[c] : starts[c] + LOADS[c]])
+        def load_scales(queue=nc.sync):
+            for r in range(4):
+                queue.dma_start(out=w_plane[r:P:32, :].bitcast(I32), in_=w8_scales[0, r:16:4, :].bitcast(I32))
 
-        for c in range(len(LOADS)):
-            load_g(c)
+        def load_w(queue=nc.sync):
+            queue.dma_start(out=w_words[:], in_=w8_words[0].rearrange("p n i -> p (n i)").bitcast(I32))
 
-        nc.vector.memset(w_plane[:].bitcast(I32), 0)
+        def load_d(m, tiles, u, units, queue=nc.sync):
+            part = sb.tile([P, tiles, units * UNIT], F32, name="d%d_%d" % (m, u), align_bytes=ALIGN)
+            queue.dma_start(out=part[:], in_=d_view[:, m : m + tiles, u * UNIT : (u + units) * UNIT])
+            for x in range(m, m + tiles):
+                for v in range(u, u + units):
+                    d_part[x, v] = (part, x - m, (v - u) * UNIT)
 
-        nc.gpsimd.iota(ramp[:], pattern=[[1, RAMP]], base=RAMP // 2, channel_multiplier=-PACK, allow_small_or_imprecise_dtypes=True)
-        for j in range(PACK):
-            for x in range(0, K, RAMP):
+        def identity(first, width):
+            for at in range(PACK * first, PACK * (first + width), RAMP):
                 nc.vector.tensor_scalar(
-                    out=eye_grouped[:, j * K + x : j * K + x + RAMP],
+                    out=eye_grouped[:, at : at + RAMP],
                     in0=ramp[:],
-                    scalar1=float(RAMP // 2 + j - x),
+                    scalar1=float(RAMP // 2 + at // K - at % K),
                     scalar2=None,
                     op0=ALU.is_equal,
                 )
-        for first in range(0, K, K // 2):
+
+        def quantise_identity(first, width):
             nc.vector.quantize_mx(
-                out=eye_words[:, first : first + K // 2].bitcast(E4M3),
-                scales=eye_plane[:, first : first + K // 2],
-                in_=eye_grouped[:, PACK * first : PACK * (first + K // 2)],
+                out=eye_words[:, first : first + width].bitcast(E4M3),
+                scales=eye_plane[:, first : first + width],
+                in_=eye_grouped[:, PACK * first : PACK * (first + width)],
             )
 
-        for r in range(4):
-            nc.sync.dma_start(out=w_plane[r:P:32, :].bitcast(I32), in_=w8_scales[0, r:16:4, :].bitcast(I32))
-        nc.sync.dma_start(out=w_words[:], in_=w8_words[0].rearrange("p n i -> p (n i)").bitcast(I32))
-        d_view = d.rearrange("(m p) t -> p m t", p=P)
-        d_pair = [sb.tile([P, 2, T], F32, name="d_pair%d" % i, align_bytes=256) for i in range(2)]
-        for m in range(n_tiles):
-            nc.sync.dma_start(out=d_pair[m // 2][:, m % 2, :], in_=d_view[:, m, :])
-
-        def factor(m, h):
-            return d_pair[m // 2][:, m % 2, h * BANK : (h + 1) * BANK]
-
-        warm_bank = bank(0)
-        for i in range(WARMUPS):
-            nc.tensor.matmul_mx(
-                out=warm_bank[:],
-                lhsT=eye_words[:, 0:P].bitcast(E4M3),
-                lhsT_scale=eye_plane[:, 0:P],
-                rhs=eye_words[:].bitcast(E4M3),
-                rhs_scale=eye_plane[:],
-                start=True,
-                stop=True,
-            )
-
-        values = {}
-        staged = {}
-        sums = {}
+        def warm_up(count, width):
+            warm_bank = bank(0)
+            for i in range(count):
+                nc.tensor.matmul_mx(
+                    out=warm_bank[:, 0:width],
+                    lhsT=eye_words[:, 0:P].bitcast(E4M3),
+                    lhsT_scale=eye_plane[:, 0:P],
+                    rhs=eye_words[:, 0:width].bitcast(E4M3),
+                    rhs_scale=eye_plane[:, 0:width],
+                    start=True,
+                    stop=True,
+                )
 
         def flat(at, lo, hi):
-            return grouped_all[:, PACK * (at + lo) : PACK * (at + hi)]
+            return grouped[:, PACK * (at + lo) : PACK * (at + hi)]
 
         def grouped_walk(at, lo, hi, run):
             return flat(at, lo, hi).rearrange("p (c i j) -> p c j i", i=run, j=PACK)
@@ -119,22 +122,18 @@ def tile_mix_tierg_mul_kernel(tc, g, w8_words, w8_scales, d, out):
             return rows.rearrange("p j (c i) -> p c j i", i=run)
 
         def g_cols(u, lo, hi):
-            c = max(x for x in range(len(LOADS)) if starts[x] <= u * UNIT)
-            first = u * UNIT - starts[c]
-            return g_rows[c][:, :, first + lo : first + hi]
+            rows, first = g_rows[u]
+            return rows[:, :, first + lo : first + hi]
 
         def value_rows(u):
             return values[u][:].rearrange("p (j t) -> p j t", j=PACK)
 
-        def staged_walk(u, lo):
-            return staged[u][:, PACK * lo :].rearrange("p (c j i) -> p c j i", j=PACK, i=RUN)
-
         def cast(copy, u, lo, hi):
-            copy(out=grouped_walk(g_at[u], lo, hi, PAIR), in_=rows_walk(g_cols(u, lo, hi), PAIR))
+            copy(out=grouped_walk(G_AT[u], lo, hi, PAIR), in_=rows_walk(g_cols(u, lo, hi), PAIR))
 
         def cast_pool(u, lo, hi):
             nc.gpsimd.tensor_scalar(
-                out=flat(g_at[u], lo, hi).rearrange("p (t j) -> p t j", j=PACK),
+                out=flat(G_AT[u], lo, hi).rearrange("p (t j) -> p t j", j=PACK),
                 in0=g_cols(u, lo, hi).rearrange("p j t -> p t j"),
                 scalar1=1.0,
                 scalar2=0.0,
@@ -146,9 +145,9 @@ def tile_mix_tierg_mul_kernel(tc, g, w8_words, w8_scales, d, out):
             cols = slice(u * UNIT, (u + count) * UNIT)
             nc.vector.quantize_mx(out=words[:, cols].bitcast(fmt), scales=plane[:, cols], in_=flat(at, 0, count * UNIT))
 
-        def dequantise(u):
+        def dequantise(u, b):
             cols = slice(u * UNIT, (u + 1) * UNIT)
-            values[u] = bank(n_tiles + u % n_tiles)
+            values[u] = bank(b)
             for j in range(PACK):
                 nc.tensor.matmul_mx(
                     out=values[u][:, j * UNIT : (j + 1) * UNIT],
@@ -161,160 +160,194 @@ def tile_mix_tierg_mul_kernel(tc, g, w8_words, w8_scales, d, out):
                 )
 
         def quantise_q(u, count):
-            quantise(q_words, q_plane, E5M2, g_at[u], u, count)
-            for v in range(u, u + count):
-                dequantise(v)
+            quantise(q_words, q_plane, E5M2, G_AT[u], u, count)
 
         def quantise_r(u, count):
-            quantise(r_words, r_plane, E4M3, r_at[u], u, count)
+            quantise(r_words, r_plane, E4M3, R_AT[u], u, count)
 
         def subtract(u, lo=0, hi=UNIT):
             nc.vector.tensor_tensor(
-                out=grouped_walk(r_at[u], lo, hi, PAIR),
+                out=grouped_walk(R_AT[u], lo, hi, PAIR),
                 in0=rows_walk(g_cols(u, lo, hi), PAIR),
                 in1=rows_walk(value_rows(u)[:, :, lo:hi], PAIR),
                 op=ALU.subtract,
             )
 
-        def stage(u, lo):
-            staged[u] = sb.tile([P, BANK], F32, name="staged%d" % u, align_bytes=256)
-            nc.scalar.copy(out=staged_walk(u, lo), in_=rows_walk(value_rows(u)[:, :, lo:UNIT], RUN))
-
-        def subtract_pool(u, lo):
-            nc.gpsimd.tensor_tensor(
-                out=grouped_walk(r_at[u], lo, UNIT, RUN),
-                in0=rows_walk(g_cols(u, lo, UNIT), RUN),
-                in1=staged_walk(u, lo),
-                op=ALU.subtract,
-            )
-
-        def product(m, h, words, plane, fmt, first):
-            cols = slice(h * BANK, (h + 1) * BANK)
-            nc.tensor.matmul_mx(
-                out=sums[m, h][:],
-                lhsT=w_words[:, m * P : (m + 1) * P].bitcast(E4M3),
-                lhsT_scale=w_plane[:, m * P : (m + 1) * P],
-                rhs=words[:, cols].bitcast(fmt),
-                rhs_scale=plane[:, cols],
-                start=first,
-                stop=not first,
-            )
-
-        def first_tier(m, h, b):
-            sums[m, h] = bank(b)
-            product(m, h, q_words, q_plane, E5M2, True)
-
-        def second_tier(m, h):
-            product(m, h, r_words, r_plane, E4M3, False)
-
-        def finish(m, h, queue):
-            cols = slice(h * BANK, (h + 1) * BANK)
-            result = sb.tile([P, BANK], F32, name="result%d_%d" % (m, h), align_bytes=256)
-            nc.vector.tensor_tensor(out=result[:], in0=factor(m, h), in1=sums[m, h][:], op=ALU.mult)
-            queue.dma_start(out=out[m * P : (m + 1) * P, cols], in_=result[:])
-
-        QUARTER = 2 * UNIT
-        out_view = out.rearrange("(m p) t -> p m t", p=P)
-
-        def narrow_tier(i, u, words, plane, fmt, first):
-            cols = slice(u * UNIT, u * UNIT + QUARTER)
-            if first:
-                sums[i, u, 2] = bank(n_tiles + (u + i) % n_tiles)
-            for s in range(2):
-                m = 2 * i + s
-                nc.tensor.matmul_mx(
-                    out=sums[i, u, 2][:, s * QUARTER : (s + 1) * QUARTER],
-                    lhsT=w_words[:, m * P : (m + 1) * P].bitcast(E4M3),
-                    lhsT_scale=w_plane[:, m * P : (m + 1) * P],
-                    rhs=words[:, cols].bitcast(fmt),
-                    rhs_scale=plane[:, cols],
-                    start=first and s == 0,
-                    stop=not first and s == 1,
-                )
-
-        def narrow_first(i, u):
-            narrow_tier(i, u, q_words, q_plane, E5M2, True)
-
-        def narrow_second(i, u):
-            narrow_tier(i, u, r_words, r_plane, E4M3, False)
-
-        def narrow_finish(i, u, queue):
-            cols = slice(u * UNIT, u * UNIT + QUARTER)
-            result = sb.tile([P, 2, QUARTER], F32, name="narrow%d_%d" % (i, u), align_bytes=256)
-            nc.vector.tensor_tensor(
-                out=result[:], in0=d_pair[i][:, :, cols], in1=sums[i, u, 2][:].rearrange("p (s t) -> p s t", s=2), op=ALU.mult
-            )
-            queue.dma_start(out=out_view[:, 2 * i : 2 * i + 2, cols], in_=result[:])
-
-        g_wide = {}
-
         def widen(u):
-            g_wide[u] = sb.tile([P, UNIT, PACK], F32, name="g_wide%d" % u, align_bytes=256)
+            g_wide[u] = sb.tile([P, UNIT, PACK], F32, name="g_wide%d" % u, align_bytes=ALIGN)
             nc.scalar.copy(out=g_wide[u][:].rearrange("p (c i) j -> p c j i", i=PAIR), in_=rows_walk(g_cols(u, 0, UNIT), PAIR))
 
         def subtract_wide(u):
             nc.vector.tensor_tensor(
-                out=flat(r_at[u], 0, UNIT).rearrange("p (t j) -> p t j", j=PACK),
+                out=flat(R_AT[u], 0, UNIT).rearrange("p (t j) -> p t j", j=PACK),
                 in0=g_wide[u][:],
                 in1=value_rows(u).rearrange("p j t -> p t j"),
                 op=ALU.subtract,
             )
 
+        def staged_walk(u, lo):
+            return staged[u][:, PACK * lo :].rearrange("p (c j i) -> p c j i", j=PACK, i=RUN)
 
-        for u in range(2):
-            cast(nc.vector.tensor_copy, u, 0, 88)
-            cast(nc.scalar.copy, u, 88, UNIT)
-        widen(0)
+        def stage(u, lo=0):
+            staged[u] = sb.tile([P, BANK], F32, name="staged%d" % u, align_bytes=ALIGN)
+            nc.scalar.copy(out=staged_walk(u, lo), in_=rows_walk(value_rows(u)[:, :, lo:UNIT], RUN))
+
+        def subtract_pool(u, lo=0):
+            nc.gpsimd.tensor_tensor(
+                out=grouped_walk(R_AT[u], lo, UNIT, RUN),
+                in0=rows_walk(g_cols(u, lo, UNIT), RUN),
+                in1=staged_walk(u, lo),
+                op=ALU.subtract,
+            )
+
+        def tier(block, words, plane, fmt, first):
+            m, tiles, u, units = block
+            width = units * UNIT
+            cols = slice(u * UNIT, u * UNIT + width)
+            for s in range(tiles):
+                nc.tensor.matmul_mx(
+                    out=sums[block][:, s * width : (s + 1) * width],
+                    lhsT=w_words[:, (m + s) * P : (m + s + 1) * P].bitcast(E4M3),
+                    lhsT_scale=w_plane[:, (m + s) * P : (m + s + 1) * P],
+                    rhs=words[:, cols].bitcast(fmt),
+                    rhs_scale=plane[:, cols],
+                    start=first and s == 0,
+                    stop=not first and s == tiles - 1,
+                )
+
+        def first_tier(block, b):
+            sums[block] = bank(b)
+            tier(block, q_words, q_plane, E5M2, True)
+
+        def second_tier(block):
+            tier(block, r_words, r_plane, E4M3, False)
+
+        def result_tile(part):
+            m, tiles, u, units = part
+            tile = sb.tile([P, tiles, units * UNIT], F32, name="result%d_%d" % (m, u), align_bytes=ALIGN)
+            for x in range(m, m + tiles):
+                for v in range(u, u + units):
+                    results[x, v] = (tile, x - m, (v - u) * UNIT)
+
+        def window(parts, block):
+            m, tiles, u, units = block
+            tile, row, col = parts[m, u]
+            return tile[:, row : row + tiles, col : col + units * UNIT]
+
+        def bank_rows(tile, block):
+            return tile[:, 0 : block[1] * block[3] * UNIT].rearrange("p (s t) -> p s t", s=block[1])
+
+        def multiply(block):
+            if (block[0], block[2]) not in results:
+                result_tile(block)
+            nc.vector.tensor_tensor(out=window(results, block), in0=window(d_part, block), in1=bank_rows(sums[block], block), op=ALU.mult)
+
+        def stage_sum(block):
+            staged[block] = sb.tile([P, BANK], F32, name="staged%d_%d" % (block[0], block[2]), align_bytes=ALIGN)
+            nc.scalar.copy(out=staged[block][:], in_=sums[block][:])
+
+        def multiply_pool(block):
+            if (block[0], block[2]) not in results:
+                result_tile(block)
+            nc.gpsimd.tensor_tensor(out=window(results, block), in0=window(d_part, block), in1=bank_rows(staged[block], block), op=ALU.mult)
+
+        def store(part, queue):
+            m, tiles, u, units = part
+            queue.dma_start(out=out_view[:, m : m + tiles, u * UNIT : (u + units) * UNIT], in_=window(results, part))
+
+        V, S = nc.vector.tensor_copy, nc.scalar.copy
+        load_g(0, 1)
+        load_g(1, 1)
+        load_g(2, 2)
+        load_g(4, 2)
+        load_g(6, 2)
+        nc.gpsimd.iota(ramp[:], pattern=[[1, RAMP]], base=RAMP // 2, channel_multiplier=-PACK, allow_small_or_imprecise_dtypes=True)
+        identity(0, 512)
+        quantise_identity(0, 256)
+        warm_up(2, 256)
+        wide = [(m, 1, 0, 4) for m in range(4)]
+        mid = [(2 * i, 2, 4, 2) for i in range(2)]
+        last = [(0, 4, 6 + i, 1) for i in range(2)]
+        cast(V, 0, 0, 80)
+        cast(S, 0, 80, UNIT)
+        quantise_identity(256, 256)
         quantise_q(0, 1)
-        widen(1)
+        dequantise(0, 4)
+        cast(V, 1, 0, 80)
+        cast(S, 1, 80, 128)
+        nc.vector.memset(w_plane[:].bitcast(I32), 0)
+        load_scales()
+        load_w()
+        load_d(0, 4, 0, 4)
+        load_d(0, 4, 4, 4)
+        widen(0)
         quantise_q(1, 1)
-        cast(nc.vector.tensor_copy, 2, 0, 184)
-        cast(nc.scalar.copy, 2, 184, 2 * UNIT)
-        widen(2)
+        dequantise(1, 5)
+        warm_up(1, 512)
+        widen(1)
+        cast(S, 2, 0, 96)
+        cast_pool(2, 96, 256)
         subtract_wide(0)
-        quantise_q(2, 2)
-        cast(nc.vector.tensor_copy, 4, 0, 144)
-        cast(nc.scalar.copy, 4, 144, 2 * UNIT)
-        widen(3)
         subtract_wide(1)
-        quantise_q(4, 2)
-        cast_pool(7, 0, 80)
-        cast(nc.scalar.copy, 6, 0, UNIT)
-        cast(nc.scalar.copy, 7, 80, UNIT)
+        quantise_q(2, 2)
+        dequantise(2, 6)
+        dequantise(3, 7)
+        cast(V, 4, 96, 256)
+        widen(2)
+        cast(S, 4, 0, 96)
+        quantise_r(0, 2)
+        widen(3)
+        quantise_q(4, 1)
+        quantise_q(5, 1)
+        dequantise(4, 4)
+        dequantise(5, 5)
+        cast_pool(7, 0, 112)
+        cast(S, 6, 0, 128)
+        cast(S, 7, 112, 128)
         subtract_wide(2)
         subtract_wide(3)
-        stage(4, 0)
+        stage(4)
+        first_tier(wide[0], 0)
+        first_tier(wide[1], 1)
+        quantise_q(6, 2)
+        dequantise(6, 6)
+        dequantise(7, 7)
+        quantise_r(2, 2)
         widen(6)
-        for m in range(2):
-            first_tier(m, 0, m)
-        quantise_q(6, 1)
-        quantise_q(7, 1)
-        quantise_r(0, 4)
-        stage(7, 0)
-        second_tier(0, 0)
-        subtract_pool(4, 0)
+        stage(7)
+        second_tier(wide[0])
+        second_tier(wide[1])
+        subtract_pool(4)
         subtract(5)
         subtract_wide(6)
-        for m in range(1, n_tiles):
-            if m >= 2:
-                first_tier(m, 0, m)
-            second_tier(m, 0)
-        finish(0, 0, nc.sync)
+        for m in (2, 3):
+            first_tier(wide[m], m)
+            second_tier(wide[m])
+        for i in range(2):
+            first_tier(mid[i], 4 + i)
+        multiply(wide[0])
+        store(wide[0], nc.sync)
+        multiply(wide[1])
+        store(wide[1], nc.sync)
         quantise_r(4, 1)
         quantise_r(5, 2)
-        subtract_pool(7, 0)
+        subtract_pool(7)
         for i in range(2):
-            narrow_first(i, 4)
-            narrow_second(i, 4)
-        for i in range(2):
-            narrow_first(i, 6)
-        finish(1, 0, nc.scalar)
-        finish(2, 0, nc.sync)
-        narrow_finish(0, 4, nc.scalar)
+            second_tier(mid[i])
+        first_tier(last[0], 6)
+        second_tier(last[0])
+        first_tier(last[1], 7)
+        multiply(wide[2])
+        store(wide[2], nc.sync)
+        multiply(wide[3])
+        store(wide[3], nc.sync)
+        multiply(mid[0])
+        store(mid[0], nc.sync)
         quantise_r(7, 1)
-        for i in range(2):
-            narrow_second(i, 6)
-        finish(3, 0, nc.sync)
-        narrow_finish(1, 4, nc.scalar)
-        narrow_finish(0, 6, nc.sync)
-        narrow_finish(1, 6, nc.scalar)
+        second_tier(last[1])
+        multiply(mid[1])
+        store(mid[1], nc.sync)
+        multiply(last[0])
+        store(last[0], nc.sync)
+        multiply(last[1])
+        store(last[1], nc.sync)

@@ -22,9 +22,9 @@ PAIR = 2
 RUN = 4
 RAMP = 256
 ALIGN = 256
-SLOTS = 12
-G_AT = [s * UNIT for s in (0, 1, 0, 1, 4, 5, 3, 4)]
-R_AT = [s * UNIT for s in (6, 7, 8, 9, 3, 10, 11, 3)]
+SLOTS = 14
+G_AT = [s * UNIT for s in (0, 1, 2, 3, 4, 5, 12, 13)]
+R_AT = [s * UNIT for s in (6, 7, 8, 9, 12, 10, 11, 12)]
 
 
 def tile_mix_tierg_mul_kernel(tc, g, w8_words, w8_scales, d, out):
@@ -58,6 +58,7 @@ def tile_mix_tierg_mul_kernel(tc, g, w8_words, w8_scales, d, out):
         g_wide = {}
         sums = {}
         results = {}
+        elsewhere = {}
 
         def bank(b):
             return psum.tile([P, BANK], F32, name="bank%d" % b, tag="bank%d" % b)
@@ -113,6 +114,8 @@ def tile_mix_tierg_mul_kernel(tc, g, w8_words, w8_scales, d, out):
                 )
 
         def flat(at, lo, hi):
+            if at in elsewhere:
+                return elsewhere[at][:, PACK * lo : PACK * hi]
             return grouped[:, PACK * (at + lo) : PACK * (at + hi)]
 
         def grouped_walk(at, lo, hi, run):
@@ -200,6 +203,31 @@ def tile_mix_tierg_mul_kernel(tc, g, w8_words, w8_scales, d, out):
                 op=ALU.subtract,
             )
 
+        def stage_grouped(u, lo=0):
+            staged[u] = sb.tile([P, UNIT, PACK], F32, name="staged%d" % u, align_bytes=ALIGN)
+            nc.scalar.copy(out=staged[u][:, lo:UNIT, :], in_=value_rows(u)[:, :, lo:UNIT].rearrange("p j t -> p t j"))
+
+        def subtract_pool_wide(u, lo=0):
+            nc.gpsimd.tensor_tensor(
+                out=flat(R_AT[u], lo, UNIT),
+                in0=g_wide[u][:, lo:UNIT, :].rearrange("p t j -> p (t j)"),
+                in1=staged[u][:, lo:UNIT, :].rearrange("p t j -> p (t j)"),
+                op=ALU.subtract,
+            )
+
+        def cast_wide(u, lo, hi):
+            nc.vector.tensor_copy(out=flat(G_AT[u], lo, hi), in_=g_wide[u][:, lo:hi, :].rearrange("p t j -> p (t j)"))
+
+        def cast_pool_wide(u, lo, hi):
+            nc.gpsimd.tensor_scalar(
+                out=flat(G_AT[u], lo, hi),
+                in0=g_wide[u][:, lo:hi, :].rearrange("p t j -> p (t j)"),
+                scalar1=1.0,
+                scalar2=0.0,
+                op0=ALU.mult,
+                op1=ALU.add,
+            )
+
         def tier(block, words, plane, fmt, first):
             m, tiles, u, units = block
             width = units * UNIT
@@ -267,7 +295,7 @@ def tile_mix_tierg_mul_kernel(tc, g, w8_words, w8_scales, d, out):
         warm_up(2, 256)
         wide = [(m, 1, 0, 4) for m in range(4)]
         mid = [(2 * i, 2, 4, 2) for i in range(2)]
-        last = [(0, 4, 6 + i, 1) for i in range(2)]
+        last = [(2 * i, 2, 6, 2) for i in range(2)]
         cast(V, 0, 0, 80)
         cast(S, 0, 80, UNIT)
         quantise_identity(256, 256)
@@ -278,43 +306,45 @@ def tile_mix_tierg_mul_kernel(tc, g, w8_words, w8_scales, d, out):
         nc.vector.memset(w_plane[:].bitcast(I32), 0)
         load_scales()
         load_w()
-        load_d(0, 4, 0, 4)
+        load_d(0, 2, 0, 4)
+        load_d(2, 2, 0, 4)
         load_d(0, 4, 4, 4)
         widen(0)
         quantise_q(1, 1)
         dequantise(1, 5)
         warm_up(1, 512)
         widen(1)
-        cast(S, 2, 0, 96)
-        cast_pool(2, 96, 256)
+        cast(V, 2, 0, 128)
+        cast(S, 2, 128, 256)
         subtract_wide(0)
         subtract_wide(1)
         quantise_q(2, 2)
         dequantise(2, 6)
         dequantise(3, 7)
-        cast(V, 4, 96, 256)
-        widen(2)
-        cast(S, 4, 0, 96)
+        cast(V, 4, 0, 96)
+        cast(S, 4, 96, 128)
+        cast(S, 5, 0, 128)
         quantise_r(0, 2)
-        widen(3)
         quantise_q(4, 1)
         quantise_q(5, 1)
         dequantise(4, 4)
         dequantise(5, 5)
-        cast_pool(7, 0, 112)
         cast(S, 6, 0, 128)
-        cast(S, 7, 112, 128)
-        subtract_wide(2)
-        subtract_wide(3)
+        cast(S, 7, 0, 128)
+        subtract(2)
+        subtract(3)
         stage(4)
         first_tier(wide[0], 0)
         first_tier(wide[1], 1)
-        quantise_q(6, 2)
+        quantise_q(6, 1)
         dequantise(6, 6)
+        quantise_q(7, 1)
         dequantise(7, 7)
         quantise_r(2, 2)
+
         widen(6)
-        stage(7)
+        widen(7)
+        stage_grouped(7)
         second_tier(wide[0])
         second_tier(wide[1])
         subtract_pool(4)
@@ -328,26 +358,26 @@ def tile_mix_tierg_mul_kernel(tc, g, w8_words, w8_scales, d, out):
         multiply(wide[0])
         store(wide[0], nc.sync)
         multiply(wide[1])
-        store(wide[1], nc.sync)
+        store(wide[1], nc.scalar)
         quantise_r(4, 1)
         quantise_r(5, 2)
-        subtract_pool(7)
+        subtract_pool_wide(7)
         for i in range(2):
             second_tier(mid[i])
-        first_tier(last[0], 6)
-        second_tier(last[0])
-        first_tier(last[1], 7)
+        for i in range(2):
+            first_tier(last[i], 6 + i)
         multiply(wide[2])
         store(wide[2], nc.sync)
         multiply(wide[3])
-        store(wide[3], nc.sync)
+        store(wide[3], nc.scalar)
         multiply(mid[0])
         store(mid[0], nc.sync)
         quantise_r(7, 1)
-        second_tier(last[1])
+        for i in range(2):
+            second_tier(last[i])
         multiply(mid[1])
-        store(mid[1], nc.sync)
+        store(mid[1], nc.scalar)
         multiply(last[0])
         store(last[0], nc.sync)
         multiply(last[1])
-        store(last[1], nc.sync)
+        store(last[1], nc.scalar)

@@ -20,11 +20,11 @@ UNIT = 128
 BANK = 512
 PAIR = 2
 RUN = 4
-RAMP = 256
+RAMP = 128
 ALIGN = 256
 SLOTS = 14
 G_AT = [s * UNIT for s in (0, 1, 2, 3, 4, 5, 12, 13)]
-R_AT = [s * UNIT for s in (6, 7, 8, 9, 12, 10, 11, 12)]
+R_AT = [s * UNIT for s in (6, 7, 8, 9, 13, 10, 11, 13)]
 
 
 def tile_mix_tierg_mul_kernel(tc, g, w8_words, w8_scales, d, out):
@@ -44,7 +44,8 @@ def tile_mix_tierg_mul_kernel(tc, g, w8_words, w8_scales, d, out):
         r_words = sb.tile([P, T], U32, name="r_words", align_bytes=ALIGN)
         r_plane = sb.tile([P, T], U8, name="r_plane", align_bytes=ALIGN)
         w_words = sb.tile([P, N], I32, name="w_words", align_bytes=ALIGN)
-        w_plane = sb.tile([P, N], U8, name="w_plane", align_bytes=ALIGN)
+        w_rows = sb.tile([P, N], U8, name="w_rows", align_bytes=ALIGN)
+        w_plane = w_rows[:, 0:N]
         ramp = sb.tile([P, RAMP], BF16, name="ramp", align_bytes=ALIGN)
         eye_grouped = sb.tile([P, PACK * K], BF16, name="eye_grouped", align_bytes=ALIGN)
 
@@ -71,7 +72,17 @@ def tile_mix_tierg_mul_kernel(tc, g, w8_words, w8_scales, d, out):
 
         def load_scales(queue=nc.sync):
             for r in range(4):
-                queue.dma_start(out=w_plane[r:P:32, :].bitcast(I32), in_=w8_scales[0, r:16:4, :].bitcast(I32))
+                queue.dma_start(out=w_rows[r:P:32, 0:N].bitcast(I32), in_=w8_scales[0, r:16:4, :].bitcast(I32))
+
+        def load_scale_rows(queue=nc.sync):
+            queue.dma_start(
+                out=w_rows[0:4, :].bitcast(I32).rearrange("r (q n) -> r q n", q=4),
+                in_=w8_scales[0].bitcast(I32).rearrange("(q r) n -> r q n", r=4),
+            )
+
+        def spread_scales(copy, dtype, first=1, last=4):
+            for q in range(first, last):
+                copy(out=w_rows[32 * q : 32 * q + 4, 0:N].bitcast(dtype), in_=w_rows[0:4, q * N : (q + 1) * N].bitcast(dtype))
 
         def load_w(queue=nc.sync):
             queue.dma_start(out=w_words[:], in_=w8_words[0].rearrange("p n i -> p (n i)").bitcast(I32))
@@ -88,7 +99,7 @@ def tile_mix_tierg_mul_kernel(tc, g, w8_words, w8_scales, d, out):
                 nc.vector.tensor_scalar(
                     out=eye_grouped[:, at : at + RAMP],
                     in0=ramp[:],
-                    scalar1=float(RAMP // 2 + at // K - at % K),
+                    scalar1=float((K - RAMP) // 2 + at // K - at % K),
                     scalar2=None,
                     op0=ALU.is_equal,
                 )
@@ -176,14 +187,17 @@ def tile_mix_tierg_mul_kernel(tc, g, w8_words, w8_scales, d, out):
                 op=ALU.subtract,
             )
 
-        def widen(u):
-            g_wide[u] = sb.tile([P, UNIT, PACK], F32, name="g_wide%d" % u, align_bytes=ALIGN)
-            nc.scalar.copy(out=g_wide[u][:].rearrange("p (c i) j -> p c j i", i=PAIR), in_=rows_walk(g_cols(u, 0, UNIT), PAIR))
+        def widen(u, at=None):
+            if at is None:
+                g_wide[u] = sb.tile([P, UNIT, PACK], F32, name="g_wide%d" % u, align_bytes=ALIGN)[:]
+            else:
+                g_wide[u] = flat(at, 0, 2 * UNIT).bitcast(F32).rearrange("p (t j) -> p t j", j=PACK)
+            nc.scalar.copy(out=g_wide[u].rearrange("p (c i) j -> p c j i", i=PAIR), in_=rows_walk(g_cols(u, 0, UNIT), PAIR))
 
         def subtract_wide(u):
             nc.vector.tensor_tensor(
                 out=flat(R_AT[u], 0, UNIT).rearrange("p (t j) -> p t j", j=PACK),
-                in0=g_wide[u][:],
+                in0=g_wide[u],
                 in1=value_rows(u).rearrange("p j t -> p t j"),
                 op=ALU.subtract,
             )
@@ -250,6 +264,20 @@ def tile_mix_tierg_mul_kernel(tc, g, w8_words, w8_scales, d, out):
         def second_tier(block):
             tier(block, r_words, r_plane, E4M3, False)
 
+        def second_tier_unit(block, u, closes):
+            m, tiles, first, units = block
+            for s in range(tiles):
+                at = (s * units + u - first) * UNIT
+                nc.tensor.matmul_mx(
+                    out=sums[block][:, at : at + UNIT],
+                    lhsT=w_words[:, (m + s) * P : (m + s + 1) * P].bitcast(E4M3),
+                    lhsT_scale=w_plane[:, (m + s) * P : (m + s + 1) * P],
+                    rhs=r_words[:, u * UNIT : (u + 1) * UNIT].bitcast(E4M3),
+                    rhs_scale=r_plane[:, u * UNIT : (u + 1) * UNIT],
+                    start=False,
+                    stop=closes and s == tiles - 1,
+                )
+
         def result_tile(part):
             m, tiles, u, units = part
             tile = sb.tile([P, tiles, units * UNIT], F32, name="result%d_%d" % (m, u), align_bytes=ALIGN)
@@ -289,7 +317,8 @@ def tile_mix_tierg_mul_kernel(tc, g, w8_words, w8_scales, d, out):
         load_g(2, 2)
         load_g(4, 2)
         load_g(6, 2)
-        nc.gpsimd.iota(ramp[:], pattern=[[1, RAMP]], base=RAMP // 2, channel_multiplier=-PACK, allow_small_or_imprecise_dtypes=True)
+        nc.vector.memset(w_plane.bitcast(I32), 0)
+        nc.gpsimd.iota(ramp[:], pattern=[[1, RAMP]], base=(K - RAMP) // 2, channel_multiplier=-PACK, allow_small_or_imprecise_dtypes=True)
         identity(0, 512)
         quantise_identity(0, 256)
         warm_up(2, 256)
@@ -303,12 +332,14 @@ def tile_mix_tierg_mul_kernel(tc, g, w8_words, w8_scales, d, out):
         dequantise(0, 4)
         cast(V, 1, 0, 80)
         cast(S, 1, 80, 128)
-        nc.vector.memset(w_plane[:].bitcast(I32), 0)
         load_scales()
         load_w()
-        load_d(0, 2, 0, 4)
-        load_d(2, 2, 0, 4)
-        load_d(0, 4, 4, 4)
+        for i in range(2):
+            pair = sb.tile([P, 2, T], F32, name="d_pair%d" % i, align_bytes=ALIGN)
+            for s in range(2):
+                nc.sync.dma_start(out=pair[:, s, :], in_=d_view[:, 2 * i + s, :])
+                for v in range(8):
+                    d_part[2 * i + s, v] = (pair, s, v * UNIT)
         widen(0)
         quantise_q(1, 1)
         dequantise(1, 5)
@@ -343,38 +374,40 @@ def tile_mix_tierg_mul_kernel(tc, g, w8_words, w8_scales, d, out):
         quantise_r(2, 2)
 
         widen(6)
-        widen(7)
-        stage_grouped(7)
+        stage(7)
         second_tier(wide[0])
-        second_tier(wide[1])
-        subtract_pool(4)
+
+        subtract_pool(4, 0)
         subtract(5)
         subtract_wide(6)
-        for m in (2, 3):
-            first_tier(wide[m], m)
+
+        for m in range(1, 4):
+            if m >= 2:
+                first_tier(wide[m], m)
             second_tier(wide[m])
-        for i in range(2):
-            first_tier(mid[i], 4 + i)
+
         multiply(wide[0])
         store(wide[0], nc.sync)
-        multiply(wide[1])
-        store(wide[1], nc.scalar)
         quantise_r(4, 1)
         quantise_r(5, 2)
-        subtract_pool_wide(7)
-        for i in range(2):
-            second_tier(mid[i])
-        for i in range(2):
-            first_tier(last[i], 6 + i)
+        subtract_pool(7)
+        for x in (mid[0], mid[1]):
+            first_tier(x, 4 + x[0] // 2)
+            second_tier(x)
+        first_tier(last[0], 6)
+        first_tier(last[1], 7)
+
+        multiply(wide[1])
+        store(wide[1], nc.scalar)
         multiply(wide[2])
         store(wide[2], nc.sync)
-        multiply(wide[3])
-        store(wide[3], nc.scalar)
         multiply(mid[0])
-        store(mid[0], nc.sync)
+        store(mid[0], nc.scalar)
         quantise_r(7, 1)
-        for i in range(2):
-            second_tier(last[i])
+        second_tier(last[0])
+        second_tier(last[1])
+        multiply(wide[3])
+        store(wide[3], nc.sync)
         multiply(mid[1])
         store(mid[1], nc.scalar)
         multiply(last[0])

from contextlib import ExitStack

import concourse.mybir as mybir

K, N, T = 512, 512, 1024
FLOPS = 2 * 2 * K * N * T

F32 = mybir.dt.float32
BF16 = mybir.dt.bfloat16
I32 = mybir.dt.int32
U32 = mybir.dt.uint32
U8 = mybir.dt.uint8
E4M3 = mybir.dt.float8_e4m3fn_x4
E5M2 = mybir.dt.float8_e5m2_x4
ALU = mybir.AluOpType

P = 128
PACK = 4
UNIT = 128
BANK = 512
PAIR = 2
RUN = 4
RAMP = 128
ALIGN = 256
SLOTS = 14
G_AT = [s * UNIT for s in (0, 1, 2, 3, 4, 5, 12, 13)]
R_AT = [s * UNIT for s in (6, 7, 8, 9, 13, 10, 11, 13)]


def tile_mix_tierg_mul_kernel(tc, g, w8_words, w8_scales, d, out):
    nc = tc.nc
    n_tiles = N // P

    with ExitStack() as ctx:
        sb = ctx.enter_context(tc.tile_pool(name="sb", bufs=1))
        psum = ctx.enter_context(tc.psum_pool(name="psum", bufs=1))
        ctx.enter_context(tc.manual_schedule())

        grouped = sb.tile([P, PACK * SLOTS * UNIT], BF16, name="grouped", align_bytes=ALIGN)
        eye_words = sb.tile([P, K], U32, name="eye_words", align_bytes=ALIGN)
        eye_plane = sb.tile([P, K], U8, name="eye_plane", align_bytes=ALIGN)
        q_words = sb.tile([P, T], U32, name="q_words", align_bytes=ALIGN)
        q_plane = sb.tile([P, T], U8, name="q_plane", align_bytes=ALIGN)
        r_words = sb.tile([P, T], U32, name="r_words", align_bytes=ALIGN)
        r_plane = sb.tile([P, T], U8, name="r_plane", align_bytes=ALIGN)
        w_words = sb.tile([P, N], I32, name="w_words", align_bytes=ALIGN)
        w_rows = sb.tile([P, N], U8, name="w_rows", align_bytes=ALIGN)
        w_plane = w_rows[:, 0:N]
        ramp = sb.tile([P, RAMP], BF16, name="ramp", align_bytes=ALIGN)
        eye_grouped = sb.tile([P, PACK * K], BF16, name="eye_grouped", align_bytes=ALIGN)

        g_view = g.rearrange("(p j) t -> p j t", j=PACK)
        d_view = d.rearrange("(m p) t -> p m t", p=P)
        out_view = out.rearrange("(m p) t -> p m t", p=P)
        g_rows = {}
        d_part = {}
        values = {}
        staged = {}
        g_wide = {}
        sums = {}
        results = {}
        elsewhere = {}

        def bank(b):
            return psum.tile([P, BANK], F32, name="bank%d" % b, tag="bank%d" % b)

        def load_g(first, count, queue=nc.sync):
            rows = sb.tile([P, PACK, count * UNIT], F32, name="g_rows%d" % first, align_bytes=ALIGN)
            queue.dma_start(out=rows[:], in_=g_view[:, :, first * UNIT : (first + count) * UNIT])
            for u in range(first, first + count):
                g_rows[u] = (rows, (u - first) * UNIT)

        def load_scales(queue=nc.sync):
            for r in range(4):
                queue.dma_start(out=w_rows[r:P:32, 0:N].bitcast(I32), in_=w8_scales[0, r:16:4, :].bitcast(I32))

        def load_scale_rows(queue=nc.sync):
            queue.dma_start(
                out=w_rows[0:4, :].bitcast(I32).rearrange("r (q n) -> r q n", q=4),
                in_=w8_scales[0].bitcast(I32).rearrange("(q r) n -> r q n", r=4),
            )

        def spread_scales(copy, dtype, first=1, last=4):
            for q in range(first, last):
                copy(out=w_rows[32 * q : 32 * q + 4, 0:N].bitcast(dtype), in_=w_rows[0:4, q * N : (q + 1) * N].bitcast(dtype))

        def load_w(queue=nc.sync):
            queue.dma_start(out=w_words[:], in_=w8_words[0].rearrange("p n i -> p (n i)").bitcast(I32))

        def load_d(m, tiles, u, units, queue=nc.sync):
            part = sb.tile([P, tiles, units * UNIT], F32, name="d%d_%d" % (m, u), align_bytes=ALIGN)
            queue.dma_start(out=part[:], in_=d_view[:, m : m + tiles, u * UNIT : (u + units) * UNIT])
            for x in range(m, m + tiles):
                for v in range(u, u + units):
                    d_part[x, v] = (part, x - m, (v - u) * UNIT)

        def identity(first, width):
            for at in range(PACK * first, PACK * (first + width), RAMP):
                nc.vector.tensor_scalar(
                    out=eye_grouped[:, at : at + RAMP],
                    in0=ramp[:],
                    scalar1=float((K - RAMP) // 2 + at // K - at % K),
                    scalar2=None,
                    op0=ALU.is_equal,
                )

        def quantise_identity(first, width):
            nc.vector.quantize_mx(
                out=eye_words[:, first : first + width].bitcast(E4M3),
                scales=eye_plane[:, first : first + width],
                in_=eye_grouped[:, PACK * first : PACK * (first + width)],
            )

        def warm_up(count, width):
            warm_bank = bank(0)
            for i in range(count):
                nc.tensor.matmul_mx(
                    out=warm_bank[:, 0:width],
                    lhsT=eye_words[:, 0:P].bitcast(E4M3),
                    lhsT_scale=eye_plane[:, 0:P],
                    rhs=eye_words[:, 0:width].bitcast(E4M3),
                    rhs_scale=eye_plane[:, 0:width],
                    start=True,
                    stop=True,
                )

        def flat(at, lo, hi):
            if at in elsewhere:
                return elsewhere[at][:, PACK * lo : PACK * hi]
            return grouped[:, PACK * (at + lo) : PACK * (at + hi)]

        def grouped_walk(at, lo, hi, run):
            return flat(at, lo, hi).rearrange("p (c i j) -> p c j i", i=run, j=PACK)

        def rows_walk(rows, run):
            return rows.rearrange("p j (c i) -> p c j i", i=run)

        def g_cols(u, lo, hi):
            rows, first = g_rows[u]
            return rows[:, :, first + lo : first + hi]

        def value_rows(u):
            return values[u][:].rearrange("p (j t) -> p j t", j=PACK)

        def cast(copy, u, lo, hi):
            copy(out=grouped_walk(G_AT[u], lo, hi, PAIR), in_=rows_walk(g_cols(u, lo, hi), PAIR))

        def cast_pool(u, lo, hi):
            nc.gpsimd.tensor_scalar(
                out=flat(G_AT[u], lo, hi).rearrange("p (t j) -> p t j", j=PACK),
                in0=g_cols(u, lo, hi).rearrange("p j t -> p t j"),
                scalar1=1.0,
                scalar2=0.0,
                op0=ALU.mult,
                op1=ALU.add,
            )

        def quantise(words, plane, fmt, at, u, count):
            cols = slice(u * UNIT, (u + count) * UNIT)
            nc.vector.quantize_mx(out=words[:, cols].bitcast(fmt), scales=plane[:, cols], in_=flat(at, 0, count * UNIT))

        def dequantise(u, b):
            cols = slice(u * UNIT, (u + 1) * UNIT)
            values[u] = bank(b)
            for j in range(PACK):
                nc.tensor.matmul_mx(
                    out=values[u][:, j * UNIT : (j + 1) * UNIT],
                    lhsT=eye_words[:, j * P : (j + 1) * P].bitcast(E4M3),
                    lhsT_scale=eye_plane[:, j * P : (j + 1) * P],
                    rhs=q_words[:, cols].bitcast(E5M2),
                    rhs_scale=q_plane[:, cols],
                    start=True,
                    stop=True,
                )

        def quantise_q(u, count):
            quantise(q_words, q_plane, E5M2, G_AT[u], u, count)

        def quantise_r(u, count):
            quantise(r_words, r_plane, E4M3, R_AT[u], u, count)

        def subtract(u, lo=0, hi=UNIT):
            nc.vector.tensor_tensor(
                out=grouped_walk(R_AT[u], lo, hi, PAIR),
                in0=rows_walk(g_cols(u, lo, hi), PAIR),
                in1=rows_walk(value_rows(u)[:, :, lo:hi], PAIR),
                op=ALU.subtract,
            )

        def widen(u, at=None):
            if at is None:
                g_wide[u] = sb.tile([P, UNIT, PACK], F32, name="g_wide%d" % u, align_bytes=ALIGN)[:]
            else:
                g_wide[u] = flat(at, 0, 2 * UNIT).bitcast(F32).rearrange("p (t j) -> p t j", j=PACK)
            nc.scalar.copy(out=g_wide[u].rearrange("p (c i) j -> p c j i", i=PAIR), in_=rows_walk(g_cols(u, 0, UNIT), PAIR))

        def subtract_wide(u):
            nc.vector.tensor_tensor(
                out=flat(R_AT[u], 0, UNIT).rearrange("p (t j) -> p t j", j=PACK),
                in0=g_wide[u],
                in1=value_rows(u).rearrange("p j t -> p t j"),
                op=ALU.subtract,
            )

        def staged_walk(u, lo):
            return staged[u][:, PACK * lo :].rearrange("p (c j i) -> p c j i", j=PACK, i=RUN)

        def stage(u, lo=0):
            staged[u] = sb.tile([P, BANK], F32, name="staged%d" % u, align_bytes=ALIGN)
            nc.scalar.copy(out=staged_walk(u, lo), in_=rows_walk(value_rows(u)[:, :, lo:UNIT], RUN))

        def subtract_pool(u, lo=0):
            nc.gpsimd.tensor_tensor(
                out=grouped_walk(R_AT[u], lo, UNIT, RUN),
                in0=rows_walk(g_cols(u, lo, UNIT), RUN),
                in1=staged_walk(u, lo),
                op=ALU.subtract,
            )

        def stage_grouped(u, lo=0):
            staged[u] = sb.tile([P, UNIT, PACK], F32, name="staged%d" % u, align_bytes=ALIGN)
            nc.scalar.copy(out=staged[u][:, lo:UNIT, :], in_=value_rows(u)[:, :, lo:UNIT].rearrange("p j t -> p t j"))

        def subtract_pool_wide(u, lo=0):
            nc.gpsimd.tensor_tensor(
                out=flat(R_AT[u], lo, UNIT),
                in0=g_wide[u][:, lo:UNIT, :].rearrange("p t j -> p (t j)"),
                in1=staged[u][:, lo:UNIT, :].rearrange("p t j -> p (t j)"),
                op=ALU.subtract,
            )

        def cast_wide(u, lo, hi):
            nc.vector.tensor_copy(out=flat(G_AT[u], lo, hi), in_=g_wide[u][:, lo:hi, :].rearrange("p t j -> p (t j)"))

        def cast_pool_wide(u, lo, hi):
            nc.gpsimd.tensor_scalar(
                out=flat(G_AT[u], lo, hi),
                in0=g_wide[u][:, lo:hi, :].rearrange("p t j -> p (t j)"),
                scalar1=1.0,
                scalar2=0.0,
                op0=ALU.mult,
                op1=ALU.add,
            )

        def tier(block, words, plane, fmt, first):
            m, tiles, u, units = block
            width = units * UNIT
            cols = slice(u * UNIT, u * UNIT + width)
            for s in range(tiles):
                nc.tensor.matmul_mx(
                    out=sums[block][:, s * width : (s + 1) * width],
                    lhsT=w_words[:, (m + s) * P : (m + s + 1) * P].bitcast(E4M3),
                    lhsT_scale=w_plane[:, (m + s) * P : (m + s + 1) * P],
                    rhs=words[:, cols].bitcast(fmt),
                    rhs_scale=plane[:, cols],
                    start=first and s == 0,
                    stop=not first and s == tiles - 1,
                )

        def first_tier(block, b):
            sums[block] = bank(b)
            tier(block, q_words, q_plane, E5M2, True)

        def second_tier(block):
            tier(block, r_words, r_plane, E4M3, False)

        def second_tier_unit(block, u, closes):
            m, tiles, first, units = block
            for s in range(tiles):
                at = (s * units + u - first) * UNIT
                nc.tensor.matmul_mx(
                    out=sums[block][:, at : at + UNIT],
                    lhsT=w_words[:, (m + s) * P : (m + s + 1) * P].bitcast(E4M3),
                    lhsT_scale=w_plane[:, (m + s) * P : (m + s + 1) * P],
                    rhs=r_words[:, u * UNIT : (u + 1) * UNIT].bitcast(E4M3),
                    rhs_scale=r_plane[:, u * UNIT : (u + 1) * UNIT],
                    start=False,
                    stop=closes and s == tiles - 1,
                )

        def result_tile(part):
            m, tiles, u, units = part
            tile = sb.tile([P, tiles, units * UNIT], F32, name="result%d_%d" % (m, u), align_bytes=ALIGN)
            for x in range(m, m + tiles):
                for v in range(u, u + units):
                    results[x, v] = (tile, x - m, (v - u) * UNIT)

        def window(parts, block):
            m, tiles, u, units = block
            tile, row, col = parts[m, u]
            return tile[:, row : row + tiles, col : col + units * UNIT]

        def bank_rows(tile, block):
            return tile[:, 0 : block[1] * block[3] * UNIT].rearrange("p (s t) -> p s t", s=block[1])

        def multiply(block):
            if (block[0], block[2]) not in results:
                result_tile(block)
            nc.vector.tensor_tensor(out=window(results, block), in0=window(d_part, block), in1=bank_rows(sums[block], block), op=ALU.mult)

        def stage_sum(block):
            staged[block] = sb.tile([P, BANK], F32, name="staged%d_%d" % (block[0], block[2]), align_bytes=ALIGN)
            nc.scalar.copy(out=staged[block][:], in_=sums[block][:])

        def multiply_pool(block):
            if (block[0], block[2]) not in results:
                result_tile(block)
            nc.gpsimd.tensor_tensor(out=window(results, block), in0=window(d_part, block), in1=bank_rows(staged[block], block), op=ALU.mult)

        def store(part, queue):
            m, tiles, u, units = part
            queue.dma_start(out=out_view[:, m : m + tiles, u * UNIT : (u + units) * UNIT], in_=window(results, part))

        V, S = nc.vector.tensor_copy, nc.scalar.copy
        load_g(0, 1)
        load_g(1, 1)
        load_g(2, 2)
        load_g(4, 2)
        load_g(6, 2)
        nc.vector.memset(w_plane.bitcast(I32), 0)
        nc.gpsimd.iota(ramp[:], pattern=[[1, RAMP]], base=(K - RAMP) // 2, channel_multiplier=-PACK, allow_small_or_imprecise_dtypes=True)
        identity(0, 512)
        quantise_identity(0, 256)
        warm_up(2, 256)
        wide = [(m, 1, 0, 4) for m in range(4)]
        mid = [(2 * i, 2, 4, 2) for i in range(2)]
        last = [(2 * i, 2, 6, 2) for i in range(2)]
        cast(V, 0, 0, 80)
        cast(S, 0, 80, UNIT)
        quantise_identity(256, 256)
        quantise_q(0, 1)
        dequantise(0, 4)
        cast(V, 1, 0, 80)
        cast(S, 1, 80, 128)
        load_scales()
        load_w()
        for i in range(2):
            pair = sb.tile([P, 2, T], F32, name="d_pair%d" % i, align_bytes=ALIGN)
            for s in range(2):
                nc.sync.dma_start(out=pair[:, s, :], in_=d_view[:, 2 * i + s, :])
                for v in range(8):
                    d_part[2 * i + s, v] = (pair, s, v * UNIT)
        widen(0)
        quantise_q(1, 1)
        dequantise(1, 5)
        warm_up(1, 512)
        widen(1)
        cast(V, 2, 0, 128)
        cast(S, 2, 128, 256)
        subtract_wide(0)
        subtract_wide(1)
        quantise_q(2, 2)
        dequantise(2, 6)
        dequantise(3, 7)
        cast(V, 4, 0, 96)
        cast(S, 4, 96, 128)
        cast(S, 5, 0, 128)
        quantise_r(0, 2)
        quantise_q(4, 1)
        quantise_q(5, 1)
        dequantise(4, 4)
        dequantise(5, 5)
        cast(S, 6, 0, 128)
        cast(S, 7, 0, 128)
        subtract(2)
        subtract(3)
        stage(4)
        first_tier(wide[0], 0)
        first_tier(wide[1], 1)
        quantise_q(6, 1)
        dequantise(6, 6)
        quantise_q(7, 1)
        dequantise(7, 7)
        quantise_r(2, 2)

        widen(6)
        stage(7)
        second_tier(wide[0])

        subtract_pool(4, 0)
        subtract(5)
        subtract_wide(6)

        for m in range(1, 4):
            if m >= 2:
                first_tier(wide[m], m)
            second_tier(wide[m])

        multiply(wide[0])
        store(wide[0], nc.sync)
        quantise_r(4, 1)
        quantise_r(5, 2)
        subtract_pool(7)
        for x in (mid[0], mid[1]):
            first_tier(x, 4 + x[0] // 2)
            second_tier(x)
        first_tier(last[0], 6)
        first_tier(last[1], 7)

        multiply(wide[1])
        store(wide[1], nc.scalar)
        multiply(wide[2])
        store(wide[2], nc.sync)
        multiply(mid[0])
        store(mid[0], nc.scalar)
        quantise_r(7, 1)
        second_tier(last[0])
        second_tier(last[1])
        multiply(wide[3])
        store(wide[3], nc.sync)
        multiply(mid[1])
        store(mid[1], nc.scalar)
        multiply(last[0])
        store(last[0], nc.sync)
        multiply(last[1])
        store(last[1], nc.scalar)
